import numpy as np
import ml_dtypes


def mxq(x, axis, fmt="e4m3"):
    dtype, down = {"e4m3": (ml_dtypes.float8_e4m3fn, 7), "e5m2": (ml_dtypes.float8_e5m2, 14)}[fmt]
    v = np.moveaxis(np.asarray(x, np.float32).astype(ml_dtypes.bfloat16).astype(np.float64), axis, -1)
    blocks = v.reshape(v.shape[:-1] + (-1, 32))
    amax = np.abs(blocks).max(-1, keepdims=True)
    byte = np.maximum(np.where(amax > 0, np.frexp(amax)[1] - 1 + 127, 0) - down, 1)
    scale = np.exp2(byte - 127.0)
    codes = (blocks / scale).astype(np.float32).astype(dtype).astype(np.float64)
    return np.moveaxis((codes * scale).reshape(v.shape), -1, axis)


WIDE = False


def mx_kscale(k):
    if not WIDE:
        return np.ones(k)
    levels = np.array([10, -10, 5, -5, 0])
    if k % 512:
        return np.exp2(np.random.permutation(np.resize(levels, k // 32))).repeat(32)
    a = np.empty((k // 512, 16))
    for p in range(k // 512):
        a[p, :8] = np.random.permutation(np.resize(levels, 8))
        for g in range(8):
            far = levels[np.abs(levels - a[p, g]) >= 10]
            a[p, g + 8] = far[np.random.randint(len(far))]
    return np.exp2(a.ravel()).repeat(32)


def f64(x):
    return np.asarray(x).astype(np.float64)


def striped(idx):
    return np.tile(idx.reshape(-1, 16).T, (8, 1)).astype(np.uint16)


def unstriped(offs):
    return offs[:16].T.reshape(-1).astype(np.int64)


E2M1 = np.array([0.0, 0.5, 1.0, 1.5, 2.0, 3.0, 4.0, 6.0, -0.0, -0.5, -1.0, -1.5, -2.0, -3.0, -4.0, -6.0])


def pack_weight(w, fmt):
    k, n = w.shape
    w = f64(np.asarray(w, np.float32).astype(ml_dtypes.bfloat16)).reshape(k // 32, 32, n)
    amax = np.abs(w).max(1)
    if fmt == "e4m3":
        byte = np.frexp(amax)[1] - 1 + 127 - 7
    else:
        mant, ex = np.frexp(amax / 6.0)
        byte = np.where(mant > 0.5, ex, ex - 1) + 127
    byte = np.clip(np.where(amax > 0, byte, 1), 1, 254)
    scaled = (w * np.exp2(127.0 - byte)[:, None, :]).reshape(k, n).astype(np.float32)
    by_word = np.ascontiguousarray(scaled.reshape(k // 512, 128, 4, n).transpose(0, 1, 3, 2))
    if fmt == "e4m3":
        words = by_word.astype(ml_dtypes.float8_e4m3fn).view(np.uint8)
    else:
        c = by_word.astype(ml_dtypes.float4_e2m1fn).view(np.uint8) & 0xF
        words = (c[..., 0::2] | (c[..., 1::2] << 4)).reshape(k // 512, 128, 2 * n)
    return np.ascontiguousarray(words), np.ascontiguousarray(byte.astype(np.uint8).reshape(k // 512, 16, n))


def unpack_weight(words, scales, fmt):
    g, _, n = scales.shape
    words = np.ascontiguousarray(words).reshape(g, 128, n, -1)
    if fmt == "e4m3":
        vals = words.view(ml_dtypes.float8_e4m3fn).astype(np.float64)
    else:
        nib = np.empty((g, 128, n, 4), np.uint8)
        nib[..., 0::2] = words & 0xF
        nib[..., 1::2] = words >> 4
        vals = E2M1[nib]
    vals = vals * np.repeat(np.exp2(scales.astype(np.float64) - 127.0), 8, axis=1)[..., None]
    return vals.transpose(0, 1, 3, 2).reshape(g * 512, n)


def gelu(v):
    return 0.5 * v * (1.0 + np.tanh(np.sqrt(2.0 / np.pi) * (v + 0.044715 * v**3)))


def bf(x):
    return np.asarray(x, np.float32).astype(ml_dtypes.bfloat16)


def planes(Y):
    n, m = Y.shape
    b = f64(bf(Y)).reshape(n // 32, 32, m)
    amax = np.abs(b).max(1)
    byte = np.clip(np.where(amax > 0, np.frexp(amax)[1] - 1 + 127 - 7, 1), 1, 254)
    codes = (b * np.exp2(127.0 - byte)[:, None, :]).reshape(n, m).astype(np.float32).astype(ml_dtypes.float8_e4m3fn).view(np.uint8)
    words = codes.reshape(n // 512, 128, 4, m).transpose(0, 1, 3, 2)
    return np.ascontiguousarray(words), np.ascontiguousarray(byte.astype(np.uint8).reshape(n // 512, 16, m))


K, H, N, T, S = 512, 1024, 384, 4096, 1024

def setup_inputs():
    n = np.random.standard_normal
    s = mx_kscale(K)[:, None]
    u = mx_kscale(H)[:, None]
    tab_words, tab_scales = pack_weight(n((K, T)) * s, "e4m3")
    wi_words, wi_scales = pack_weight(n((K, H)) / np.sqrt(K) / s * u.T, "e4m3")
    wc_words, wc_scales = pack_weight(n((K, N)) / np.sqrt(K) / s, "e2m1")
    return {
        "tab_words": tab_words, "tab_scales": tab_scales,
        "offs": striped(np.random.permutation(T)[:S]),
        "wi_words": wi_words, "wi_scales": wi_scales,
        "wq": (n((K, H)) / np.sqrt(K) / s * u.T).astype(np.float32),
        "amb": (0.5 * np.exp(0.3 * n(H)) * u[:, 0] ** 2).astype(np.float32),
        "wd": (n((H, N)) / np.sqrt(H) / u).astype(np.float32),
        "wc_words": wc_words, "wc_scales": wc_scales,
    }

def reference(tab_words, tab_scales, offs, wi_words, wi_scales, wq, amb, wd, wc_words, wc_scales):
    v = unpack_weight(tab_words, tab_scales, "e4m3")[:, unstriped(offs)]
    wi = unpack_weight(wi_words, wi_scales, "e4m3")
    wc = unpack_weight(wc_words, wc_scales, "e2m1")
    bi = wi.T @ v
    bq = mxq(f64(wq), 0, "e4m3").T @ v
    h = np.sqrt(bi * bi + bq * bq + f64(amb)[:, None])
    clutter = wc.T @ v
    y = (mxq(f64(wd), 0, "e4m3").T @ mxq(h, 0, "e4m3")) - clutter
    words, scales = planes(h)
    return y, h, words, scales

@@ -1,0 +1,299 @@
+from contextlib import ExitStack
+
+import concourse.mybir as mybir
+
+K, H, N, T, S = 512, 1024, 384, 4096, 1024
+FLOPS = 2 * (2 * K * H * S + K * N * S + H * N * S)
+
+F32 = mybir.dt.float32
+BF16 = mybir.dt.bfloat16
+I32 = mybir.dt.int32
+U32 = mybir.dt.uint32
+U16 = mybir.dt.uint16
+U8 = mybir.dt.uint8
+FP8X4 = mybir.dt.float8_e4m3fn_x4
+FP4X4 = mybir.dt.float4_e2m1fn_x4
+ACT = mybir.ActivationFunctionType
+ALU = mybir.AluOpType
+
+P = 128
+PACK = 4
+PASS = P * PACK
+W = 512
+GROUPS = H // PASS
+HALVES = S // W
+NT = N // P
+AHEAD = 4
+LAG = 2
+
+
+def tile_list_sonar_envelopes_kernel(
+    tc, tab_words, tab_scales, offs, wi_words, wi_scales, wq, amb, wd, wc_words, wc_scales,
+    out_0, out_1, out_2, out_3,
+):
+    nc = tc.nc
+    with ExitStack() as ctx:
+        lists = ctx.enter_context(tc.tile_pool(name="lists", bufs=1))
+        keep = ctx.enter_context(tc.tile_pool(name="keep", bufs=1))
+        ring = ctx.enter_context(tc.tile_pool(name="ring", bufs=3))
+        beams = ctx.enter_context(tc.psum_pool(name="beams", bufs=5))
+        reads = ctx.enter_context(tc.psum_pool(name="reads", bufs=3))
+
+        def held(shape, dtype, name):
+            return keep.tile(shape, dtype, name=name, align_bytes=64)
+
+        offsets = lists.tile([P, S // 16], U16, name="offsets")
+        nc.sync.dma_start(offsets[:], offs)
+
+        warm = held([P, 1], F32, "warm")
+        nc.vector.memset(warm[:], 1.0)
+        warm_out = held([P, 1], F32, "warm_out")
+        nc.scalar.activation(warm_out[:], warm[:], ACT.Sqrt)
+
+        tab_plane = held([P, T], U8, "tab_plane")
+        nc.vector.memset(tab_plane[:].bitcast(I32), 0)
+        w_plane = held([P, H + N], U8, "w_plane")
+        nc.vector.memset(w_plane[:].bitcast(I32), 0)
+
+        def load_scale_rows(plane, rows):
+            for q in range(4):
+                nc.gpsimd.dma_start(
+                    plane[32 * q : 32 * q + 4, :].bitcast(I32), rows[4 * q : 4 * q + 4, :].bitcast(I32)
+                )
+
+        load_scale_rows(tab_plane[:], tab_scales[0])
+        load_scale_rows(w_plane[:, 0:H], wi_scales[0])
+        load_scale_rows(w_plane[:, H : H + N], wc_scales[0])
+
+        tab = held([P, T], I32, "tab")
+        nc.sync.dma_start(tab[:], tab_words[0].rearrange("p t i -> p (t i)").bitcast(I32))
+
+        wi_dram = wi_words[0].rearrange("p c i -> p (c i)").bitcast(I32)
+        wq_dram = wq.rearrange("(p i) c -> p i c", i=PACK)
+        wi_raw, wq_raw = [], []
+        amb_sb = held([P, GROUPS, PACK], F32, "amb_sb")
+        for g in range(GROUPS):
+            wi_raw.append(held([P, PASS], I32, "wi_raw%d" % g))
+            nc.sync.dma_start(wi_raw[g][:], wi_dram[:, g * PASS : (g + 1) * PASS])
+            wq_raw.append(held([P, PACK, PASS], F32, "wq_raw%d" % g))
+            nc.sync.dma_start(wq_raw[g][:], wq_dram[:, :, g * PASS : (g + 1) * PASS])
+            if g == 0:
+                nc.sync.dma_start(amb_sb[:], amb.rearrange("(g p t) -> p g t", g=GROUPS, t=PACK))
+        wd_raw = held([P, GROUPS, PACK * N], F32, "wd_raw")
+        nc.sync.dma_start(wd_raw[:], wd.rearrange("(g p i) n -> p g (i n)", g=GROUPS, i=PACK))
+        wc = held([P, 2 * N], U8, "wc")
+        nc.sync.dma_start(wc[:].bitcast(I32), wc_words[0].bitcast(I32))
+
+        v_words = [held([P, W], U32, "v_words%d" % b) for b in range(HALVES)]
+        v_scales = [held([P, W], U8, "v_scales%d" % b) for b in range(HALVES)]
+
+        def part(b):
+            return offsets[:, b * (W // 16) : (b + 1) * (W // 16)]
+
+        def gather_scales(b):
+            nc.vector.tensor_copy(v_scales[b][:], tab_plane[:].indirect(part(b)))
+
+        def gather_words(b):
+            nc.vector.tensor_copy(v_words[b][:], tab[:].bitcast(U32).indirect(part(b)))
+
+        wi_codes = [held([P, PASS], I32, "wi_codes%d" % g) for g in range(GROUPS)]
+        wi_plane = [held([P, PASS], U8, "wi_plane%d" % g) for g in range(GROUPS)]
+
+        def deal_wi_scales(g):
+            nc.vector.tensor_copy(
+                wi_plane[g][:].rearrange("p (t m) -> p m t", t=PACK),
+                w_plane[:, g * PASS : (g + 1) * PASS].rearrange("p (m t) -> p m t", t=PACK),
+            )
+
+        def deal_wi_words(g):
+            nc.vector.tensor_copy(
+                wi_codes[g][:].rearrange("p (t m) -> p m t", t=PACK),
+                wi_raw[g][:].rearrange("p (m t) -> p m t", t=PACK),
+            )
+
+        wq_bf = [held([P, PACK * PASS], BF16, "wq_bf%d" % g) for g in range(GROUPS)]
+        wq_codes = [held([P, PASS], U32, "wq_codes%d" % g) for g in range(GROUPS)]
+        wq_plane = [held([P, PASS], U8, "wq_plane%d" % g) for g in range(GROUPS)]
+
+        def round_wq(g, half):
+            m = slice(half * (P // 2), (half + 1) * (P // 2))
+            nc.vector.tensor_copy(
+                wq_bf[g][:].rearrange("p (t m i) -> p m i t", t=PACK, i=PACK)[:, m],
+                wq_raw[g][:].rearrange("p i (m t) -> p m i t", t=PACK)[:, m],
+            )
+
+        def quantize_wq(g, half):
+            c = slice(half * (PASS // 2), (half + 1) * (PASS // 2))
+            e = slice(half * 2 * PASS, (half + 1) * 2 * PASS)
+            nc.vector.quantize_mx(
+                out=wq_codes[g][:, c].bitcast(FP8X4), scales=wq_plane[g][:, c], in_=wq_bf[g][:, e]
+            )
+
+        wd_bf = held([P, GROUPS * N * PACK], BF16, "wd_bf")
+        wd_codes = held([P, GROUPS * N], U32, "wd_codes")
+        wd_plane = held([P, GROUPS * N], U8, "wd_plane")
+
+        def round_wd(g):
+            nc.vector.tensor_scalar(
+                out=wd_bf[:, g * N * PACK : (g + 1) * N * PACK].rearrange("p (c e i) -> p c i e", e=4, i=PACK),
+                in0=wd_raw[:, g, :].rearrange("p (i c e) -> p c i e", i=PACK, e=4),
+                scalar1=-1.0,
+                scalar2=None,
+                op0=ALU.mult,
+            )
+
+        def quantize_wd(part_index):
+            c = slice(part_index * 256, (part_index + 1) * 256)
+            e = slice(part_index * 1024, (part_index + 1) * 1024)
+            nc.vector.quantize_mx(out=wd_codes[:, c].bitcast(FP8X4), scales=wd_plane[:, c], in_=wd_bf[:, e])
+
+        units = [(g, b) for g in range(GROUPS) for b in range(HALVES)]
+        steps = [(u, t) for u in range(len(units)) for t in range(PACK)]
+        env = [held([P, PACK, W], F32, "env%d" % u) for u in range(len(units))]
+        env_codes = [held([P, W], U32, "env_codes%d" % u) for u in range(len(units))]
+        env_plane = [held([P, S], U8, "env_plane%d" % g) for g in range(GROUPS)]
+        env_bf = [held([P, W * PACK], BF16, "env_bf%d" % u) for u in range(len(units))]
+        out_1_rows = out_1.rearrange("(g p t) j -> g p t j", g=GROUPS, t=PACK)
+        in_phase, power = {}, {}
+
+        def squared_beam(codes, plane, n, name, bufs):
+            u, t = steps[n]
+            g, b = units[u]
+            cols = slice(t * P, (t + 1) * P)
+            bank = beams.tile([P, W], F32, name="bank")
+            nc.tensor.matmul_mx(
+                out=bank[:],
+                lhsT=codes[g][:, cols].bitcast(FP8X4),
+                lhsT_scale=plane[g][:, cols],
+                rhs=v_words[b][:].bitcast(FP8X4),
+                rhs_scale=v_scales[b][:],
+                start=True,
+                stop=True,
+            )
+            square = ring.tile([P, W], F32, name=name, bufs=bufs)
+            nc.scalar.activation(square[:], bank[:], ACT.Square)
+            return square
+
+        def square_in_phase(n):
+            in_phase[n] = squared_beam(wi_codes, wi_plane, n, "bi2", AHEAD + 3)
+
+        def add_quadrature(n):
+            quad = squared_beam(wq_codes, wq_plane, n, "bq2", 3)
+            power[n] = ring.tile([P, W], F32, name="power", bufs=LAG + 2)
+            nc.vector.tensor_tensor(power[n][:], in_phase[n][:], quad[:], ALU.add)
+
+        def envelope(n):
+            u, t = steps[n]
+            g, b = units[u]
+            nc.scalar.activation(env[u][:, t, :], power[n][:], ACT.Sqrt, bias=amb_sb[:, g, t : t + 1])
+            nc.sync.dma_start(out_1_rows[g, :, t, b * W : (b + 1) * W], env[u][:, t, :])
+
+        def round_env(u, half):
+            c = slice(half * (W // 8), (half + 1) * (W // 8))
+            nc.vector.tensor_copy(
+                env_bf[u][:].rearrange("p (c e t) -> p c t e", e=4, t=PACK)[:, c],
+                env[u][:].rearrange("p t (c e) -> p c t e", e=4)[:, c],
+            )
+
+        def quantize_env(u):
+            g, b = units[u]
+            cols = slice(b * W, (b + 1) * W)
+            nc.vector.quantize_mx(
+                out=env_codes[u][:].bitcast(FP8X4), scales=env_plane[g][:, cols], in_=env_bf[u][:]
+            )
+            nc.sync.dma_start(
+                out_2[g].rearrange("p m t -> p (m t)").bitcast(I32)[:, cols], env_codes[u][:].bitcast(I32)
+            )
+            if b == HALVES - 1:
+                for q in range(4):
+                    nc.sync.dma_start(
+                        out_3[g, 4 * q : 4 * q + 4, :].bitcast(I32),
+                        env_plane[g][32 * q : 32 * q + 4, :].bitcast(I32),
+                    )
+
+        readout = {}
+
+        def open_readout(b):
+            for n in range(NT):
+                readout[b, n] = reads.tile([P, W], F32, name="readout")
+                nc.tensor.matmul_mx(
+                    out=readout[b, n][:],
+                    lhsT=wc[:, 2 * n * P : 2 * (n + 1) * P].bitcast(FP4X4),
+                    lhsT_scale=w_plane[:, H + n * P : H + (n + 1) * P],
+                    rhs=v_words[b][:].bitcast(FP8X4),
+                    rhs_scale=v_scales[b][:],
+                    start=True,
+                    stop=False,
+                )
+
+        def add_readout(u):
+            g, b = units[u]
+            for n in range(NT):
+                cols = slice(g * N + n * P, g * N + (n + 1) * P)
+                nc.tensor.matmul_mx(
+                    out=readout[b, n][:],
+                    lhsT=wd_codes[:, cols].bitcast(FP8X4),
+                    lhsT_scale=wd_plane[:, cols],
+                    rhs=env_codes[u][:].bitcast(FP8X4),
+                    rhs_scale=env_plane[g][:, b * W : (b + 1) * W],
+                    start=False,
+                    stop=(g == GROUPS - 1),
+                )
+
+        def store_readout(b):
+            for n in range(NT):
+                y = ring.tile([P, W], F32, name="y")
+                if n % 2 == b:
+                    nc.vector.tensor_scalar(out=y[:], in0=readout[b, n][:], scalar1=-1.0, scalar2=None, op0=ALU.mult)
+                else:
+                    nc.scalar.activation(y[:], readout[b, n][:], ACT.Copy, scale=-1.0)
+                nc.sync.dma_start(out_0[n * P : (n + 1) * P, b * W : (b + 1) * W], y[:])
+
+        gather_scales(0)
+        deal_wi_scales(0)
+        gather_scales(1)
+        gather_words(0)
+        deal_wi_words(0)
+        for n in range(AHEAD):
+            square_in_phase(n)
+        gather_words(1)
+        round_wq(0, 0)
+        round_wq(0, 1)
+        quantize_wq(0, 0)
+        quantize_wq(0, 1)
+
+        chores = {
+            0: [lambda: deal_wi_scales(1)],
+            1: [lambda: deal_wi_words(1)],
+            2: [lambda: round_wq(1, 0)],
+            3: [lambda: round_wq(1, 1)],
+            4: [lambda: quantize_wq(1, 0), lambda: quantize_wq(1, 1)],
+            7: [lambda: round_wd(0)],
+            8: [lambda: round_wd(1)],
+            11: [lambda: quantize_wd(0), lambda: quantize_wd(1), lambda: quantize_wd(2),
+                 lambda: open_readout(0), lambda: add_readout(0)],
+        }
+        for n in range(len(steps) + LAG + 1):
+            if n < len(steps):
+                add_quadrature(n)
+            if n + AHEAD < len(steps):
+                square_in_phase(n + AHEAD)
+            done = n - LAG
+            if 0 <= done < len(steps):
+                envelope(done)
+                if steps[done][1] == PACK - 1:
+                    round_env(steps[done][0], 0)
+                    round_env(steps[done][0], 1)
+            if done >= 1 and steps[done - 1][1] == PACK - 1:
+                u = steps[done - 1][0]
+                quantize_env(u)
+                if u == 2:
+                    add_readout(2)
+                    store_readout(0)
+                    open_readout(1)
+                    add_readout(1)
+                if u == 3:
+                    add_readout(3)
+                    store_readout(1)
+            for chore in chores.get(n, []):
+                chore()

@@ -45,28 +45,31 @@ def tile_list_sonar_envelopes_kernel(
         offsets = lists.tile([P, S // 16], U16, name="offsets")
         nc.sync.dma_start(offsets[:], offs)
 
+        tab = held([P, T], I32, "tab")
+        tab_dram = tab_words[0].rearrange("p t i -> p (t i)").bitcast(I32)
+        nc.sync.dma_start(tab[:, 0:1024], tab_dram[:, 0:1024])
+
+        tab_plane = held([P, T], U8, "tab_plane")
+        nc.vector.memset(tab_plane[:].bitcast(I32), 0)
+        w_plane = held([P, H], U8, "w_plane")
+        nc.vector.memset(w_plane[:].bitcast(I32), 0)
+        wc_plane = held([P, N], U8, "wc_plane")
+        nc.vector.memset(wc_plane[:].bitcast(I32), 0)
+
+        def load_scale_rows(queue, plane, rows):
+            for q in range(4):
+                queue.dma_start(
+                    plane[32 * q : 32 * q + 4, :].bitcast(I32), rows[4 * q : 4 * q + 4, :].bitcast(I32)
+                )
+
+        load_scale_rows(nc.sync, tab_plane, tab_scales[0])
+        nc.sync.dma_start(tab[:, 1024:2560], tab_dram[:, 1024:2560])
+        load_scale_rows(nc.sync, w_plane, wi_scales[0])
+
         warm = held([P, 1], F32, "warm")
         nc.vector.memset(warm[:], 1.0)
         warm_out = held([P, 1], F32, "warm_out")
         nc.scalar.activation(warm_out[:], warm[:], ACT.Sqrt)
-
-        tab_plane = held([P, T], U8, "tab_plane")
-        nc.vector.memset(tab_plane[:].bitcast(I32), 0)
-        w_plane = held([P, H + N], U8, "w_plane")
-        nc.vector.memset(w_plane[:].bitcast(I32), 0)
-
-        def load_scale_rows(plane, rows):
-            for q in range(4):
-                nc.gpsimd.dma_start(
-                    plane[32 * q : 32 * q + 4, :].bitcast(I32), rows[4 * q : 4 * q + 4, :].bitcast(I32)
-                )
-
-        load_scale_rows(tab_plane[:], tab_scales[0])
-        load_scale_rows(w_plane[:, 0:H], wi_scales[0])
-        load_scale_rows(w_plane[:, H : H + N], wc_scales[0])
-
-        tab = held([P, T], I32, "tab")
-        nc.sync.dma_start(tab[:], tab_words[0].rearrange("p t i -> p (t i)").bitcast(I32))
 
         wi_dram = wi_words[0].rearrange("p c i -> p (c i)").bitcast(I32)
         wq_dram = wq.rearrange("(p i) c -> p i c", i=PACK)
@@ -75,6 +78,8 @@ def tile_list_sonar_envelopes_kernel(
         for g in range(GROUPS):
             wi_raw.append(held([P, PASS], I32, "wi_raw%d" % g))
             nc.sync.dma_start(wi_raw[g][:], wi_dram[:, g * PASS : (g + 1) * PASS])
+            if g == 0:
+                nc.sync.dma_start(tab[:, 2560:T], tab_dram[:, 2560:T])
             wq_raw.append(held([P, PACK, PASS], F32, "wq_raw%d" % g))
             nc.sync.dma_start(wq_raw[g][:], wq_dram[:, :, g * PASS : (g + 1) * PASS])
             if g == 0:
@@ -83,6 +88,7 @@ def tile_list_sonar_envelopes_kernel(
         nc.sync.dma_start(wd_raw[:], wd.rearrange("(g p i) n -> p g (i n)", g=GROUPS, i=PACK))
         wc = held([P, 2 * N], U8, "wc")
         nc.sync.dma_start(wc[:].bitcast(I32), wc_words[0].bitcast(I32))
+        load_scale_rows(nc.sync, wc_plane, wc_scales[0])
 
         v_words = [held([P, W], U32, "v_words%d" % b) for b in range(HALVES)]
         v_scales = [held([P, W], U8, "v_scales%d" % b) for b in range(HALVES)]
@@ -147,64 +153,69 @@ def tile_list_sonar_envelopes_kernel(
             e = slice(part_index * 1024, (part_index + 1) * 1024)
             nc.vector.quantize_mx(out=wd_codes[:, c].bitcast(FP8X4), scales=wd_plane[:, c], in_=wd_bf[:, e])
 
-        units = [(g, b) for g in range(GROUPS) for b in range(HALVES)]
+        units = [(0, 0, W), (0, W, W), (1, 0, W), (1, W, W // 2), (1, W + W // 2, W // 2)]
         steps = [(u, t) for u in range(len(units)) for t in range(PACK)]
-        env = [held([P, PACK, W], F32, "env%d" % u) for u in range(len(units))]
-        env_codes = [held([P, W], U32, "env_codes%d" % u) for u in range(len(units))]
+        env = [held([P, PACK, w], F32, "env%d" % u) for u, (g, j0, w) in enumerate(units)]
+        env_bf = [held([P, w * PACK], BF16, "env_bf%d" % u) for u, (g, j0, w) in enumerate(units)]
+        env_codes = [held([P, w], U32, "env_codes%d" % u) for u, (g, j0, w) in enumerate(units)]
         env_plane = [held([P, S], U8, "env_plane%d" % g) for g in range(GROUPS)]
-        env_bf = [held([P, W * PACK], BF16, "env_bf%d" % u) for u in range(len(units))]
         out_1_rows = out_1.rearrange("(g p t) j -> g p t j", g=GROUPS, t=PACK)
         in_phase, power = {}, {}
 
+        def snapshots(j0, w):
+            cols = slice(j0 % W, j0 % W + w)
+            return v_words[j0 // W][:, cols].bitcast(FP8X4), v_scales[j0 // W][:, cols]
+
         def squared_beam(codes, plane, n, name, bufs):
             u, t = steps[n]
-            g, b = units[u]
+            g, j0, w = units[u]
             cols = slice(t * P, (t + 1) * P)
-            bank = beams.tile([P, W], F32, name="bank")
+            words, scales = snapshots(j0, w)
+            bank = beams.tile([P, w], F32, name="bank")
             nc.tensor.matmul_mx(
                 out=bank[:],
                 lhsT=codes[g][:, cols].bitcast(FP8X4),
                 lhsT_scale=plane[g][:, cols],
-                rhs=v_words[b][:].bitcast(FP8X4),
-                rhs_scale=v_scales[b][:],
+                rhs=words,
+                rhs_scale=scales,
                 start=True,
                 stop=True,
             )
-            square = ring.tile([P, W], F32, name=name, bufs=bufs)
+            square = ring.tile([P, w], F32, name=name, bufs=bufs)
             nc.scalar.activation(square[:], bank[:], ACT.Square)
             return square
 
         def square_in_phase(n):
-            in_phase[n] = squared_beam(wi_codes, wi_plane, n, "bi2", AHEAD + 3)
+            in_phase[n] = squared_beam(wi_codes, wi_plane, n, "bi2", AHEAD + 5)
 
         def add_quadrature(n):
             quad = squared_beam(wq_codes, wq_plane, n, "bq2", 3)
-            power[n] = ring.tile([P, W], F32, name="power", bufs=LAG + 2)
+            power[n] = ring.tile([P, units[steps[n][0]][2]], F32, name="power", bufs=LAG + 2)
             nc.vector.tensor_tensor(power[n][:], in_phase[n][:], quad[:], ALU.add)
 
         def envelope(n):
             u, t = steps[n]
-            g, b = units[u]
+            g, j0, w = units[u]
             nc.scalar.activation(env[u][:, t, :], power[n][:], ACT.Sqrt, bias=amb_sb[:, g, t : t + 1])
-            nc.sync.dma_start(out_1_rows[g, :, t, b * W : (b + 1) * W], env[u][:, t, :])
+            if t % 2 == 1:
+                nc.sync.dma_start(out_1_rows[g, :, t - 1 : t + 1, j0 : j0 + w], env[u][:, t - 1 : t + 1, :])
 
-        def round_env(u, half):
-            c = slice(half * (W // 8), (half + 1) * (W // 8))
-            nc.vector.tensor_copy(
-                env_bf[u][:].rearrange("p (c e t) -> p c t e", e=4, t=PACK)[:, c],
-                env[u][:].rearrange("p t (c e) -> p c t e", e=4)[:, c],
-            )
+        def round_env(u):
+            for c0 in range(0, units[u][2] // 4, 64):
+                nc.vector.tensor_copy(
+                    env_bf[u][:].rearrange("p (c e t) -> p c t e", e=4, t=PACK)[:, c0 : c0 + 64],
+                    env[u][:].rearrange("p t (c e) -> p c t e", e=4)[:, c0 : c0 + 64],
+                )
 
         def quantize_env(u):
-            g, b = units[u]
-            cols = slice(b * W, (b + 1) * W)
+            g, j0, w = units[u]
             nc.vector.quantize_mx(
-                out=env_codes[u][:].bitcast(FP8X4), scales=env_plane[g][:, cols], in_=env_bf[u][:]
+                out=env_codes[u][:].bitcast(FP8X4), scales=env_plane[g][:, j0 : j0 + w], in_=env_bf[u][:]
             )
             nc.sync.dma_start(
-                out_2[g].rearrange("p m t -> p (m t)").bitcast(I32)[:, cols], env_codes[u][:].bitcast(I32)
+                out_2[g].rearrange("p m t -> p (m t)").bitcast(I32)[:, j0 : j0 + w], env_codes[u][:].bitcast(I32)
             )
-            if b == HALVES - 1:
+            if j0 + w == S:
                 for q in range(4):
                     nc.sync.dma_start(
                         out_3[g, 4 * q : 4 * q + 4, :].bitcast(I32),
@@ -213,47 +224,54 @@ def tile_list_sonar_envelopes_kernel(
 
         readout = {}
 
-        def open_readout(b):
-            for n in range(NT):
-                readout[b, n] = reads.tile([P, W], F32, name="readout")
-                nc.tensor.matmul_mx(
-                    out=readout[b, n][:],
-                    lhsT=wc[:, 2 * n * P : 2 * (n + 1) * P].bitcast(FP4X4),
-                    lhsT_scale=w_plane[:, H + n * P : H + (n + 1) * P],
-                    rhs=v_words[b][:].bitcast(FP8X4),
-                    rhs_scale=v_scales[b][:],
-                    start=True,
-                    stop=False,
-                )
-
-        def add_readout(u):
-            g, b = units[u]
+        def add_readout(u, j0, w):
+            g, first, width = units[u]
             for n in range(NT):
                 cols = slice(g * N + n * P, g * N + (n + 1) * P)
                 nc.tensor.matmul_mx(
-                    out=readout[b, n][:],
+                    out=readout[n][:],
                     lhsT=wd_codes[:, cols].bitcast(FP8X4),
                     lhsT_scale=wd_plane[:, cols],
-                    rhs=env_codes[u][:].bitcast(FP8X4),
-                    rhs_scale=env_plane[g][:, b * W : (b + 1) * W],
+                    rhs=env_codes[u][:, j0 - first : j0 - first + w].bitcast(FP8X4),
+                    rhs_scale=env_plane[g][:, j0 : j0 + w],
                     start=False,
                     stop=(g == GROUPS - 1),
                 )
 
-        def store_readout(b):
+        def open_readout(u):
+            g, j0, w = units[u]
+            piece = W if w == W else P
             for n in range(NT):
-                y = ring.tile([P, W], F32, name="y")
-                if n % 2 == b:
-                    nc.vector.tensor_scalar(out=y[:], in0=readout[b, n][:], scalar1=-1.0, scalar2=None, op0=ALU.mult)
+                readout[n] = reads.tile([P, w], F32, name="readout")
+                for c0 in range(0, w, piece):
+                    words, scales = snapshots(j0 + c0, piece)
+                    nc.tensor.matmul_mx(
+                        out=readout[n][:, c0 : c0 + piece],
+                        lhsT=wc[:, 2 * n * P : 2 * (n + 1) * P].bitcast(FP4X4),
+                        lhsT_scale=wc_plane[:, n * P : (n + 1) * P],
+                        rhs=words,
+                        rhs_scale=scales,
+                        start=(c0 == 0),
+                        stop=False,
+                    )
+            add_readout(j0 // W, j0, w)
+
+        def close_readout(u):
+            g, j0, w = units[u]
+            add_readout(u, j0, w)
+            for n in range(NT):
+                y = ring.tile([P, w], F32, name="y")
+                if n == 1 or w == W:
+                    nc.vector.tensor_scalar(out=y[:], in0=readout[n][:], scalar1=-1.0, scalar2=None, op0=ALU.mult)
                 else:
-                    nc.scalar.activation(y[:], readout[b, n][:], ACT.Copy, scale=-1.0)
-                nc.sync.dma_start(out_0[n * P : (n + 1) * P, b * W : (b + 1) * W], y[:])
+                    nc.scalar.activation(y[:], readout[n][:], ACT.Copy, scale=-1.0)
+                nc.sync.dma_start(out_0[n * P : (n + 1) * P, j0 : j0 + w], y[:])
 
         gather_scales(0)
-        deal_wi_scales(0)
         gather_scales(1)
-        gather_words(0)
         deal_wi_words(0)
+        deal_wi_scales(0)
+        gather_words(0)
         for n in range(AHEAD):
             square_in_phase(n)
         gather_words(1)
@@ -270,8 +288,7 @@ def tile_list_sonar_envelopes_kernel(
             4: [lambda: quantize_wq(1, 0), lambda: quantize_wq(1, 1)],
             7: [lambda: round_wd(0)],
             8: [lambda: round_wd(1)],
-            11: [lambda: quantize_wd(0), lambda: quantize_wd(1), lambda: quantize_wd(2),
-                 lambda: open_readout(0), lambda: add_readout(0)],
+            11: [lambda: quantize_wd(0), lambda: quantize_wd(1), lambda: quantize_wd(2), lambda: open_readout(2)],
         }
         for n in range(len(steps) + LAG + 1):
             if n < len(steps):
@@ -282,18 +299,13 @@ def tile_list_sonar_envelopes_kernel(
             if 0 <= done < len(steps):
                 envelope(done)
                 if steps[done][1] == PACK - 1:
-                    round_env(steps[done][0], 0)
-                    round_env(steps[done][0], 1)
+                    round_env(steps[done][0])
             if done >= 1 and steps[done - 1][1] == PACK - 1:
                 u = steps[done - 1][0]
                 quantize_env(u)
-                if u == 2:
-                    add_readout(2)
-                    store_readout(0)
-                    open_readout(1)
-                    add_readout(1)
-                if u == 3:
-                    add_readout(3)
-                    store_readout(1)
+                if units[u][0] == GROUPS - 1:
+                    close_readout(u)
+                    if u + 1 < len(units):
+                        open_readout(u + 1)
             for chore in chores.get(n, []):
                 chore()

@@ -1,6 +1,7 @@
 from contextlib import ExitStack
 
 import concourse.mybir as mybir
+from concourse.masks import make_identity
 
 K, H, N, T, S = 512, 1024, 384, 4096, 1024
 FLOPS = 2 * (2 * K * H * S + K * N * S + H * N * S)
@@ -25,6 +26,7 @@ HALVES = S // W
 NT = N // P
 AHEAD = 4
 LAG = 2
+ON_VECTOR = (5, 7)
 
 
 def tile_list_sonar_envelopes_kernel(
@@ -102,30 +104,19 @@ def tile_list_sonar_envelopes_kernel(
         def gather_words(b):
             nc.vector.tensor_copy(v_words[b][:], tab[:].bitcast(U32).indirect(part(b)))
 
-        wi_codes = [held([P, PASS], I32, "wi_codes%d" % g) for g in range(GROUPS)]
-        wi_plane = [held([P, PASS], U8, "wi_plane%d" % g) for g in range(GROUPS)]
-
-        def deal_wi_scales(g):
-            nc.vector.tensor_copy(
-                wi_plane[g][:].rearrange("p (t m) -> p m t", t=PACK),
-                w_plane[:, g * PASS : (g + 1) * PASS].rearrange("p (m t) -> p m t", t=PACK),
-            )
-
-        def deal_wi_words(g):
-            nc.vector.tensor_copy(
-                wi_codes[g][:].rearrange("p (t m) -> p m t", t=PACK),
-                wi_raw[g][:].rearrange("p (m t) -> p m t", t=PACK),
-            )
+        ident = held([P, P], F32, "ident")
+        make_identity(nc, ident[:])
 
         wq_bf = [held([P, PACK * PASS], BF16, "wq_bf%d" % g) for g in range(GROUPS)]
-        wq_codes = [held([P, PASS], U32, "wq_codes%d" % g) for g in range(GROUPS)]
+        wq_codes = [held([P, PASS], I32, "wq_codes%d" % g) for g in range(GROUPS)]
         wq_plane = [held([P, PASS], U8, "wq_plane%d" % g) for g in range(GROUPS)]
+        nc.vector.memset(wq_plane[1][:].bitcast(I32), 0)
 
         def round_wq(g, half):
-            m = slice(half * (P // 2), (half + 1) * (P // 2))
+            c = slice(half * (PASS // 4), (half + 1) * (PASS // 4))
             nc.vector.tensor_copy(
-                wq_bf[g][:].rearrange("p (t m i) -> p m i t", t=PACK, i=PACK)[:, m],
-                wq_raw[g][:].rearrange("p i (m t) -> p m i t", t=PACK)[:, m],
+                wq_bf[g][:].rearrange("p (c e i) -> p c i e", e=2, i=PACK)[:, c],
+                wq_raw[g][:].rearrange("p i (c e) -> p c i e", e=2)[:, c],
             )
 
         def quantize_wq(g, half):
@@ -135,14 +126,29 @@ def tile_list_sonar_envelopes_kernel(
                 out=wq_codes[g][:, c].bitcast(FP8X4), scales=wq_plane[g][:, c], in_=wq_bf[g][:, e]
             )
 
+        def deal(words, scales, name):
+            dealt_words = held([P, PASS], I32, name + "_words")
+            dealt_scales = held([P, PASS], U8, name + "_scales")
+            nc.vector.tensor_copy(
+                dealt_words[:].rearrange("p (t c m) -> p c t m", t=PACK, m=4),
+                words.rearrange("p (c m t) -> p c t m", m=4, t=PACK),
+            )
+            nc.vector.tensor_copy(
+                dealt_scales[:].rearrange("p (t c m) -> p c t m", t=PACK, m=16),
+                scales.rearrange("p (c m t) -> p c t m", m=16, t=PACK),
+            )
+            dealt[name] = (dealt_words, dealt_scales)
+
+        dealt = {}
+
         wd_bf = held([P, GROUPS * N * PACK], BF16, "wd_bf")
         wd_codes = held([P, GROUPS * N], U32, "wd_codes")
         wd_plane = held([P, GROUPS * N], U8, "wd_plane")
 
         def round_wd(g):
             nc.vector.tensor_scalar(
-                out=wd_bf[:, g * N * PACK : (g + 1) * N * PACK].rearrange("p (c e i) -> p c i e", e=4, i=PACK),
-                in0=wd_raw[:, g, :].rearrange("p (i c e) -> p c i e", i=PACK, e=4),
+                out=wd_bf[:, g * N * PACK : (g + 1) * N * PACK].rearrange("p (c e i) -> p c i e", e=2, i=PACK),
+                in0=wd_raw[:, g, :].rearrange("p (i c e) -> p c i e", i=PACK, e=2),
                 scalar1=-1.0,
                 scalar2=None,
                 op0=ALU.mult,
@@ -160,51 +166,88 @@ def tile_list_sonar_envelopes_kernel(
         env_codes = [held([P, w], U32, "env_codes%d" % u) for u, (g, j0, w) in enumerate(units)]
         env_plane = [held([P, S], U8, "env_plane%d" % g) for g in range(GROUPS)]
         out_1_rows = out_1.rearrange("(g p t) j -> g p t j", g=GROUPS, t=PACK)
-        in_phase, power = {}, {}
+        in_phase, quadrature, power = {}, {}, {}
 
         def snapshots(j0, w):
             cols = slice(j0 % W, j0 % W + w)
             return v_words[j0 // W][:, cols].bitcast(FP8X4), v_scales[j0 // W][:, cols]
 
-        def squared_beam(codes, plane, n, name, bufs):
+        def squared_beam(which, n, bufs):
             u, t = steps[n]
             g, j0, w = units[u]
+            bank = beams.tile([P, w], F32, name="bank")
+            square = ring.tile([P, w], F32, name=which + "_square", bufs=bufs)
+            if g == 0:
+                words, scales = snapshots(j0 + t * P, P)
+                w_words, w_scales = (
+                    (wi_raw[0][:], w_plane[:, 0:PASS]) if which == "wi" else (wq_codes[0][:], wq_plane[0][:])
+                )
+                nc.tensor.matmul_mx(
+                    out=bank[:], lhsT=words, lhsT_scale=scales, rhs=w_words.bitcast(FP8X4), rhs_scale=w_scales,
+                    start=True, stop=True,
+                )
+                source = bank[:].rearrange("p (m t) -> p t m", t=PACK)
+                target = square[:].rearrange("p (t m) -> p t m", t=PACK)
+                if which == "wq" and n in ON_VECTOR:
+                    plain = ring.tile([P, w], F32, name="plain", bufs=2)
+                    nc.vector.tensor_copy(plain[:].rearrange("p (t m) -> p t m", t=PACK), source)
+                    nc.vector.tensor_tensor(square[:], plain[:], plain[:], ALU.mult)
+                else:
+                    nc.scalar.activation(target, source, ACT.Square)
+                return square
             cols = slice(t * P, (t + 1) * P)
             words, scales = snapshots(j0, w)
-            bank = beams.tile([P, w], F32, name="bank")
             nc.tensor.matmul_mx(
                 out=bank[:],
-                lhsT=codes[g][:, cols].bitcast(FP8X4),
-                lhsT_scale=plane[g][:, cols],
+                lhsT=dealt[which][0][:, cols].bitcast(FP8X4),
+                lhsT_scale=dealt[which][1][:, cols],
                 rhs=words,
                 rhs_scale=scales,
                 start=True,
                 stop=True,
             )
-            square = ring.tile([P, w], F32, name=name, bufs=bufs)
             nc.scalar.activation(square[:], bank[:], ACT.Square)
             return square
 
         def square_in_phase(n):
-            in_phase[n] = squared_beam(wi_codes, wi_plane, n, "bi2", AHEAD + 5)
+            in_phase[n] = squared_beam("wi", n, 13)
 
         def add_quadrature(n):
-            quad = squared_beam(wq_codes, wq_plane, n, "bq2", 3)
-            power[n] = ring.tile([P, units[steps[n][0]][2]], F32, name="power", bufs=LAG + 2)
-            nc.vector.tensor_tensor(power[n][:], in_phase[n][:], quad[:], ALU.add)
+            quadrature[n] = squared_beam("wq", n, 9)
+            if units[steps[n][0]][0] == 1:
+                power[n] = ring.tile([P, units[steps[n][0]][2]], F32, name="power", bufs=LAG + 2)
+                nc.vector.tensor_tensor(power[n][:], in_phase[n][:], quadrature[n][:], ALU.add)
+
+        def turn_and_add(n):
+            u, t = steps[n]
+            power[n] = reads.tile([P, W], F32, name="wide")
+            parts = [(squares[PACK * u + c], c) for squares in (in_phase, quadrature) for c in range(PACK)]
+            for i, (square, c) in enumerate(parts):
+                nc.tensor.matmul(
+                    power[n][:, c * P : (c + 1) * P],
+                    lhsT=square[:, t * P : (t + 1) * P],
+                    rhs=ident[:],
+                    is_transpose=True,
+                    start=(i == 0),
+                    stop=(i == len(parts) - 1),
+                )
 
         def envelope(n):
             u, t = steps[n]
             g, j0, w = units[u]
+            if g == 0:
+                turn_and_add(n)
             nc.scalar.activation(env[u][:, t, :], power[n][:], ACT.Sqrt, bias=amb_sb[:, g, t : t + 1])
             if t % 2 == 1:
                 nc.sync.dma_start(out_1_rows[g, :, t - 1 : t + 1, j0 : j0 + w], env[u][:, t - 1 : t + 1, :])
+            if t == PACK - 1:
+                round_env(u)
 
         def round_env(u):
-            for c0 in range(0, units[u][2] // 4, 64):
+            for c0 in range(0, units[u][2] // 2, 128):
                 nc.vector.tensor_copy(
-                    env_bf[u][:].rearrange("p (c e t) -> p c t e", e=4, t=PACK)[:, c0 : c0 + 64],
-                    env[u][:].rearrange("p t (c e) -> p c t e", e=4)[:, c0 : c0 + 64],
+                    env_bf[u][:].rearrange("p (c e t) -> p c t e", e=2, t=PACK)[:, c0 : c0 + 128],
+                    env[u][:].rearrange("p t (c e) -> p c t e", e=2)[:, c0 : c0 + 128],
                 )
 
         def quantize_env(u):
@@ -242,7 +285,7 @@ def tile_list_sonar_envelopes_kernel(
             g, j0, w = units[u]
             piece = W if w == W else P
             for n in range(NT):
-                readout[n] = reads.tile([P, w], F32, name="readout")
+                readout[n] = reads.tile([P, w], F32, name="wide")
                 for c0 in range(0, w, piece):
                     words, scales = snapshots(j0 + c0, piece)
                     nc.tensor.matmul_mx(
@@ -269,8 +312,6 @@ def tile_list_sonar_envelopes_kernel(
 
         gather_scales(0)
         gather_scales(1)
-        deal_wi_words(0)
-        deal_wi_scales(0)
         gather_words(0)
         for n in range(AHEAD):
             square_in_phase(n)
@@ -281,31 +322,32 @@ def tile_list_sonar_envelopes_kernel(
         quantize_wq(0, 1)
 
         chores = {
-            0: [lambda: deal_wi_scales(1)],
-            1: [lambda: deal_wi_words(1)],
-            2: [lambda: round_wq(1, 0)],
-            3: [lambda: round_wq(1, 1)],
-            4: [lambda: quantize_wq(1, 0), lambda: quantize_wq(1, 1)],
-            7: [lambda: round_wd(0)],
-            8: [lambda: round_wd(1)],
-            11: [lambda: quantize_wd(0), lambda: quantize_wd(1), lambda: quantize_wd(2), lambda: open_readout(2)],
+            0: [lambda: deal(wi_raw[1][:], w_plane[:, PASS:H], "wi")],
+            1: [lambda: round_wq(1, 0), lambda: round_wq(1, 1)],
+            2: [lambda: quantize_wq(1, 0), lambda: quantize_wq(1, 1)],
+            3: [lambda: deal(wq_codes[1][:], wq_plane[1][:], "wq")],
+            4: [lambda: round_wd(0)],
+            5: [lambda: round_wd(1)],
+            6: [lambda: quantize_wd(0), lambda: quantize_wd(1), lambda: quantize_wd(2)],
         }
+        turned = 2 * PACK
+        due = {}
+        for n in range(len(steps)):
+            due.setdefault(n + (PACK if n < turned else LAG), []).append(n)
         for n in range(len(steps) + LAG + 1):
             if n < len(steps):
                 add_quadrature(n)
             if n + AHEAD < len(steps):
                 square_in_phase(n + AHEAD)
-            done = n - LAG
-            if 0 <= done < len(steps):
-                envelope(done)
-                if steps[done][1] == PACK - 1:
-                    round_env(steps[done][0])
-            if done >= 1 and steps[done - 1][1] == PACK - 1:
-                u = steps[done - 1][0]
-                quantize_env(u)
-                if units[u][0] == GROUPS - 1:
-                    close_readout(u)
-                    if u + 1 < len(units):
+            for done in due.get(n - 1, []):
+                u, t = steps[done]
+                if t == PACK - 1:
+                    quantize_env(u)
+                    if units[u][0] == GROUPS - 1:
+                        close_readout(u)
+                    if 1 <= u < len(units) - 1:
                         open_readout(u + 1)
+            for done in due.get(n, []):
+                envelope(done)
             for chore in chores.get(n, []):
                 chore()

@@ -20,13 +20,28 @@ ALU = mybir.AluOpType
 P = 128
 PACK = 4
 PASS = P * PACK
-W = 512
+BANK = 512
 GROUPS = H // PASS
-HALVES = S // W
-NT = N // P
-AHEAD = 4
-LAG = 2
-ON_VECTOR = (5, 7)
+HALVES = S // BANK
+ROW_TILES = N // P
+LIST_ROWS = 16
+SCALE_ROWS = PASS // 32
+WI_ROW = 4
+TURNED, DIRECT = 0, 1
+TAB_FIRST = T // 4
+PIECE = 1024
+
+UNITS = (
+    (TURNED, 0, BANK),
+    (DIRECT, 0, BANK),
+    (TURNED, BANK, BANK),
+    (DIRECT, BANK, BANK // 2),
+    (DIRECT, BANK + BANK // 2, BANK // 2),
+)
+FIRST, SECOND, THIRD, FOURTH, LAST = range(len(UNITS))
+SQUARES_ON_VECTOR = 3
+SQUARE_EVERY = 3
+WD_STEP = 3
 
 
 def tile_list_sonar_envelopes_kernel(
@@ -37,317 +52,333 @@ def tile_list_sonar_envelopes_kernel(
     with ExitStack() as ctx:
         lists = ctx.enter_context(tc.tile_pool(name="lists", bufs=1))
         keep = ctx.enter_context(tc.tile_pool(name="keep", bufs=1))
-        ring = ctx.enter_context(tc.tile_pool(name="ring", bufs=3))
-        beams = ctx.enter_context(tc.psum_pool(name="beams", bufs=5))
-        reads = ctx.enter_context(tc.psum_pool(name="reads", bufs=3))
+        ring = ctx.enter_context(tc.tile_pool(name="ring", bufs=PACK + 2))
+        beam_banks = ctx.enter_context(tc.psum_pool(name="beam_banks", bufs=3))
+        side_bank = ctx.enter_context(tc.psum_pool(name="side_bank", bufs=1))
+        sum_banks = ctx.enter_context(tc.psum_pool(name="sum_banks", bufs=2))
+        read_banks = ctx.enter_context(tc.psum_pool(name="read_banks", bufs=2))
 
         def held(shape, dtype, name):
             return keep.tile(shape, dtype, name=name, align_bytes=64)
 
-        offsets = lists.tile([P, S // 16], U16, name="offsets")
+        offsets = lists.tile([P, S // LIST_ROWS], U16, name="offsets")
         nc.sync.dma_start(offsets[:], offs)
 
         tab = held([P, T], I32, "tab")
         tab_dram = tab_words[0].rearrange("p t i -> p (t i)").bitcast(I32)
-        nc.sync.dma_start(tab[:, 0:1024], tab_dram[:, 0:1024])
+        nc.sync.dma_start(tab[:, 0:TAB_FIRST], tab_dram[:, 0:TAB_FIRST])
 
         tab_plane = held([P, T], U8, "tab_plane")
         nc.vector.memset(tab_plane[:].bitcast(I32), 0)
-        w_plane = held([P, H], U8, "w_plane")
-        nc.vector.memset(w_plane[:].bitcast(I32), 0)
+        wi_plane = held([P, H], U8, "wi_plane")
+        nc.vector.memset(wi_plane[:].bitcast(I32), 0)
         wc_plane = held([P, N], U8, "wc_plane")
         nc.vector.memset(wc_plane[:].bitcast(I32), 0)
 
-        def load_scale_rows(queue, plane, rows):
-            for q in range(4):
-                queue.dma_start(
-                    plane[32 * q : 32 * q + 4, :].bitcast(I32), rows[4 * q : 4 * q + 4, :].bitcast(I32)
-                )
+        def load_plane(plane, rows, first_row):
+            for s in range(4):
+                nc.sync.dma_start(plane[first_row + s : P : 32, :].bitcast(I32), rows[s:SCALE_ROWS:4, :].bitcast(I32))
 
-        load_scale_rows(nc.sync, tab_plane, tab_scales[0])
-        nc.sync.dma_start(tab[:, 1024:2560], tab_dram[:, 1024:2560])
-        load_scale_rows(nc.sync, w_plane, wi_scales[0])
-
-        warm = held([P, 1], F32, "warm")
-        nc.vector.memset(warm[:], 1.0)
-        warm_out = held([P, 1], F32, "warm_out")
-        nc.scalar.activation(warm_out[:], warm[:], ACT.Sqrt)
+        load_plane(tab_plane, tab_scales[0], 0)
+        nc.sync.dma_start(tab[:, TAB_FIRST:T], tab_dram[:, TAB_FIRST:T])
+        load_plane(wi_plane, wi_scales[0], WI_ROW)
 
         wi_dram = wi_words[0].rearrange("p c i -> p (c i)").bitcast(I32)
         wq_dram = wq.rearrange("(p i) c -> p i c", i=PACK)
-        wi_raw, wq_raw = [], []
-        amb_sb = held([P, GROUPS, PACK], F32, "amb_sb")
+        wi_codes, wq_raw = [], []
         for g in range(GROUPS):
-            wi_raw.append(held([P, PASS], I32, "wi_raw%d" % g))
-            nc.sync.dma_start(wi_raw[g][:], wi_dram[:, g * PASS : (g + 1) * PASS])
-            if g == 0:
-                nc.sync.dma_start(tab[:, 2560:T], tab_dram[:, 2560:T])
+            wi_codes.append(held([P, PASS], I32, "wi_codes%d" % g))
+            nc.sync.dma_start(wi_codes[g][:], wi_dram[:, g * PASS : (g + 1) * PASS])
             wq_raw.append(held([P, PACK, PASS], F32, "wq_raw%d" % g))
             nc.sync.dma_start(wq_raw[g][:], wq_dram[:, :, g * PASS : (g + 1) * PASS])
-            if g == 0:
-                nc.sync.dma_start(amb_sb[:], amb.rearrange("(g p t) -> p g t", g=GROUPS, t=PACK))
+        ambient = held([P, GROUPS, PACK], F32, "ambient")
+        nc.sync.dma_start(ambient[:], amb.rearrange("(g p t) -> p g t", g=GROUPS, t=PACK))
         wd_raw = held([P, GROUPS, PACK * N], F32, "wd_raw")
         nc.sync.dma_start(wd_raw[:], wd.rearrange("(g p i) n -> p g (i n)", g=GROUPS, i=PACK))
-        wc = held([P, 2 * N], U8, "wc")
-        nc.sync.dma_start(wc[:].bitcast(I32), wc_words[0].bitcast(I32))
-        load_scale_rows(nc.sync, wc_plane, wc_scales[0])
-
-        v_words = [held([P, W], U32, "v_words%d" % b) for b in range(HALVES)]
-        v_scales = [held([P, W], U8, "v_scales%d" % b) for b in range(HALVES)]
-
-        def part(b):
-            return offsets[:, b * (W // 16) : (b + 1) * (W // 16)]
-
-        def gather_scales(b):
-            nc.vector.tensor_copy(v_scales[b][:], tab_plane[:].indirect(part(b)))
-
-        def gather_words(b):
-            nc.vector.tensor_copy(v_words[b][:], tab[:].bitcast(U32).indirect(part(b)))
+        wc_codes = held([P, 2 * N], U8, "wc_codes")
+        nc.sync.dma_start(wc_codes[:].bitcast(I32), wc_words[0].bitcast(I32))
+        load_plane(wc_plane, wc_scales[0], 0)
 
         ident = held([P, P], F32, "ident")
         make_identity(nc, ident[:])
 
-        wq_bf = [held([P, PACK * PASS], BF16, "wq_bf%d" % g) for g in range(GROUPS)]
+        v_codes = [held([P, BANK], U32, "v_codes%d" % b) for b in range(HALVES)]
+        v_plane = [held([P, BANK], U8, "v_plane%d" % b) for b in range(HALVES)]
+
+        def half_list(b):
+            return offsets[:, b * (BANK // LIST_ROWS) : (b + 1) * (BANK // LIST_ROWS)]
+
+        def gather_scales(b):
+            nc.vector.tensor_copy(v_plane[b][:], tab_plane[:].indirect(half_list(b)))
+
+        def gather_words(b):
+            nc.vector.tensor_copy(v_codes[b][:], tab[:].bitcast(U32).indirect(half_list(b)))
+
+        def snapshots(j0, width):
+            cols = slice(j0 % BANK, j0 % BANK + width)
+            return v_codes[j0 // BANK][:, cols].bitcast(FP8X4), v_plane[j0 // BANK][:, cols]
+
+        def by_row(rows):
+            return rows.rearrange("p i (c e) -> p c i e", e=2)
+
+        def by_column(packed):
+            return packed.rearrange("p (c e i) -> p c i e", e=2, i=PACK)
+
+        def round_rows(packed, rows):
+            pairs = PIECE // (2 * PACK)
+            for c0 in range(0, rows.shape[2] // 2, pairs):
+                nc.vector.tensor_copy(by_column(packed)[:, c0 : c0 + pairs], by_row(rows)[:, c0 : c0 + pairs])
+
+        def quantize_weight(codes, plane, packed):
+            cols = PIECE // PACK
+            for c0 in range(0, codes.shape[1], cols):
+                nc.vector.quantize_mx(
+                    out=codes[:, c0 : c0 + cols].bitcast(FP8X4),
+                    scales=plane[:, c0 : c0 + cols],
+                    in_=packed[:, c0 * PACK : (c0 + cols) * PACK],
+                )
+
         wq_codes = [held([P, PASS], I32, "wq_codes%d" % g) for g in range(GROUPS)]
         wq_plane = [held([P, PASS], U8, "wq_plane%d" % g) for g in range(GROUPS)]
-        nc.vector.memset(wq_plane[1][:].bitcast(I32), 0)
+        nc.vector.memset(wq_plane[DIRECT][:].bitcast(I32), 0)
 
-        def round_wq(g, half):
-            c = slice(half * (PASS // 4), (half + 1) * (PASS // 4))
-            nc.vector.tensor_copy(
-                wq_bf[g][:].rearrange("p (c e i) -> p c i e", e=2, i=PACK)[:, c],
-                wq_raw[g][:].rearrange("p i (c e) -> p c i e", e=2)[:, c],
-            )
+        def prepare_wq(g):
+            packed = held([P, PACK * PASS], BF16, "wq_packed%d" % g)
+            round_rows(packed[:], wq_raw[g][:])
+            quantize_weight(wq_codes[g], wq_plane[g], packed)
 
-        def quantize_wq(g, half):
-            c = slice(half * (PASS // 2), (half + 1) * (PASS // 2))
-            e = slice(half * 2 * PASS, (half + 1) * 2 * PASS)
-            nc.vector.quantize_mx(
-                out=wq_codes[g][:, c].bitcast(FP8X4), scales=wq_plane[g][:, c], in_=wq_bf[g][:, e]
-            )
+        wd_codes = held([P, GROUPS * N], U32, "wd_codes")
+        wd_plane = held([P, GROUPS * N], U8, "wd_plane")
+        wd_packed = held([P, GROUPS * N * PACK], BF16, "wd_packed")
 
-        def deal(words, scales, name):
-            dealt_words = held([P, PASS], I32, name + "_words")
-            dealt_scales = held([P, PASS], U8, name + "_scales")
-            nc.vector.tensor_copy(
-                dealt_words[:].rearrange("p (t c m) -> p c t m", t=PACK, m=4),
-                words.rearrange("p (c m t) -> p c t m", m=4, t=PACK),
-            )
-            nc.vector.tensor_copy(
-                dealt_scales[:].rearrange("p (t c m) -> p c t m", t=PACK, m=16),
-                scales.rearrange("p (c m t) -> p c t m", m=16, t=PACK),
-            )
-            dealt[name] = (dealt_words, dealt_scales)
+        def round_negated_wd():
+            for g in range(GROUPS):
+                nc.vector.tensor_scalar(
+                    out=by_column(wd_packed[:, g * N * PACK : (g + 1) * N * PACK]),
+                    in0=by_row(wd_raw[:, g, :].rearrange("p (i n) -> p i n", i=PACK)),
+                    scalar1=-1.0,
+                    scalar2=None,
+                    op0=ALU.mult,
+                )
 
         dealt = {}
 
-        wd_bf = held([P, GROUPS * N * PACK], BF16, "wd_bf")
-        wd_codes = held([P, GROUPS * N], U32, "wd_codes")
-        wd_plane = held([P, GROUPS * N], U8, "wd_plane")
+        def deal(name, codes, plane):
+            dealt[name] = (held([P, PASS], I32, name + "_dealt_codes"), held([P, PASS], U8, name + "_dealt_plane"))
+            for target, source, run in zip(dealt[name], (codes, plane), (4, 16)):
+                nc.vector.tensor_copy(
+                    target[:].rearrange("p (t c m) -> p c t m", t=PACK, m=run),
+                    source.rearrange("p (c m t) -> p c t m", m=run, t=PACK),
+                )
 
-        def round_wd(g):
-            nc.vector.tensor_scalar(
-                out=wd_bf[:, g * N * PACK : (g + 1) * N * PACK].rearrange("p (c e i) -> p c i e", e=2, i=PACK),
-                in0=wd_raw[:, g, :].rearrange("p (i c e) -> p c i e", i=PACK, e=2),
-                scalar1=-1.0,
-                scalar2=None,
-                op0=ALU.mult,
-            )
-
-        def quantize_wd(part_index):
-            c = slice(part_index * 256, (part_index + 1) * 256)
-            e = slice(part_index * 1024, (part_index + 1) * 1024)
-            nc.vector.quantize_mx(out=wd_codes[:, c].bitcast(FP8X4), scales=wd_plane[:, c], in_=wd_bf[:, e])
-
-        units = [(0, 0, W), (0, W, W), (1, 0, W), (1, W, W // 2), (1, W + W // 2, W // 2)]
-        steps = [(u, t) for u in range(len(units)) for t in range(PACK)]
-        env = [held([P, PACK, w], F32, "env%d" % u) for u, (g, j0, w) in enumerate(units)]
-        env_bf = [held([P, w * PACK], BF16, "env_bf%d" % u) for u, (g, j0, w) in enumerate(units)]
-        env_codes = [held([P, w], U32, "env_codes%d" % u) for u, (g, j0, w) in enumerate(units)]
+        steps = [(u, c) for u, (g, j0, width) in enumerate(UNITS) for c in range(width // P)]
+        env = [held([P, PACK, width], F32, "env%d" % u) for u, (g, j0, width) in enumerate(UNITS)]
+        env_packed = [held([P, width * PACK], BF16, "env_packed%d" % u) for u, (g, j0, width) in enumerate(UNITS)]
+        env_codes = {
+            (g, b): held([P, BANK], U32, "env_codes%d%d" % (g, b)) for g in range(GROUPS) for b in range(HALVES)
+        }
         env_plane = [held([P, S], U8, "env_plane%d" % g) for g in range(GROUPS)]
         out_1_rows = out_1.rearrange("(g p t) j -> g p t j", g=GROUPS, t=PACK)
-        in_phase, quadrature, power = {}, {}, {}
+        squares, power = {}, {}
 
-        def snapshots(j0, w):
-            cols = slice(j0 % W, j0 % W + w)
-            return v_words[j0 // W][:, cols].bitcast(FP8X4), v_scales[j0 // W][:, cols]
-
-        def squared_beam(which, n, bufs):
-            u, t = steps[n]
-            g, j0, w = units[u]
-            bank = beams.tile([P, w], F32, name="bank")
-            square = ring.tile([P, w], F32, name=which + "_square", bufs=bufs)
-            if g == 0:
-                words, scales = snapshots(j0 + t * P, P)
-                w_words, w_scales = (
-                    (wi_raw[0][:], w_plane[:, 0:PASS]) if which == "wi" else (wq_codes[0][:], wq_plane[0][:])
-                )
+        def beam_products(name, u, c, bank):
+            g, j0, width = UNITS[u]
+            first_row = WI_ROW if name == "wi" else 0
+            if g == TURNED:
+                codes, plane = (wi_codes[g], wi_plane) if name == "wi" else (wq_codes[g], wq_plane[g])
+                v, v_scale = snapshots(j0 + c * P, P)
                 nc.tensor.matmul_mx(
-                    out=bank[:], lhsT=words, lhsT_scale=scales, rhs=w_words.bitcast(FP8X4), rhs_scale=w_scales,
+                    out=bank[:], lhsT=v, lhsT_scale=v_scale, rhs=codes[:].bitcast(FP8X4),
+                    rhs_scale=plane[first_row:P, 0:PASS], start=True, stop=True,
+                )
+                return bank[:].rearrange("p (m t) -> p t m", t=PACK)
+            codes, plane = dealt[name]
+            v, v_scale = snapshots(j0, width)
+            per_bank = BANK // width
+            for i in range(per_bank):
+                t = c * per_bank + i
+                nc.tensor.matmul_mx(
+                    out=bank[:, i * width : (i + 1) * width], lhsT=codes[:, t * P : (t + 1) * P].bitcast(FP8X4),
+                    lhsT_scale=plane[first_row:P, t * P : (t + 1) * P], rhs=v, rhs_scale=v_scale,
                     start=True, stop=True,
                 )
-                source = bank[:].rearrange("p (m t) -> p t m", t=PACK)
-                target = square[:].rearrange("p (t m) -> p t m", t=PACK)
-                if which == "wq" and n in ON_VECTOR:
-                    plain = ring.tile([P, w], F32, name="plain", bufs=2)
-                    nc.vector.tensor_copy(plain[:].rearrange("p (t m) -> p t m", t=PACK), source)
-                    nc.vector.tensor_tensor(square[:], plain[:], plain[:], ALU.mult)
-                else:
-                    nc.scalar.activation(target, source, ACT.Square)
-                return square
-            cols = slice(t * P, (t + 1) * P)
-            words, scales = snapshots(j0, w)
-            nc.tensor.matmul_mx(
-                out=bank[:],
-                lhsT=dealt[which][0][:, cols].bitcast(FP8X4),
-                lhsT_scale=dealt[which][1][:, cols],
-                rhs=words,
-                rhs_scale=scales,
-                start=True,
-                stop=True,
-            )
-            nc.scalar.activation(square[:], bank[:], ACT.Square)
-            return square
+            return bank[:].rearrange("p (a m) -> p a m", a=PACK)
 
-        def square_in_phase(n):
-            in_phase[n] = squared_beam("wi", n, 13)
+        def square_tile(name, u, c):
+            if u == THIRD:
+                squares[name, u, c] = held([P, PACK, P], F32, "%s_square%d" % (name, c))
+            else:
+                squares[name, u, c] = ring.tile([P, PACK, P], F32, name=name + "_square")
+            return squares[name, u, c]
 
-        def add_quadrature(n):
-            quadrature[n] = squared_beam("wq", n, 9)
-            if units[steps[n][0]][0] == 1:
-                power[n] = ring.tile([P, units[steps[n][0]][2]], F32, name="power", bufs=LAG + 2)
-                nc.vector.tensor_tensor(power[n][:], in_phase[n][:], quadrature[n][:], ALU.add)
+        def square_on_scalar(name, u, c):
+            products = beam_products(name, u, c, beam_banks.tile([P, BANK], F32, name="beam_bank"))
+            nc.scalar.activation(square_tile(name, u, c)[:], products, ACT.Square)
 
-        def turn_and_add(n):
-            u, t = steps[n]
-            power[n] = reads.tile([P, W], F32, name="wide")
-            parts = [(squares[PACK * u + c], c) for squares in (in_phase, quadrature) for c in range(PACK)]
-            for i, (square, c) in enumerate(parts):
-                nc.tensor.matmul(
-                    power[n][:, c * P : (c + 1) * P],
-                    lhsT=square[:, t * P : (t + 1) * P],
-                    rhs=ident[:],
-                    is_transpose=True,
-                    start=(i == 0),
-                    stop=(i == len(parts) - 1),
-                )
+        def square_on_vector(name, u, c):
+            products = beam_products(name, u, c, side_bank.tile([P, BANK], F32, name="side"))
+            plain = ring.tile([P, PACK, P], F32, name="plain", bufs=2)
+            nc.vector.tensor_copy(plain[:], products)
+            nc.vector.tensor_tensor(square_tile(name, u, c)[:], plain[:], plain[:], ALU.mult)
 
-        def envelope(n):
-            u, t = steps[n]
-            g, j0, w = units[u]
-            if g == 0:
-                turn_and_add(n)
-            nc.scalar.activation(env[u][:, t, :], power[n][:], ACT.Sqrt, bias=amb_sb[:, g, t : t + 1])
+        def add_squares(u, c):
+            power[u, c] = ring.tile([P, PACK, P], F32, name="power")
+            nc.vector.tensor_tensor(power[u, c][:], squares["wi", u, c][:], squares["wq", u, c][:], ALU.add)
+
+        def root(u, t, source):
+            g, j0, width = UNITS[u]
+            nc.scalar.activation(env[u][:, t, :], source, ACT.Sqrt, bias=ambient[:, g, t : t + 1])
             if t % 2 == 1:
-                nc.sync.dma_start(out_1_rows[g, :, t - 1 : t + 1, j0 : j0 + w], env[u][:, t - 1 : t + 1, :])
+                nc.sync.dma_start(out_1_rows[g, :, t - 1 : t + 1, j0 : j0 + width], env[u][:, t - 1 : t + 1, :])
             if t == PACK - 1:
-                round_env(u)
+                round_rows(env_packed[u][:], env[u][:])
 
-        def round_env(u):
-            for c0 in range(0, units[u][2] // 2, 128):
-                nc.vector.tensor_copy(
-                    env_bf[u][:].rearrange("p (c e t) -> p c t e", e=2, t=PACK)[:, c0 : c0 + 128],
-                    env[u][:].rearrange("p t (c e) -> p c t e", e=2)[:, c0 : c0 + 128],
-                )
+        def roots_direct(u, c):
+            width = UNITS[u][2]
+            per_bank = BANK // width
+            for i in range(per_bank):
+                root(u, c * per_bank + i, power[u, c][:].rearrange("p a m -> p (a m)")[:, i * width : (i + 1) * width])
+
+        def roots_turned(u):
+            tiles = UNITS[u][2] // P
+            for t in range(PACK):
+                bank = sum_banks.tile([P, BANK], F32, name="sum")
+                for c in range(tiles):
+                    for name in ("wi", "wq"):
+                        nc.tensor.matmul(
+                            bank[:, c * P : (c + 1) * P], lhsT=squares[name, u, c][:, t, :], rhs=ident[:],
+                            is_transpose=True, start=(c == 0 and name == "wi"), stop=(c == tiles - 1 and name == "wq"),
+                        )
+                root(u, t, bank[:])
 
         def quantize_env(u):
-            g, j0, w = units[u]
+            g, j0, width = UNITS[u]
+            codes = env_codes[g, j0 // BANK]
             nc.vector.quantize_mx(
-                out=env_codes[u][:].bitcast(FP8X4), scales=env_plane[g][:, j0 : j0 + w], in_=env_bf[u][:]
+                out=codes[:, j0 % BANK : j0 % BANK + width].bitcast(FP8X4),
+                scales=env_plane[g][:, j0 : j0 + width],
+                in_=env_packed[u][:],
             )
-            nc.sync.dma_start(
-                out_2[g].rearrange("p m t -> p (m t)").bitcast(I32)[:, j0 : j0 + w], env_codes[u][:].bitcast(I32)
-            )
-            if j0 + w == S:
-                for q in range(4):
+            end = j0 + width
+            if end % BANK == 0:
+                out_2_words = out_2[g].rearrange("p m t -> p (m t)").bitcast(I32)
+                nc.sync.dma_start(out_2_words[:, end - BANK : end], codes[:].bitcast(I32))
+            if end == S:
+                for s in range(4):
                     nc.sync.dma_start(
-                        out_3[g, 4 * q : 4 * q + 4, :].bitcast(I32),
-                        env_plane[g][32 * q : 32 * q + 4, :].bitcast(I32),
+                        out_3[g, s:SCALE_ROWS:4, :].bitcast(I32), env_plane[g][s:P:32, :].bitcast(I32)
                     )
 
+        out_0_rows = out_0.rearrange("(n p) j -> p n j", p=P)
+        y = {u: held([P, ROW_TILES, UNITS[u][2]], F32, "y%d" % u) for u in (SECOND, FOURTH, LAST)}
         readout = {}
 
-        def add_readout(u, j0, w):
-            g, first, width = units[u]
-            for n in range(NT):
+        def bank_rows(u):
+            per_bank = BANK // UNITS[u][2]
+            return [range(n0, min(n0 + per_bank, ROW_TILES)) for n0 in range(0, ROW_TILES, per_bank)]
+
+        def add_envelopes(g, u, rows):
+            j0, width = UNITS[u][1:]
+            for n in rows:
                 cols = slice(g * N + n * P, g * N + (n + 1) * P)
                 nc.tensor.matmul_mx(
-                    out=readout[n][:],
+                    out=readout[u, rows][:, n - rows.start, :],
                     lhsT=wd_codes[:, cols].bitcast(FP8X4),
                     lhsT_scale=wd_plane[:, cols],
-                    rhs=env_codes[u][:, j0 - first : j0 - first + w].bitcast(FP8X4),
-                    rhs_scale=env_plane[g][:, j0 : j0 + w],
+                    rhs=env_codes[g, j0 // BANK][:, j0 % BANK : j0 % BANK + width].bitcast(FP8X4),
+                    rhs_scale=env_plane[g][:, j0 : j0 + width],
                     start=False,
-                    stop=(g == GROUPS - 1),
+                    stop=(g == DIRECT and n == rows.stop - 1),
                 )
 
-        def open_readout(u):
-            g, j0, w = units[u]
-            piece = W if w == W else P
-            for n in range(NT):
-                readout[n] = reads.tile([P, w], F32, name="wide")
-                for c0 in range(0, w, piece):
-                    words, scales = snapshots(j0 + c0, piece)
+        def open_readout(u, rows, pool, tag):
+            j0, width = UNITS[u][1:]
+            readout[u, rows] = pool.tile([P, len(rows), width], F32, name=tag)
+            piece = BANK if width == BANK else P
+            for n in rows:
+                for c0 in range(0, width, piece):
+                    v, v_scale = snapshots(j0 + c0, piece)
                     nc.tensor.matmul_mx(
-                        out=readout[n][:, c0 : c0 + piece],
-                        lhsT=wc[:, 2 * n * P : 2 * (n + 1) * P].bitcast(FP4X4),
+                        out=readout[u, rows][:, n - rows.start, c0 : c0 + piece],
+                        lhsT=wc_codes[:, 2 * n * P : 2 * (n + 1) * P].bitcast(FP4X4),
                         lhsT_scale=wc_plane[:, n * P : (n + 1) * P],
-                        rhs=words,
-                        rhs_scale=scales,
-                        start=(c0 == 0),
+                        rhs=v,
+                        rhs_scale=v_scale,
+                        start=(n == rows.start and c0 == 0),
                         stop=False,
                     )
-            add_readout(j0 // W, j0, w)
+            add_envelopes(TURNED, u, rows)
 
         def close_readout(u):
-            g, j0, w = units[u]
-            add_readout(u, j0, w)
-            for n in range(NT):
-                y = ring.tile([P, w], F32, name="y")
-                if n == 1 or w == W:
-                    nc.vector.tensor_scalar(out=y[:], in0=readout[n][:], scalar1=-1.0, scalar2=None, op0=ALU.mult)
+            j0, width = UNITS[u][1:]
+            for rows in bank_rows(u):
+                add_envelopes(DIRECT, u, rows)
+                target = y[u][:, rows.start : rows.stop, :]
+                if width < BANK and rows.start == 0:
+                    nc.scalar.activation(target, readout[u, rows][:], ACT.Copy, scale=-1.0)
                 else:
-                    nc.scalar.activation(y[:], readout[n][:], ACT.Copy, scale=-1.0)
-                nc.sync.dma_start(out_0[n * P : (n + 1) * P, j0 : j0 + w], y[:])
+                    nc.vector.tensor_scalar(
+                        out=target, in0=readout[u, rows][:], scalar1=-1.0, scalar2=None, op0=ALU.mult
+                    )
+                if width == BANK:
+                    nc.sync.dma_start(out_0_rows[:, rows.start : rows.stop, j0 : j0 + width], target)
+            if width < BANK:
+                nc.sync.dma_start(out_0_rows[:, :, j0 : j0 + width], y[u][:])
+
+        def after_rounding(u):
+            quantize_env(u)
+            if u == FIRST:
+                for rows in bank_rows(SECOND)[:2]:
+                    open_readout(SECOND, rows, read_banks, "read")
+            if u == SECOND:
+                open_readout(SECOND, bank_rows(SECOND)[2], side_bank, "side")
+            if u == THIRD:
+                for rows in bank_rows(FOURTH):
+                    open_readout(FOURTH, rows, read_banks, "read")
+                for rows in bank_rows(LAST):
+                    open_readout(LAST, rows, sum_banks, "sum")
+            if UNITS[u][0] == DIRECT:
+                close_readout(u)
 
         gather_scales(0)
         gather_scales(1)
         gather_words(0)
-        for n in range(AHEAD):
-            square_in_phase(n)
+        for c in range(PACK):
+            square_on_scalar("wi", FIRST, c)
         gather_words(1)
-        round_wq(0, 0)
-        round_wq(0, 1)
-        quantize_wq(0, 0)
-        quantize_wq(0, 1)
+        for c in range(PACK):
+            square_on_scalar("wi", THIRD, c)
+        prepare_wq(TURNED)
 
-        chores = {
-            0: [lambda: deal(wi_raw[1][:], w_plane[:, PASS:H], "wi")],
-            1: [lambda: round_wq(1, 0), lambda: round_wq(1, 1)],
-            2: [lambda: quantize_wq(1, 0), lambda: quantize_wq(1, 1)],
-            3: [lambda: deal(wq_codes[1][:], wq_plane[1][:], "wq")],
-            4: [lambda: round_wd(0)],
-            5: [lambda: round_wd(1)],
-            6: [lambda: quantize_wd(0), lambda: quantize_wd(1), lambda: quantize_wd(2)],
-        }
-        turned = 2 * PACK
-        due = {}
-        for n in range(len(steps)):
-            due.setdefault(n + (PACK if n < turned else LAG), []).append(n)
-        for n in range(len(steps) + LAG + 1):
+        def prepare_direct_weights():
+            deal("wi", wi_codes[DIRECT][:], wi_plane[:, DIRECT * PASS : (DIRECT + 1) * PASS])
+            prepare_wq(DIRECT)
+            deal("wq", wq_codes[DIRECT][:], wq_plane[DIRECT][:])
+
+        for n in range(len(steps) + 2):
             if n < len(steps):
-                add_quadrature(n)
-            if n + AHEAD < len(steps):
-                square_in_phase(n + AHEAD)
-            for done in due.get(n - 1, []):
-                u, t = steps[done]
-                if t == PACK - 1:
-                    quantize_env(u)
-                    if units[u][0] == GROUPS - 1:
-                        close_readout(u)
-                    if 1 <= u < len(units) - 1:
-                        open_readout(u + 1)
-            for done in due.get(n, []):
-                envelope(done)
-            for chore in chores.get(n, []):
-                chore()
+                u, c = steps[n]
+                if ("wi", u, c) not in squares:
+                    square_on_scalar("wi", u, c)
+                if ("wq", u, c) not in squares:
+                    square_on_scalar("wq", u, c)
+                if UNITS[u][0] == DIRECT:
+                    add_squares(u, c)
+            if n >= 2:
+                u, c = steps[n - 2]
+                if c == UNITS[u][2] // P - 1:
+                    after_rounding(u)
+            if 1 <= n <= len(steps):
+                u, c = steps[n - 1]
+                if UNITS[u][0] == DIRECT:
+                    roots_direct(u, c)
+                elif c == PACK - 1:
+                    roots_turned(u)
+            if n == 0:
+                prepare_direct_weights()
+            if n == WD_STEP:
+                round_negated_wd()
+            if n == WD_STEP + 1:
+                quantize_weight(wd_codes, wd_plane, wd_packed)
+            if n % SQUARE_EVERY == 0 and n // SQUARE_EVERY < SQUARES_ON_VECTOR:
+                square_on_vector("wq", THIRD, n // SQUARE_EVERY)

@@ -25,7 +25,9 @@ GROUPS = H // PASS
 HALVES = S // BANK
 ROW_TILES = N // P
 LIST_ROWS = 16
+QUADRANT = 32
 SCALE_ROWS = PASS // 32
+LIVE_ROWS = 4
 WI_ROW = 4
 TURNED, DIRECT = 0, 1
 TAB_FIRST = T // 4
@@ -65,7 +67,7 @@ def tile_list_sonar_envelopes_kernel(
         nc.sync.dma_start(offsets[:], offs)
 
         tab = held([P, T], I32, "tab")
-        tab_dram = tab_words[0].rearrange("p t i -> p (t i)").bitcast(I32)
+        tab_dram = tab_words[0].rearrange("p col i -> p (col i)").bitcast(I32)
         nc.sync.dma_start(tab[:, 0:TAB_FIRST], tab_dram[:, 0:TAB_FIRST])
 
         tab_plane = held([P, T], U8, "tab_plane")
@@ -75,16 +77,23 @@ def tile_list_sonar_envelopes_kernel(
         wc_plane = held([P, N], U8, "wc_plane")
         nc.vector.memset(wc_plane[:].bitcast(I32), 0)
 
-        def load_plane(plane, rows, first_row):
-            for s in range(4):
-                nc.sync.dma_start(plane[first_row + s : P : 32, :].bitcast(I32), rows[s:SCALE_ROWS:4, :].bitcast(I32))
+        def load_plane(plane, scales, first_row):
+            for s in range(LIVE_ROWS):
+                nc.sync.dma_start(
+                    plane[first_row + s : P : QUADRANT, :].bitcast(I32), scales[s:SCALE_ROWS:LIVE_ROWS, :].bitcast(I32)
+                )
 
         load_plane(tab_plane, tab_scales[0], 0)
         nc.sync.dma_start(tab[:, TAB_FIRST:T], tab_dram[:, TAB_FIRST:T])
         load_plane(wi_plane, wi_scales[0], WI_ROW)
 
-        wi_dram = wi_words[0].rearrange("p c i -> p (c i)").bitcast(I32)
-        wq_dram = wq.rearrange("(p i) c -> p i c", i=PACK)
+        warm = held([P, 1], F32, "warm")
+        nc.vector.memset(warm[:], 1.0)
+        warm_out = held([P, 1], F32, "warm_out")
+        nc.scalar.activation(warm_out[:], warm[:], ACT.Sqrt)
+
+        wi_dram = wi_words[0].rearrange("p col i -> p (col i)").bitcast(I32)
+        wq_dram = wq.rearrange("(p i) col -> p i col", i=PACK)
         wi_codes, wq_raw = [], []
         for g in range(GROUPS):
             wi_codes.append(held([P, PASS], I32, "wi_codes%d" % g))
@@ -118,24 +127,25 @@ def tile_list_sonar_envelopes_kernel(
             cols = slice(j0 % BANK, j0 % BANK + width)
             return v_codes[j0 // BANK][:, cols].bitcast(FP8X4), v_plane[j0 // BANK][:, cols]
 
-        def by_row(rows):
-            return rows.rearrange("p i (c e) -> p c i e", e=2)
+        def by_row(source):
+            return source.rearrange("p i (pair e) -> p pair i e", e=2)
 
         def by_column(packed):
-            return packed.rearrange("p (c e i) -> p c i e", e=2, i=PACK)
+            return packed.rearrange("p (pair e i) -> p pair i e", e=2, i=PACK)
 
-        def round_rows(packed, rows):
+        def round_rows(packed, source):
             pairs = PIECE // (2 * PACK)
-            for c0 in range(0, rows.shape[2] // 2, pairs):
-                nc.vector.tensor_copy(by_column(packed)[:, c0 : c0 + pairs], by_row(rows)[:, c0 : c0 + pairs])
+            for first in range(0, source.shape[2] // 2, pairs):
+                part = slice(first, first + pairs)
+                nc.vector.tensor_copy(by_column(packed)[:, part], by_row(source)[:, part])
 
         def quantize_weight(codes, plane, packed):
-            cols = PIECE // PACK
-            for c0 in range(0, codes.shape[1], cols):
+            words = PIECE // PACK
+            for first in range(0, codes.shape[1], words):
                 nc.vector.quantize_mx(
-                    out=codes[:, c0 : c0 + cols].bitcast(FP8X4),
-                    scales=plane[:, c0 : c0 + cols],
-                    in_=packed[:, c0 * PACK : (c0 + cols) * PACK],
+                    out=codes[:, first : first + words].bitcast(FP8X4),
+                    scales=plane[:, first : first + words],
+                    in_=packed[:, first * PACK : (first + words) * PACK],
                 )
 
         wq_codes = [held([P, PASS], I32, "wq_codes%d" % g) for g in range(GROUPS)]
@@ -163,12 +173,12 @@ def tile_list_sonar_envelopes_kernel(
 
         dealt = {}
 
-        def deal(name, codes, plane):
-            dealt[name] = (held([P, PASS], I32, name + "_dealt_codes"), held([P, PASS], U8, name + "_dealt_plane"))
-            for target, source, run in zip(dealt[name], (codes, plane), (4, 16)):
+        def deal(beam, codes, plane):
+            dealt[beam] = (held([P, PASS], I32, beam + "_dealt_codes"), held([P, PASS], U8, beam + "_dealt_plane"))
+            for target, source, run in zip(dealt[beam], (codes, plane), (4, 16)):
                 nc.vector.tensor_copy(
-                    target[:].rearrange("p (t c m) -> p c t m", t=PACK, m=run),
-                    source.rearrange("p (c m t) -> p c t m", m=run, t=PACK),
+                    target[:].rearrange("p (t hi lo) -> p hi t lo", t=PACK, lo=run),
+                    source.rearrange("p (hi lo t) -> p hi t lo", lo=run, t=PACK),
                 )
 
         steps = [(u, c) for u, (g, j0, width) in enumerate(UNITS) for c in range(width // P)]
@@ -181,45 +191,46 @@ def tile_list_sonar_envelopes_kernel(
         out_1_rows = out_1.rearrange("(g p t) j -> g p t j", g=GROUPS, t=PACK)
         squares, power = {}, {}
 
-        def beam_products(name, u, c, bank):
+        def beam_products(beam, u, c, bank):
             g, j0, width = UNITS[u]
-            first_row = WI_ROW if name == "wi" else 0
+            first_row = WI_ROW if beam == "wi" else 0
             if g == TURNED:
-                codes, plane = (wi_codes[g], wi_plane) if name == "wi" else (wq_codes[g], wq_plane[g])
+                codes, plane = (wi_codes[g], wi_plane) if beam == "wi" else (wq_codes[g], wq_plane[g])
                 v, v_scale = snapshots(j0 + c * P, P)
                 nc.tensor.matmul_mx(
                     out=bank[:], lhsT=v, lhsT_scale=v_scale, rhs=codes[:].bitcast(FP8X4),
                     rhs_scale=plane[first_row:P, 0:PASS], start=True, stop=True,
                 )
                 return bank[:].rearrange("p (m t) -> p t m", t=PACK)
-            codes, plane = dealt[name]
+            codes, plane = dealt[beam]
             v, v_scale = snapshots(j0, width)
             per_bank = BANK // width
-            for i in range(per_bank):
-                t = c * per_bank + i
+            for place in range(per_bank):
+                t = c * per_bank + place
                 nc.tensor.matmul_mx(
-                    out=bank[:, i * width : (i + 1) * width], lhsT=codes[:, t * P : (t + 1) * P].bitcast(FP8X4),
+                    out=bank[:, place * width : (place + 1) * width],
+                    lhsT=codes[:, t * P : (t + 1) * P].bitcast(FP8X4),
                     lhsT_scale=plane[first_row:P, t * P : (t + 1) * P], rhs=v, rhs_scale=v_scale,
                     start=True, stop=True,
                 )
-            return bank[:].rearrange("p (a m) -> p a m", a=PACK)
+            return bank[:].rearrange("p (a z) -> p a z", a=PACK)
 
-        def square_tile(name, u, c):
+        def square_tile(beam, u, c):
             if u == THIRD:
-                squares[name, u, c] = held([P, PACK, P], F32, "%s_square%d" % (name, c))
+                squares[beam, u, c] = held([P, PACK, P], F32, "%s_square%d" % (beam, c))
             else:
-                squares[name, u, c] = ring.tile([P, PACK, P], F32, name=name + "_square")
-            return squares[name, u, c]
+                squares[beam, u, c] = ring.tile([P, PACK, P], F32, name=beam + "_square")
+            return squares[beam, u, c]
 
-        def square_on_scalar(name, u, c):
-            products = beam_products(name, u, c, beam_banks.tile([P, BANK], F32, name="beam_bank"))
-            nc.scalar.activation(square_tile(name, u, c)[:], products, ACT.Square)
+        def square_on_scalar(beam, u, c):
+            products = beam_products(beam, u, c, beam_banks.tile([P, BANK], F32, name="beam_bank"))
+            nc.scalar.activation(square_tile(beam, u, c)[:], products, ACT.Square)
 
-        def square_on_vector(name, u, c):
-            products = beam_products(name, u, c, side_bank.tile([P, BANK], F32, name="side"))
+        def square_on_vector(beam, u, c):
+            products = beam_products(beam, u, c, side_bank.tile([P, BANK], F32, name="side"))
             plain = ring.tile([P, PACK, P], F32, name="plain", bufs=2)
             nc.vector.tensor_copy(plain[:], products)
-            nc.vector.tensor_tensor(square_tile(name, u, c)[:], plain[:], plain[:], ALU.mult)
+            nc.vector.tensor_tensor(square_tile(beam, u, c)[:], plain[:], plain[:], ALU.mult)
 
         def add_squares(u, c):
             power[u, c] = ring.tile([P, PACK, P], F32, name="power")
@@ -236,18 +247,19 @@ def tile_list_sonar_envelopes_kernel(
         def roots_direct(u, c):
             width = UNITS[u][2]
             per_bank = BANK // width
-            for i in range(per_bank):
-                root(u, c * per_bank + i, power[u, c][:].rearrange("p a m -> p (a m)")[:, i * width : (i + 1) * width])
+            flat = power[u, c][:].rearrange("p a z -> p (a z)")
+            for place in range(per_bank):
+                root(u, c * per_bank + place, flat[:, place * width : (place + 1) * width])
 
         def roots_turned(u):
-            tiles = UNITS[u][2] // P
+            count = UNITS[u][2] // P
             for t in range(PACK):
                 bank = sum_banks.tile([P, BANK], F32, name="sum")
-                for c in range(tiles):
-                    for name in ("wi", "wq"):
+                for c in range(count):
+                    for beam in ("wi", "wq"):
                         nc.tensor.matmul(
-                            bank[:, c * P : (c + 1) * P], lhsT=squares[name, u, c][:, t, :], rhs=ident[:],
-                            is_transpose=True, start=(c == 0 and name == "wi"), stop=(c == tiles - 1 and name == "wq"),
+                            bank[:, c * P : (c + 1) * P], lhsT=squares[beam, u, c][:, t, :], rhs=ident[:],
+                            is_transpose=True, start=(c == 0 and beam == "wi"), stop=(c == count - 1 and beam == "wq"),
                         )
                 root(u, t, bank[:])
 
@@ -261,82 +273,82 @@ def tile_list_sonar_envelopes_kernel(
             )
             end = j0 + width
             if end % BANK == 0:
-                out_2_words = out_2[g].rearrange("p m t -> p (m t)").bitcast(I32)
+                out_2_words = out_2[g].rearrange("p j t -> p (j t)").bitcast(I32)
                 nc.sync.dma_start(out_2_words[:, end - BANK : end], codes[:].bitcast(I32))
             if end == S:
-                for s in range(4):
+                for s in range(LIVE_ROWS):
                     nc.sync.dma_start(
-                        out_3[g, s:SCALE_ROWS:4, :].bitcast(I32), env_plane[g][s:P:32, :].bitcast(I32)
+                        out_3[g, s:SCALE_ROWS:LIVE_ROWS, :].bitcast(I32), env_plane[g][s:P:QUADRANT, :].bitcast(I32)
                     )
 
         out_0_rows = out_0.rearrange("(n p) j -> p n j", p=P)
         y = {u: held([P, ROW_TILES, UNITS[u][2]], F32, "y%d" % u) for u in (SECOND, FOURTH, LAST)}
         readout = {}
 
-        def bank_rows(u):
+        def bank_tiles(u):
             per_bank = BANK // UNITS[u][2]
             return [range(n0, min(n0 + per_bank, ROW_TILES)) for n0 in range(0, ROW_TILES, per_bank)]
 
-        def add_envelopes(g, u, rows):
+        def add_envelopes(g, u, tiles):
             j0, width = UNITS[u][1:]
-            for n in rows:
+            for n in tiles:
                 cols = slice(g * N + n * P, g * N + (n + 1) * P)
                 nc.tensor.matmul_mx(
-                    out=readout[u, rows][:, n - rows.start, :],
+                    out=readout[u, tiles][:, n - tiles.start, :],
                     lhsT=wd_codes[:, cols].bitcast(FP8X4),
                     lhsT_scale=wd_plane[:, cols],
                     rhs=env_codes[g, j0 // BANK][:, j0 % BANK : j0 % BANK + width].bitcast(FP8X4),
                     rhs_scale=env_plane[g][:, j0 : j0 + width],
                     start=False,
-                    stop=(g == DIRECT and n == rows.stop - 1),
+                    stop=(g == DIRECT and n == tiles.stop - 1),
                 )
 
-        def open_readout(u, rows, pool, tag):
+        def open_readout(u, tiles, pool, tag):
             j0, width = UNITS[u][1:]
-            readout[u, rows] = pool.tile([P, len(rows), width], F32, name=tag)
+            readout[u, tiles] = pool.tile([P, len(tiles), width], F32, name=tag)
             piece = BANK if width == BANK else P
-            for n in rows:
-                for c0 in range(0, width, piece):
-                    v, v_scale = snapshots(j0 + c0, piece)
+            for n in tiles:
+                for first in range(0, width, piece):
+                    v, v_scale = snapshots(j0 + first, piece)
                     nc.tensor.matmul_mx(
-                        out=readout[u, rows][:, n - rows.start, c0 : c0 + piece],
+                        out=readout[u, tiles][:, n - tiles.start, first : first + piece],
                         lhsT=wc_codes[:, 2 * n * P : 2 * (n + 1) * P].bitcast(FP4X4),
                         lhsT_scale=wc_plane[:, n * P : (n + 1) * P],
                         rhs=v,
                         rhs_scale=v_scale,
-                        start=(n == rows.start and c0 == 0),
+                        start=(n == tiles.start and first == 0),
                         stop=False,
                     )
-            add_envelopes(TURNED, u, rows)
+            add_envelopes(TURNED, u, tiles)
 
         def close_readout(u):
             j0, width = UNITS[u][1:]
-            for rows in bank_rows(u):
-                add_envelopes(DIRECT, u, rows)
-                target = y[u][:, rows.start : rows.stop, :]
-                if width < BANK and rows.start == 0:
-                    nc.scalar.activation(target, readout[u, rows][:], ACT.Copy, scale=-1.0)
+            for tiles in bank_tiles(u):
+                add_envelopes(DIRECT, u, tiles)
+                target = y[u][:, tiles.start : tiles.stop, :]
+                if width < BANK and tiles.start == 0:
+                    nc.scalar.activation(target, readout[u, tiles][:], ACT.Copy, scale=-1.0)
                 else:
                     nc.vector.tensor_scalar(
-                        out=target, in0=readout[u, rows][:], scalar1=-1.0, scalar2=None, op0=ALU.mult
+                        out=target, in0=readout[u, tiles][:], scalar1=-1.0, scalar2=None, op0=ALU.mult
                     )
                 if width == BANK:
-                    nc.sync.dma_start(out_0_rows[:, rows.start : rows.stop, j0 : j0 + width], target)
+                    nc.sync.dma_start(out_0_rows[:, tiles.start : tiles.stop, j0 : j0 + width], target)
             if width < BANK:
                 nc.sync.dma_start(out_0_rows[:, :, j0 : j0 + width], y[u][:])
 
         def after_rounding(u):
             quantize_env(u)
             if u == FIRST:
-                for rows in bank_rows(SECOND)[:2]:
-                    open_readout(SECOND, rows, read_banks, "read")
+                for tiles in bank_tiles(SECOND)[:-1]:
+                    open_readout(SECOND, tiles, read_banks, "read")
             if u == SECOND:
-                open_readout(SECOND, bank_rows(SECOND)[2], side_bank, "side")
+                open_readout(SECOND, bank_tiles(SECOND)[-1], side_bank, "side")
             if u == THIRD:
-                for rows in bank_rows(FOURTH):
-                    open_readout(FOURTH, rows, read_banks, "read")
-                for rows in bank_rows(LAST):
-                    open_readout(LAST, rows, sum_banks, "sum")
+                for tiles in bank_tiles(FOURTH):
+                    open_readout(FOURTH, tiles, read_banks, "read")
+                for tiles in bank_tiles(LAST):
+                    open_readout(LAST, tiles, sum_banks, "sum")
             if UNITS[u][0] == DIRECT:
                 close_readout(u)
 
@@ -355,30 +367,29 @@ def tile_list_sonar_envelopes_kernel(
             prepare_wq(DIRECT)
             deal("wq", wq_codes[DIRECT][:], wq_plane[DIRECT][:])
 
-        for n in range(len(steps) + 2):
-            if n < len(steps):
-                u, c = steps[n]
-                if ("wi", u, c) not in squares:
-                    square_on_scalar("wi", u, c)
-                if ("wq", u, c) not in squares:
-                    square_on_scalar("wq", u, c)
+        for step in range(len(steps) + 2):
+            if step < len(steps):
+                u, c = steps[step]
+                for beam in ("wi", "wq"):
+                    if (beam, u, c) not in squares:
+                        square_on_scalar(beam, u, c)
                 if UNITS[u][0] == DIRECT:
                     add_squares(u, c)
-            if n >= 2:
-                u, c = steps[n - 2]
+            if step >= 2:
+                u, c = steps[step - 2]
                 if c == UNITS[u][2] // P - 1:
                     after_rounding(u)
-            if 1 <= n <= len(steps):
-                u, c = steps[n - 1]
+            if 1 <= step <= len(steps):
+                u, c = steps[step - 1]
                 if UNITS[u][0] == DIRECT:
                     roots_direct(u, c)
                 elif c == PACK - 1:
                     roots_turned(u)
-            if n == 0:
+            if step == 0:
                 prepare_direct_weights()
-            if n == WD_STEP:
+            if step == WD_STEP:
                 round_negated_wd()
-            if n == WD_STEP + 1:
+            if step == WD_STEP + 1:
                 quantize_weight(wd_codes, wd_plane, wd_packed)
-            if n % SQUARE_EVERY == 0 and n // SQUARE_EVERY < SQUARES_ON_VECTOR:
-                square_on_vector("wq", THIRD, n // SQUARE_EVERY)
+            if step % SQUARE_EVERY == 0 and step // SQUARE_EVERY < SQUARES_ON_VECTOR:
+                square_on_vector("wq", THIRD, step // SQUARE_EVERY)

@@ -16,6 +16,7 @@ FP8X4 = mybir.dt.float8_e4m3fn_x4
 FP4X4 = mybir.dt.float4_e2m1fn_x4
 ACT = mybir.ActivationFunctionType
 ALU = mybir.AluOpType
+AXIS = mybir.AxisListType
 
 P = 128
 PACK = 4
@@ -29,21 +30,18 @@ QUADRANT = 32
 SCALE_ROWS = PASS // 32
 LIVE_ROWS = 4
 WI_ROW = 4
-TURNED, DIRECT = 0, 1
 TAB_FIRST = T // 4
-PIECE = 1024
+SCALAR_BANKS = 5
+DEALT = 1
 
+TURNED, DIRECT = 0, 1
 UNITS = (
-    (TURNED, 0, BANK),
-    (DIRECT, 0, BANK),
-    (TURNED, BANK, BANK),
-    (DIRECT, BANK, BANK // 2),
-    (DIRECT, BANK + BANK // 2, BANK // 2),
+    (0, 0, 256, TURNED), (0, 256, 256, TURNED), (0, 512, 256, TURNED), (0, 768, 256, TURNED),
+    (1, 0, 256, DIRECT), (1, 256, 256, DIRECT), (1, 512, 256, DIRECT), (1, 768, 128, DIRECT), (1, 896, 128, DIRECT),
 )
-FIRST, SECOND, THIRD, FOURTH, LAST = range(len(UNITS))
-SQUARES_ON_VECTOR = 3
-SQUARE_EVERY = 3
-WD_STEP = 3
+ON_VECTOR = (("wq", 1, 0), ("wq", 2, 0), ("wq", 3, 0), ("wi", 7, 0))
+BLOCK = 256
+BLOCKS = S // BLOCK
 
 
 def tile_list_sonar_envelopes_kernel(
@@ -54,11 +52,14 @@ def tile_list_sonar_envelopes_kernel(
     with ExitStack() as ctx:
         lists = ctx.enter_context(tc.tile_pool(name="lists", bufs=1))
         keep = ctx.enter_context(tc.tile_pool(name="keep", bufs=1))
-        ring = ctx.enter_context(tc.tile_pool(name="ring", bufs=PACK + 2))
-        beam_banks = ctx.enter_context(tc.psum_pool(name="beam_banks", bufs=3))
-        side_bank = ctx.enter_context(tc.psum_pool(name="side_bank", bufs=1))
-        sum_banks = ctx.enter_context(tc.psum_pool(name="sum_banks", bufs=2))
-        read_banks = ctx.enter_context(tc.psum_pool(name="read_banks", bufs=2))
+        psum = ctx.enter_context(tc.psum_pool(name="psum", bufs=1))
+        banks = [psum.tile([P, BANK], F32, name="bank%d" % k) for k in range(8)]
+        rings = {"scalar": banks[:SCALAR_BANKS], "vector": banks[SCALAR_BANKS:]}
+        taken = {"scalar": [], "vector": []}
+
+        def take_bank(ring):
+            taken[ring].append(rings[ring][len(taken[ring]) % len(rings[ring])])
+            return taken[ring][-1]
 
         def held(shape, dtype, name):
             return keep.tile(shape, dtype, name=name, align_bytes=64)
@@ -77,6 +78,10 @@ def tile_list_sonar_envelopes_kernel(
         wc_plane = held([P, N], U8, "wc_plane")
         nc.vector.memset(wc_plane[:].bitcast(I32), 0)
 
+        ident = held([P, P], F32, "ident")
+        nc.vector.memset(ident[:], 0.0)
+        make_identity(nc, ident[:], nomemset=True)
+
         def load_plane(plane, scales, first_row):
             for s in range(LIVE_ROWS):
                 nc.sync.dma_start(
@@ -94,10 +99,10 @@ def tile_list_sonar_envelopes_kernel(
 
         wi_dram = wi_words[0].rearrange("p col i -> p (col i)").bitcast(I32)
         wq_dram = wq.rearrange("(p i) col -> p i col", i=PACK)
-        wi_codes, wq_raw = [], []
+        wi_raw, wq_raw = [], []
         for g in range(GROUPS):
-            wi_codes.append(held([P, PASS], I32, "wi_codes%d" % g))
-            nc.sync.dma_start(wi_codes[g][:], wi_dram[:, g * PASS : (g + 1) * PASS])
+            wi_raw.append(held([P, PASS], I32, "wi_raw%d" % g))
+            nc.sync.dma_start(wi_raw[g][:], wi_dram[:, g * PASS : (g + 1) * PASS])
             wq_raw.append(held([P, PACK, PASS], F32, "wq_raw%d" % g))
             nc.sync.dma_start(wq_raw[g][:], wq_dram[:, :, g * PASS : (g + 1) * PASS])
         ambient = held([P, GROUPS, PACK], F32, "ambient")
@@ -108,8 +113,6 @@ def tile_list_sonar_envelopes_kernel(
         nc.sync.dma_start(wc_codes[:].bitcast(I32), wc_words[0].bitcast(I32))
         load_plane(wc_plane, wc_scales[0], 0)
 
-        ident = held([P, P], F32, "ident")
-        make_identity(nc, ident[:])
 
         v_codes = [held([P, BANK], U32, "v_codes%d" % b) for b in range(HALVES)]
         v_plane = [held([P, BANK], U8, "v_plane%d" % b) for b in range(HALVES)]
@@ -133,29 +136,42 @@ def tile_list_sonar_envelopes_kernel(
         def by_column(packed):
             return packed.rearrange("p (pair e i) -> p pair i e", e=2, i=PACK)
 
-        def round_rows(packed, source):
-            pairs = PIECE // (2 * PACK)
-            for first in range(0, source.shape[2] // 2, pairs):
-                part = slice(first, first + pairs)
-                nc.vector.tensor_copy(by_column(packed)[:, part], by_row(source)[:, part])
+        def quantize(codes, plane, packed):
+            nc.vector.quantize_mx(out=codes.bitcast(FP8X4), scales=plane, in_=packed)
 
-        def quantize_weight(codes, plane, packed):
-            words = PIECE // PACK
-            for first in range(0, codes.shape[1], words):
-                nc.vector.quantize_mx(
-                    out=codes[:, first : first + words].bitcast(FP8X4),
-                    scales=plane[:, first : first + words],
-                    in_=packed[:, first * PACK : (first + words) * PACK],
+        weights = {}
+        wq_packed = [held([P, PACK * PASS], BF16, "wq_packed%d" % g) for g in range(GROUPS)]
+
+        def round_wq(g):
+            for half in range(2):
+                if g == DEALT:
+                    nc.vector.tensor_copy(
+                        wq_packed[g][:].rearrange("p (t m i) -> p m t i", t=PACK, i=PACK)[:, :, 2 * half : 2 * half + 2],
+                        wq_raw[g][:].rearrange("p i (m t) -> p m t i", t=PACK)[:, :, 2 * half : 2 * half + 2],
+                    )
+                else:
+                    pairs = slice(half * PASS // 4, (half + 1) * PASS // 4)
+                    nc.vector.tensor_copy(by_column(wq_packed[g][:])[:, pairs], by_row(wq_raw[g][:])[:, pairs])
+
+        def quantize_wq(g):
+            codes, plane = held([P, PASS], I32, "wq_codes%d" % g), held([P, PASS], U8, "wq_plane%d" % g)
+            for half in range(2):
+                cols = slice(half * PASS // 2, (half + 1) * PASS // 2)
+                quantize(codes[:, cols], plane[:, cols], wq_packed[g][:, cols.start * PACK : cols.stop * PACK])
+            weights["wq", g, g == DEALT] = (codes[:], plane[:])
+
+        for g in range(GROUPS):
+            weights["wi", g, False] = (wi_raw[g][:], wi_plane[WI_ROW:P, g * PASS : (g + 1) * PASS])
+
+        def deal_wi():
+            codes, plane = held([P, PASS], I32, "wi_dealt_codes"), held([P, PASS], U8, "wi_dealt_plane")
+            sources = (wi_raw[DEALT][:], wi_plane[:, DEALT * PASS : (DEALT + 1) * PASS])
+            for target, source, run in zip((codes, plane), sources, (4, 16)):
+                nc.vector.tensor_copy(
+                    target[:].rearrange("p (t hi lo) -> p hi t lo", t=PACK, lo=run),
+                    source.rearrange("p (hi lo t) -> p hi t lo", lo=run, t=PACK),
                 )
-
-        wq_codes = [held([P, PASS], I32, "wq_codes%d" % g) for g in range(GROUPS)]
-        wq_plane = [held([P, PASS], U8, "wq_plane%d" % g) for g in range(GROUPS)]
-        nc.vector.memset(wq_plane[DIRECT][:].bitcast(I32), 0)
-
-        def prepare_wq(g):
-            packed = held([P, PACK * PASS], BF16, "wq_packed%d" % g)
-            round_rows(packed[:], wq_raw[g][:])
-            quantize_weight(wq_codes[g], wq_plane[g], packed)
+            weights["wi", DEALT, True] = (codes[:], plane[WI_ROW:P, :])
 
         wd_codes = held([P, GROUPS * N], U32, "wd_codes")
         wd_plane = held([P, GROUPS * N], U8, "wd_plane")
@@ -166,112 +182,119 @@ def tile_list_sonar_envelopes_kernel(
                 nc.vector.tensor_scalar(
                     out=by_column(wd_packed[:, g * N * PACK : (g + 1) * N * PACK]),
                     in0=by_row(wd_raw[:, g, :].rearrange("p (i n) -> p i n", i=PACK)),
-                    scalar1=-1.0,
-                    scalar2=None,
-                    op0=ALU.mult,
+                    scalar1=-1.0, scalar2=None, op0=ALU.mult,
                 )
 
-        dealt = {}
+        def quantize_wd():
+            for first, stop in ((0, PASS), (PASS, GROUPS * N)):
+                quantize(wd_codes[:, first:stop], wd_plane[:, first:stop], wd_packed[:, first * PACK : stop * PACK])
 
-        def deal(beam, codes, plane):
-            dealt[beam] = (held([P, PASS], I32, beam + "_dealt_codes"), held([P, PASS], U8, beam + "_dealt_plane"))
-            for target, source, run in zip(dealt[beam], (codes, plane), (4, 16)):
-                nc.vector.tensor_copy(
-                    target[:].rearrange("p (t hi lo) -> p hi t lo", t=PACK, lo=run),
-                    source.rearrange("p (hi lo t) -> p hi t lo", lo=run, t=PACK),
-                )
-
-        steps = [(u, c) for u, (g, j0, width) in enumerate(UNITS) for c in range(width // P)]
-        env = [held([P, PACK, width], F32, "env%d" % u) for u, (g, j0, width) in enumerate(UNITS)]
-        env_packed = [held([P, width * PACK], BF16, "env_packed%d" % u) for u, (g, j0, width) in enumerate(UNITS)]
         env_codes = {
             (g, b): held([P, BANK], U32, "env_codes%d%d" % (g, b)) for g in range(GROUPS) for b in range(HALVES)
         }
         env_plane = [held([P, S], U8, "env_plane%d" % g) for g in range(GROUPS)]
         out_1_rows = out_1.rearrange("(g p t) j -> g p t j", g=GROUPS, t=PACK)
-        squares, power = {}, {}
+        out_0_rows = out_0.rearrange("(n p) j -> p n j", p=P)
+        squares = {}
 
-        def beam_products(beam, u, c, bank):
-            g, j0, width = UNITS[u]
-            first_row = WI_ROW if beam == "wi" else 0
-            if g == TURNED:
-                codes, plane = (wi_codes[g], wi_plane) if beam == "wi" else (wq_codes[g], wq_plane[g])
+        def square(beam, u, c):
+            g, j0, width, road = UNITS[u]
+            dealt = g == DEALT and (beam == "wq" or road == DIRECT)
+            codes, plane = weights[beam, g, dealt]
+            on_vector = (beam, u, c) in ON_VECTOR
+            bank = take_bank("vector" if on_vector else "scalar")
+            if road == DIRECT:
+                v, v_scale = snapshots(j0, width)
+                per_bank = BANK // width
+                for place in range(per_bank):
+                    cols = slice((c * per_bank + place) * P, (c * per_bank + place + 1) * P)
+                    nc.tensor.matmul_mx(
+                        out=bank[:, place * width : (place + 1) * width], lhsT=codes[:, cols].bitcast(FP8X4),
+                        lhsT_scale=plane[:, cols], rhs=v, rhs_scale=v_scale, start=True, stop=True,
+                    )
+            else:
                 v, v_scale = snapshots(j0 + c * P, P)
                 nc.tensor.matmul_mx(
-                    out=bank[:], lhsT=v, lhsT_scale=v_scale, rhs=codes[:].bitcast(FP8X4),
-                    rhs_scale=plane[first_row:P, 0:PASS], start=True, stop=True,
+                    out=bank[:], lhsT=v, lhsT_scale=v_scale, rhs=codes.bitcast(FP8X4), rhs_scale=plane,
+                    start=True, stop=True,
                 )
-                return bank[:].rearrange("p (m t) -> p t m", t=PACK)
-            codes, plane = dealt[beam]
-            v, v_scale = snapshots(j0, width)
+            if dealt:
+                products = bank[:].rearrange("p (t m) -> p t m", t=PACK)
+            else:
+                products = bank[:].rearrange("p (m t) -> p t m", t=PACK)
+            target = held([P, PACK, P], F32, "%s_square%d%d" % (beam, u, c))
+            squares[beam, u, c] = target
+            if on_vector:
+                nc.vector.tensor_reduce(
+                    target[:], products.unsqueeze(3).to_broadcast([P, PACK, P, 2]), AXIS.X, ALU.mult
+                )
+            else:
+                nc.scalar.activation(target[:], products, ACT.Square)
+
+        def squares_of(beam, u):
+            for c in range(UNITS[u][2] // P):
+                if (beam, u, c) not in squares:
+                    square(beam, u, c)
+
+        env = [held([P, PACK, width], F32, "env%d" % u) for u, (g, j0, width, road) in enumerate(UNITS)]
+        env_packed = [held([P, PACK * width], BF16, "env_packed%d" % u) for u, (g, j0, width, road) in enumerate(UNITS)]
+
+        def roots_turned(u, t0):
+            g, j0, width, road = UNITS[u]
+            count, per_bank = width // P, BANK // width
+            bank = take_bank("scalar")[:].rearrange("p (a z) -> p a z", a=per_bank)
+            terms = [
+                (beam, c, place) for beam in ("wq", "wi") for c in reversed(range(count)) for place in range(per_bank)
+            ]
+            for term in terms:
+                beam, c, place = term
+                nc.tensor.matmul(
+                    bank[:, place, c * P : (c + 1) * P], lhsT=squares[beam, u, c][:, t0 + place, :], rhs=ident[:],
+                    is_transpose=True, start=(term == terms[0]), stop=(term == terms[-1]),
+                )
+            for t in range(t0, t0 + per_bank):
+                nc.scalar.activation(env[u][:, t, :], bank[:, t - t0, :], ACT.Sqrt, bias=ambient[:, g, t : t + 1])
+            if t0 + per_bank == PACK:
+                nc.sync.dma_start(out_1_rows[g, :, :, j0 : j0 + width], env[u][:])
+
+        power = {}
+
+        def add_squares(u, c):
+            g, j0, width, road = UNITS[u]
+            if u not in power:
+                power[u] = held([P, PACK, width], F32, "power%d" % u)
             per_bank = BANK // width
             for place in range(per_bank):
                 t = c * per_bank + place
-                nc.tensor.matmul_mx(
-                    out=bank[:, place * width : (place + 1) * width],
-                    lhsT=codes[:, t * P : (t + 1) * P].bitcast(FP8X4),
-                    lhsT_scale=plane[first_row:P, t * P : (t + 1) * P], rhs=v, rhs_scale=v_scale,
-                    start=True, stop=True,
+                cols = slice(place * width, (place + 1) * width)
+                nc.vector.scalar_tensor_tensor(
+                    out=power[u][:, t, :],
+                    in0=squares["wi", u, c][:].rearrange("p a z -> p (a z)")[:, cols],
+                    scalar=ambient[:, g, t : t + 1],
+                    in1=squares["wq", u, c][:].rearrange("p a z -> p (a z)")[:, cols],
+                    op0=ALU.add, op1=ALU.add,
                 )
-            return bank[:].rearrange("p (a z) -> p a z", a=PACK)
 
-        def square_tile(beam, u, c):
-            if u == THIRD:
-                squares[beam, u, c] = held([P, PACK, P], F32, "%s_square%d" % (beam, c))
-            else:
-                squares[beam, u, c] = ring.tile([P, PACK, P], F32, name=beam + "_square")
-            return squares[beam, u, c]
+        def roots_direct(u):
+            g, j0, width, road = UNITS[u]
+            for first in range(0, width, P):
+                nc.scalar.activation(env[u][:, :, first : first + P], power[u][:, :, first : first + P], ACT.Sqrt)
+            nc.sync.dma_start(out_1_rows[g, :, :, j0 : j0 + width], env[u][:])
 
-        def square_on_scalar(beam, u, c):
-            products = beam_products(beam, u, c, beam_banks.tile([P, BANK], F32, name="beam_bank"))
-            nc.scalar.activation(square_tile(beam, u, c)[:], products, ACT.Square)
-
-        def square_on_vector(beam, u, c):
-            products = beam_products(beam, u, c, side_bank.tile([P, BANK], F32, name="side"))
-            plain = ring.tile([P, PACK, P], F32, name="plain", bufs=2)
-            nc.vector.tensor_copy(plain[:], products)
-            nc.vector.tensor_tensor(square_tile(beam, u, c)[:], plain[:], plain[:], ALU.mult)
-
-        def add_squares(u, c):
-            power[u, c] = ring.tile([P, PACK, P], F32, name="power")
-            nc.vector.tensor_tensor(power[u, c][:], squares["wi", u, c][:], squares["wq", u, c][:], ALU.add)
-
-        def root(u, t, source):
-            g, j0, width = UNITS[u]
-            nc.scalar.activation(env[u][:, t, :], source, ACT.Sqrt, bias=ambient[:, g, t : t + 1])
-            if t % 2 == 1:
-                nc.sync.dma_start(out_1_rows[g, :, t - 1 : t + 1, j0 : j0 + width], env[u][:, t - 1 : t + 1, :])
-            if t == PACK - 1:
-                round_rows(env_packed[u][:], env[u][:])
-
-        def roots_direct(u, c):
-            width = UNITS[u][2]
-            per_bank = BANK // width
-            flat = power[u, c][:].rearrange("p a z -> p (a z)")
-            for place in range(per_bank):
-                root(u, c * per_bank + place, flat[:, place * width : (place + 1) * width])
-
-        def roots_turned(u):
-            count = UNITS[u][2] // P
-            for t in range(PACK):
-                bank = sum_banks.tile([P, BANK], F32, name="sum")
-                for c in range(count):
-                    for beam in ("wi", "wq"):
-                        nc.tensor.matmul(
-                            bank[:, c * P : (c + 1) * P], lhsT=squares[beam, u, c][:, t, :], rhs=ident[:],
-                            is_transpose=True, start=(c == 0 and beam == "wi"), stop=(c == count - 1 and beam == "wq"),
-                        )
-                root(u, t, bank[:])
-
-        def quantize_env(u):
-            g, j0, width = UNITS[u]
-            codes = env_codes[g, j0 // BANK]
-            nc.vector.quantize_mx(
-                out=codes[:, j0 % BANK : j0 % BANK + width].bitcast(FP8X4),
-                scales=env_plane[g][:, j0 : j0 + width],
-                in_=env_packed[u][:],
+        def round_env(u, first, count):
+            nc.vector.tensor_copy(
+                by_column(env_packed[u][:, first * PACK : (first + count) * PACK]),
+                by_row(env[u][:, :, first : first + count]),
             )
-            end = j0 + width
+
+        def quantize_env(u, first, count):
+            g, j0, width, road = UNITS[u]
+            start, end = j0 + first, j0 + first + count
+            codes = env_codes[g, j0 // BANK]
+            quantize(
+                codes[:, start % BANK : start % BANK + count], env_plane[g][:, start:end],
+                env_packed[u][:, first * PACK : (first + count) * PACK],
+            )
             if end % BANK == 0:
                 out_2_words = out_2[g].rearrange("p j t -> p (j t)").bitcast(I32)
                 nc.sync.dma_start(out_2_words[:, end - BANK : end], codes[:].bitcast(I32))
@@ -281,115 +304,122 @@ def tile_list_sonar_envelopes_kernel(
                         out_3[g, s:SCALE_ROWS:LIVE_ROWS, :].bitcast(I32), env_plane[g][s:P:QUADRANT, :].bitcast(I32)
                     )
 
-        out_0_rows = out_0.rearrange("(n p) j -> p n j", p=P)
-        y = {u: held([P, ROW_TILES, UNITS[u][2]], F32, "y%d" % u) for u in (SECOND, FOURTH, LAST)}
-        readout = {}
-
-        def bank_tiles(u):
-            per_bank = BANK // UNITS[u][2]
-            return [range(n0, min(n0 + per_bank, ROW_TILES)) for n0 in range(0, ROW_TILES, per_bank)]
-
-        def add_envelopes(g, u, tiles):
-            j0, width = UNITS[u][1:]
-            for n in tiles:
-                cols = slice(g * N + n * P, g * N + (n + 1) * P)
+        def readout_pass(target, source, n, j0, width, start, stop):
+            if source == "clutter":
+                v, v_scale = snapshots(j0, width)
                 nc.tensor.matmul_mx(
-                    out=readout[u, tiles][:, n - tiles.start, :],
-                    lhsT=wd_codes[:, cols].bitcast(FP8X4),
-                    lhsT_scale=wd_plane[:, cols],
-                    rhs=env_codes[g, j0 // BANK][:, j0 % BANK : j0 % BANK + width].bitcast(FP8X4),
-                    rhs_scale=env_plane[g][:, j0 : j0 + width],
-                    start=False,
-                    stop=(g == DIRECT and n == tiles.stop - 1),
+                    out=target, lhsT=wc_codes[:, 2 * n * P : 2 * (n + 1) * P].bitcast(FP4X4),
+                    lhsT_scale=wc_plane[:, n * P : (n + 1) * P], rhs=v, rhs_scale=v_scale, start=start, stop=stop,
                 )
+                return
+            cols = slice(source * N + n * P, source * N + (n + 1) * P)
+            nc.tensor.matmul_mx(
+                out=target, lhsT=wd_codes[:, cols].bitcast(FP8X4), lhsT_scale=wd_plane[:, cols],
+                rhs=env_codes[source, j0 // BANK][:, j0 % BANK : j0 % BANK + width].bitcast(FP8X4),
+                rhs_scale=env_plane[source][:, j0 : j0 + width], start=start, stop=stop,
+            )
 
-        def open_readout(u, tiles, pool, tag):
-            j0, width = UNITS[u][1:]
-            readout[u, tiles] = pool.tile([P, len(tiles), width], F32, name=tag)
-            piece = BANK if width == BANK else P
-            for n in tiles:
-                for first in range(0, width, piece):
-                    v, v_scale = snapshots(j0 + first, piece)
-                    nc.tensor.matmul_mx(
-                        out=readout[u, tiles][:, n - tiles.start, first : first + piece],
-                        lhsT=wc_codes[:, 2 * n * P : 2 * (n + 1) * P].bitcast(FP4X4),
-                        lhsT_scale=wc_plane[:, n * P : (n + 1) * P],
-                        rhs=v,
-                        rhs_scale=v_scale,
-                        start=(n == tiles.start and first == 0),
-                        stop=False,
-                    )
-            add_envelopes(TURNED, u, tiles)
+        def empty(target, bank, on_scalar):
+            if on_scalar:
+                nc.scalar.activation(target, bank, ACT.Copy, scale=-1.0)
+            else:
+                nc.vector.tensor_scalar(out=target, in0=bank, scalar1=-1.0, scalar2=None, op0=ALU.mult)
 
-        def close_readout(u):
-            j0, width = UNITS[u][1:]
-            for tiles in bank_tiles(u):
-                add_envelopes(DIRECT, u, tiles)
-                target = y[u][:, tiles.start : tiles.stop, :]
-                if width < BANK and tiles.start == 0:
-                    nc.scalar.activation(target, readout[u, tiles][:], ACT.Copy, scale=-1.0)
-                else:
-                    nc.vector.tensor_scalar(
-                        out=target, in0=readout[u, tiles][:], scalar1=-1.0, scalar2=None, op0=ALU.mult
-                    )
-                if width == BANK:
-                    nc.sync.dma_start(out_0_rows[:, tiles.start : tiles.stop, j0 : j0 + width], target)
-            if width < BANK:
-                nc.sync.dma_start(out_0_rows[:, :, j0 : j0 + width], y[u][:])
+        y = {u: held([P, ROW_TILES, UNITS[u][2]], F32, "y%d" % u) for u in range(BLOCKS, len(UNITS))}
+        opened = {}
 
-        def after_rounding(u):
-            quantize_env(u)
-            if u == FIRST:
-                for tiles in bank_tiles(SECOND)[:-1]:
-                    open_readout(SECOND, tiles, read_banks, "read")
-            if u == SECOND:
-                open_readout(SECOND, bank_tiles(SECOND)[-1], side_bank, "side")
-            if u == THIRD:
-                for tiles in bank_tiles(FOURTH):
-                    open_readout(FOURTH, tiles, read_banks, "read")
-                for tiles in bank_tiles(LAST):
-                    open_readout(LAST, tiles, sum_banks, "sum")
-            if UNITS[u][0] == DIRECT:
-                close_readout(u)
+        def readout_passes(u, ring, sources, start, stop):
+            g, j0, width, road = UNITS[u]
+            for first in range(0, width, P):
+                if start:
+                    opened[u, first] = take_bank(ring)[:, 0 : ROW_TILES * P].rearrange("p (n j) -> p n j", n=ROW_TILES)
+                for source in sources:
+                    for n in range(ROW_TILES):
+                        readout_pass(
+                            opened[u, first][:, n, :], source, n, j0 + first, P,
+                            start and source == sources[0] and n == 0,
+                            stop and source == sources[-1] and n == ROW_TILES - 1,
+                        )
+
+        def empty_readout(u, on_scalar):
+            g, j0, width, road = UNITS[u]
+            for first in range(0, width, P):
+                empty(y[u][:, :, first : first + P], opened[u, first], on_scalar)
+            nc.sync.dma_start(out_0_rows[:, :, j0 : j0 + width], y[u][:])
 
         gather_scales(0)
         gather_scales(1)
         gather_words(0)
-        for c in range(PACK):
-            square_on_scalar("wi", FIRST, c)
         gather_words(1)
-        for c in range(PACK):
-            square_on_scalar("wi", THIRD, c)
-        prepare_wq(TURNED)
+        def vector_squares(*units):
+            for term in ON_VECTOR:
+                if term[1] in units and term not in squares:
+                    square(*term)
 
-        def prepare_direct_weights():
-            deal("wi", wi_codes[DIRECT][:], wi_plane[:, DIRECT * PASS : (DIRECT + 1) * PASS])
-            prepare_wq(DIRECT)
-            deal("wq", wq_codes[DIRECT][:], wq_plane[DIRECT][:])
+        def round_unit(u):
+            round_env(u, 0, UNITS[u][2])
 
-        for step in range(len(steps) + 2):
-            if step < len(steps):
-                u, c = steps[step]
-                for beam in ("wi", "wq"):
-                    if (beam, u, c) not in squares:
-                        square_on_scalar(beam, u, c)
-                if UNITS[u][0] == DIRECT:
-                    add_squares(u, c)
-            if step >= 2:
-                u, c = steps[step - 2]
-                if c == UNITS[u][2] // P - 1:
-                    after_rounding(u)
-            if 1 <= step <= len(steps):
-                u, c = steps[step - 1]
-                if UNITS[u][0] == DIRECT:
-                    roots_direct(u, c)
-                elif c == PACK - 1:
-                    roots_turned(u)
-            if step == 0:
-                prepare_direct_weights()
-            if step == WD_STEP:
+        def quantize_unit(u):
+            quantize_env(u, 0, UNITS[u][2])
+
+        def turned_roots(u):
+            roots_turned(u, 0)
+            roots_turned(u, 2)
+            round_unit(u)
+
+        def quadrature(u):
+            for c in range(UNITS[u][2] // P):
+                square("wq", u, c)
+                add_squares(u, c)
+
+        for u in range(BLOCKS):
+            squares_of("wi", u)
+        round_wq(0)
+        quantize_wq(0)
+        deal_wi()
+        squares_of("wq", 0)
+        vector_squares(1)
+        round_wq(1)
+        quantize_wq(1)
+        for b in range(BLOCKS - 1):
+            direct = BLOCKS + b
+            squares_of("wq", b + 1)
+            squares_of("wi", direct)
+            if b == 0:
+                turned_roots(0)
                 round_negated_wd()
-            if step == WD_STEP + 1:
-                quantize_weight(wd_codes, wd_plane, wd_packed)
-            if step % SQUARE_EVERY == 0 and step // SQUARE_EVERY < SQUARES_ON_VECTOR:
-                square_on_vector("wq", THIRD, step // SQUARE_EVERY)
+                quantize_unit(0)
+            else:
+                roots_direct(direct - 1)
+                round_unit(direct - 1)
+            quadrature(direct)
+            if b == 0:
+                quantize_wd()
+            else:
+                quantize_unit(direct - 1)
+                readout_passes(direct - 1, "vector", (1, 0, "clutter"), True, True)
+            vector_squares(b + 2, direct + 1)
+            turned_roots(b + 1)
+            if b > 0:
+                empty_readout(direct - 1, False)
+            quantize_unit(b + 1)
+        third, fourth, fifth = range(len(UNITS) - 3, len(UNITS))
+        squares_of("wi", fourth)
+        quadrature(fourth)
+        roots_direct(third)
+        round_unit(third)
+        squares_of("wi", fifth)
+        quantize_unit(third)
+        readout_passes(third, "vector", (1, 0, "clutter"), True, True)
+        quadrature(fifth)
+        for u in (fourth, fifth):
+            readout_passes(u, "scalar", (0, "clutter"), True, False)
+        for u in (fourth, fifth):
+            roots_direct(u)
+            round_unit(u)
+        empty_readout(third, True)
+        for u in (fourth, fifth):
+            quantize_unit(u)
+        for u in (fourth, fifth):
+            readout_passes(u, "scalar", (1,), False, True)
+            empty_readout(u, True)

@@ -36,12 +36,9 @@ DEALT = 1
 
 TURNED, DIRECT = 0, 1
 UNITS = (
-    (0, 0, 256, TURNED), (0, 256, 256, TURNED), (0, 512, 256, TURNED), (0, 768, 256, TURNED),
-    (1, 0, 256, DIRECT), (1, 256, 256, DIRECT), (1, 512, 256, DIRECT), (1, 768, 128, DIRECT), (1, 896, 128, DIRECT),
+    (0, 0, 512, TURNED), (1, 0, 512, DIRECT), (0, 512, 512, TURNED), (1, 512, 256, DIRECT), (1, 768, 256, DIRECT),
 )
-ON_VECTOR = (("wq", 1, 0), ("wq", 2, 0), ("wq", 3, 0), ("wi", 7, 0))
-BLOCK = 256
-BLOCKS = S // BLOCK
+ON_VECTOR = (("wq", 2, 0), ("wq", 2, 1), ("wq", 2, 2))
 
 
 def tile_list_sonar_envelopes_kernel(
@@ -143,21 +140,17 @@ def tile_list_sonar_envelopes_kernel(
         wq_packed = [held([P, PACK * PASS], BF16, "wq_packed%d" % g) for g in range(GROUPS)]
 
         def round_wq(g):
-            for half in range(2):
-                if g == DEALT:
-                    nc.vector.tensor_copy(
-                        wq_packed[g][:].rearrange("p (t m i) -> p m t i", t=PACK, i=PACK)[:, :, 2 * half : 2 * half + 2],
-                        wq_raw[g][:].rearrange("p i (m t) -> p m t i", t=PACK)[:, :, 2 * half : 2 * half + 2],
-                    )
-                else:
-                    pairs = slice(half * PASS // 4, (half + 1) * PASS // 4)
-                    nc.vector.tensor_copy(by_column(wq_packed[g][:])[:, pairs], by_row(wq_raw[g][:])[:, pairs])
+            if g == DEALT:
+                nc.vector.tensor_copy(
+                    wq_packed[g][:].rearrange("p (t m i) -> p m t i", t=PACK, i=PACK),
+                    wq_raw[g][:].rearrange("p i (m t) -> p m t i", t=PACK),
+                )
+            else:
+                nc.vector.tensor_copy(by_column(wq_packed[g][:]), by_row(wq_raw[g][:]))
 
         def quantize_wq(g):
             codes, plane = held([P, PASS], I32, "wq_codes%d" % g), held([P, PASS], U8, "wq_plane%d" % g)
-            for half in range(2):
-                cols = slice(half * PASS // 2, (half + 1) * PASS // 2)
-                quantize(codes[:, cols], plane[:, cols], wq_packed[g][:, cols.start * PACK : cols.stop * PACK])
+            quantize(codes[:], plane[:], wq_packed[g][:])
             weights["wq", g, g == DEALT] = (codes[:], plane[:])
 
         for g in range(GROUPS):
@@ -197,12 +190,11 @@ def tile_list_sonar_envelopes_kernel(
         out_0_rows = out_0.rearrange("(n p) j -> p n j", p=P)
         squares = {}
 
-        def square(beam, u, c):
+        def products_of(beam, u, c, ring):
             g, j0, width, road = UNITS[u]
             dealt = g == DEALT and (beam == "wq" or road == DIRECT)
             codes, plane = weights[beam, g, dealt]
-            on_vector = (beam, u, c) in ON_VECTOR
-            bank = take_bank("vector" if on_vector else "scalar")
+            bank = take_bank(ring)
             if road == DIRECT:
                 v, v_scale = snapshots(j0, width)
                 per_bank = BANK // width
@@ -219,43 +211,42 @@ def tile_list_sonar_envelopes_kernel(
                     start=True, stop=True,
                 )
             if dealt:
-                products = bank[:].rearrange("p (t m) -> p t m", t=PACK)
-            else:
-                products = bank[:].rearrange("p (m t) -> p t m", t=PACK)
-            target = held([P, PACK, P], F32, "%s_square%d%d" % (beam, u, c))
-            squares[beam, u, c] = target
-            if on_vector:
-                nc.vector.tensor_reduce(
-                    target[:], products.unsqueeze(3).to_broadcast([P, PACK, P, 2]), AXIS.X, ALU.mult
-                )
-            else:
-                nc.scalar.activation(target[:], products, ACT.Square)
+                return bank[:].rearrange("p (t m) -> p t m", t=PACK)
+            return bank[:].rearrange("p (m t) -> p t m", t=PACK)
 
-        def squares_of(beam, u):
-            for c in range(UNITS[u][2] // P):
-                if (beam, u, c) not in squares:
-                    square(beam, u, c)
+        def square_tile(beam, u, c):
+            squares[beam, u, c] = held([P, PACK, P], F32, "%s_square%d%d" % (beam, u, c))
+            return squares[beam, u, c][:]
+
+        def square_on_vector(beam, u, c):
+            products = products_of(beam, u, c, "vector")
+            nc.vector.tensor_reduce(
+                square_tile(beam, u, c), products.unsqueeze(3).to_broadcast([P, PACK, P, 2]), AXIS.X, ALU.mult
+            )
+
+        def squares_on_scalar(*terms):
+            filled = [(term, products_of(*term, "scalar")) for term in terms]
+            for term, products in reversed(filled):
+                nc.scalar.activation(square_tile(*term), products, ACT.Square)
+
+        def square_pair(beam, u, c):
+            squares_on_scalar((beam, u, c), (beam, u, c + 1))
 
         env = [held([P, PACK, width], F32, "env%d" % u) for u, (g, j0, width, road) in enumerate(UNITS)]
         env_packed = [held([P, PACK * width], BF16, "env_packed%d" % u) for u, (g, j0, width, road) in enumerate(UNITS)]
 
-        def roots_turned(u, t0):
+        def root_turned(u, t):
             g, j0, width, road = UNITS[u]
-            count, per_bank = width // P, BANK // width
-            bank = take_bank("scalar")[:].rearrange("p (a z) -> p a z", a=per_bank)
-            terms = [
-                (beam, c, place) for beam in ("wq", "wi") for c in reversed(range(count)) for place in range(per_bank)
-            ]
-            for term in terms:
-                beam, c, place = term
+            bank = take_bank("scalar")
+            terms = [(beam, c) for beam in ("wq", "wi") for c in reversed(range(PACK))]
+            for beam, c in terms:
                 nc.tensor.matmul(
-                    bank[:, place, c * P : (c + 1) * P], lhsT=squares[beam, u, c][:, t0 + place, :], rhs=ident[:],
-                    is_transpose=True, start=(term == terms[0]), stop=(term == terms[-1]),
+                    bank[:, c * P : (c + 1) * P], lhsT=squares[beam, u, c][:, t, :], rhs=ident[:],
+                    is_transpose=True, start=((beam, c) == terms[0]), stop=((beam, c) == terms[-1]),
                 )
-            for t in range(t0, t0 + per_bank):
-                nc.scalar.activation(env[u][:, t, :], bank[:, t - t0, :], ACT.Sqrt, bias=ambient[:, g, t : t + 1])
-            if t0 + per_bank == PACK:
-                nc.sync.dma_start(out_1_rows[g, :, :, j0 : j0 + width], env[u][:])
+            nc.scalar.activation(env[u][:, t, :], bank[:], ACT.Sqrt, bias=ambient[:, g, t : t + 1])
+            if t % 2 == 1:
+                store_env(u, slice(t - 1, t + 1))
 
         power = {}
 
@@ -275,11 +266,12 @@ def tile_list_sonar_envelopes_kernel(
                     op0=ALU.add, op1=ALU.add,
                 )
 
-        def roots_direct(u):
+        def roots_direct(u, rows, first, count):
+            nc.scalar.activation(env[u][:, rows, first : first + count], power[u][:, rows, first : first + count], ACT.Sqrt)
+
+        def store_env(u, rows):
             g, j0, width, road = UNITS[u]
-            for first in range(0, width, P):
-                nc.scalar.activation(env[u][:, :, first : first + P], power[u][:, :, first : first + P], ACT.Sqrt)
-            nc.sync.dma_start(out_1_rows[g, :, :, j0 : j0 + width], env[u][:])
+            nc.sync.dma_start(out_1_rows[g, :, rows, j0 : j0 + width], env[u][:, rows, :])
 
         def round_env(u, first, count):
             nc.vector.tensor_copy(
@@ -325,101 +317,118 @@ def tile_list_sonar_envelopes_kernel(
             else:
                 nc.vector.tensor_scalar(out=target, in0=bank, scalar1=-1.0, scalar2=None, op0=ALU.mult)
 
-        y = {u: held([P, ROW_TILES, UNITS[u][2]], F32, "y%d" % u) for u in range(BLOCKS, len(UNITS))}
+        y = {u: held([P, ROW_TILES, UNITS[u][2]], F32, "y%d" % u) for u in (1, 3, 4)}
         opened = {}
 
-        def readout_passes(u, ring, sources, start, stop):
-            g, j0, width, road = UNITS[u]
-            for first in range(0, width, P):
-                if start:
-                    opened[u, first] = take_bank(ring)[:, 0 : ROW_TILES * P].rearrange("p (n j) -> p n j", n=ROW_TILES)
-                for source in sources:
-                    for n in range(ROW_TILES):
-                        readout_pass(
-                            opened[u, first][:, n, :], source, n, j0 + first, P,
-                            start and source == sources[0] and n == 0,
-                            stop and source == sources[-1] and n == ROW_TILES - 1,
-                        )
+        def wide_passes(u, source):
+            for n in range(ROW_TILES):
+                if source == "clutter":
+                    opened[u, n] = take_bank("vector")
+                readout_pass(opened[u, n][:], source, n, UNITS[u][1], BANK, source == "clutter", source == 1)
 
-        def empty_readout(u, on_scalar):
-            g, j0, width, road = UNITS[u]
-            for first in range(0, width, P):
-                empty(y[u][:, :, first : first + P], opened[u, first], on_scalar)
-            nc.sync.dma_start(out_0_rows[:, :, j0 : j0 + width], y[u][:])
+        def empty_wide(u, n, on_scalar):
+            j0 = UNITS[u][1]
+            empty(y[u][:, n, :], opened[u, n][:], on_scalar)
+            nc.sync.dma_start(out_0_rows[:, n, j0 : j0 + BANK], y[u][:, n, :])
+
+        def readout_passes(u, first, ring, sources, start, stop):
+            j0 = UNITS[u][1]
+            if start:
+                opened[u, first] = take_bank(ring)[:, 0 : ROW_TILES * P].rearrange("p (n j) -> p n j", n=ROW_TILES)
+            for source in sources:
+                for n in range(ROW_TILES):
+                    readout_pass(
+                        opened[u, first][:, n, :], source, n, j0 + first, P,
+                        start and source == sources[0] and n == 0,
+                        stop and source == sources[-1] and n == ROW_TILES - 1,
+                    )
+
+        def empty_narrow(u, first, on_scalar):
+            empty(y[u][:, :, first : first + P], opened[u, first], on_scalar)
+
+        def store_y(u, first, count):
+            j0 = UNITS[u][1]
+            nc.sync.dma_start(out_0_rows[:, :, j0 + first : j0 + first + count], y[u][:, :, first : first + count])
 
         gather_scales(0)
         gather_scales(1)
         gather_words(0)
         gather_words(1)
-        def vector_squares(*units):
-            for term in ON_VECTOR:
-                if term[1] in units and term not in squares:
-                    square(*term)
-
-        def round_unit(u):
-            round_env(u, 0, UNITS[u][2])
-
-        def quantize_unit(u):
-            quantize_env(u, 0, UNITS[u][2])
-
-        def turned_roots(u):
-            roots_turned(u, 0)
-            roots_turned(u, 2)
-            round_unit(u)
-
-        def quadrature(u):
-            for c in range(UNITS[u][2] // P):
-                square("wq", u, c)
-                add_squares(u, c)
-
-        for u in range(BLOCKS):
-            squares_of("wi", u)
+        low, high, every = slice(0, 2), slice(2, 4), slice(0, 4)
+        for u in (0, 2):
+            square_pair("wi", u, 0)
+            square_pair("wi", u, 2)
         round_wq(0)
-        quantize_wq(0)
         deal_wi()
-        squares_of("wq", 0)
-        vector_squares(1)
+        quantize_wq(0)
+        square_pair("wq", 0, 0)
+        square_pair("wq", 0, 2)
         round_wq(1)
+        square_on_vector("wq", 2, 0)
         quantize_wq(1)
-        for b in range(BLOCKS - 1):
-            direct = BLOCKS + b
-            squares_of("wq", b + 1)
-            squares_of("wi", direct)
-            if b == 0:
-                turned_roots(0)
-                round_negated_wd()
-                quantize_unit(0)
-            else:
-                roots_direct(direct - 1)
-                round_unit(direct - 1)
-            quadrature(direct)
-            if b == 0:
-                quantize_wd()
-            else:
-                quantize_unit(direct - 1)
-                readout_passes(direct - 1, "vector", (1, 0, "clutter"), True, True)
-            vector_squares(b + 2, direct + 1)
-            turned_roots(b + 1)
-            if b > 0:
-                empty_readout(direct - 1, False)
-            quantize_unit(b + 1)
-        third, fourth, fifth = range(len(UNITS) - 3, len(UNITS))
-        squares_of("wi", fourth)
-        quadrature(fourth)
-        roots_direct(third)
-        round_unit(third)
-        squares_of("wi", fifth)
-        quantize_unit(third)
-        readout_passes(third, "vector", (1, 0, "clutter"), True, True)
-        quadrature(fifth)
-        for u in (fourth, fifth):
-            readout_passes(u, "scalar", (0, "clutter"), True, False)
-        for u in (fourth, fifth):
-            roots_direct(u)
-            round_unit(u)
-        empty_readout(third, True)
-        for u in (fourth, fifth):
-            quantize_unit(u)
-        for u in (fourth, fifth):
-            readout_passes(u, "scalar", (1,), False, True)
-            empty_readout(u, True)
+        square_pair("wi", 1, 0)
+        root_turned(0, 0)
+        square_on_vector("wq", 2, 1)
+        square_pair("wi", 1, 2)
+        root_turned(0, 1)
+        round_negated_wd()
+        square_on_vector("wq", 2, 2)
+        quantize_wd()
+        square_pair("wq", 1, 0)
+        root_turned(0, 2)
+        square_on_vector("wq", 2, 3)
+        square_pair("wq", 1, 2)
+        root_turned(0, 3)
+        for t in range(PACK):
+            add_squares(1, t)
+        round_env(0, 0, BANK)
+        square_pair("wi", 3, 0)
+        roots_direct(1, low, 0, BANK)
+        store_env(1, low)
+        roots_direct(1, high, 0, BANK)
+        store_env(1, high)
+        quantize_env(0, 0, BANK)
+        round_env(1, 0, BANK)
+        root_turned(2, 0)
+        wide_passes(1, "clutter")
+        root_turned(2, 1)
+        square_pair("wq", 3, 0)
+        quantize_env(1, 0, BANK)
+        add_squares(3, 0)
+        add_squares(3, 1)
+        wide_passes(1, 0)
+        root_turned(2, 2)
+        root_turned(2, 3)
+        square_pair("wi", 4, 0)
+        wide_passes(1, 1)
+        round_env(2, 0, BANK)
+        for n in range(ROW_TILES - 2):
+            empty_wide(1, n, False)
+        quantize_env(2, 0, BANK)
+        roots_direct(3, every, 0, 2 * P)
+        store_env(3, every)
+        square_pair("wq", 4, 0)
+        round_env(3, 0, 2 * P)
+        add_squares(4, 0)
+        add_squares(4, 1)
+        for n in range(ROW_TILES - 2, ROW_TILES):
+            empty_wide(1, n, True)
+        quantize_env(3, 0, 2 * P)
+        for first in (0, P):
+            readout_passes(3, first, "scalar", ("clutter", 0, 1), True, True)
+        for first in (0, P):
+            readout_passes(4, first, "scalar", ("clutter", 0), True, False)
+        for first in (0, P):
+            roots_direct(4, every, first, P)
+        store_env(4, every)
+        for first in (0, P):
+            round_env(4, first, P)
+        for first in (0, P):
+            quantize_env(4, first, P)
+        for first in (0, P):
+            empty_narrow(3, first, True)
+        store_y(3, 0, 2 * P)
+        for first in (0, P):
+            readout_passes(4, first, "scalar", (1,), False, True)
+            empty_narrow(4, first, first == 0)
+        store_y(4, 0, 2 * P)

@@ -29,6 +29,7 @@ LIST_ROWS = 16
 QUADRANT = 32
 SCALE_ROWS = PASS // 32
 LIVE_ROWS = 4
+SPREAD = P // SCALE_ROWS
 WI_ROW = 4
 TAB_FIRST = T // 4
 SCALAR_BANKS = 5
@@ -85,9 +86,9 @@ def tile_list_sonar_envelopes_kernel(
                     plane[first_row + s : P : QUADRANT, :].bitcast(I32), scales[s:SCALE_ROWS:LIVE_ROWS, :].bitcast(I32)
                 )
 
-        load_plane(tab_plane, tab_scales[0], 0)
-        nc.sync.dma_start(tab[:, TAB_FIRST:T], tab_dram[:, TAB_FIRST:T])
+        nc.sync.dma_start(tab_plane[0:P:SPREAD, :].bitcast(I32), tab_scales[0].bitcast(I32))
         load_plane(wi_plane, wi_scales[0], WI_ROW)
+        nc.sync.dma_start(tab[:, TAB_FIRST:T], tab_dram[:, TAB_FIRST:T])
 
         warm = held([P, 1], F32, "warm")
         nc.vector.memset(warm[:], 1.0)
@@ -112,20 +113,22 @@ def tile_list_sonar_envelopes_kernel(
 
 
         v_codes = [held([P, BANK], U32, "v_codes%d" % b) for b in range(HALVES)]
-        v_plane = [held([P, BANK], U8, "v_plane%d" % b) for b in range(HALVES)]
+        v_rows = held([P, S], U8, "v_rows")
+        v_plane = held([P, S], U8, "v_plane")
+        nc.vector.memset(v_plane[:].bitcast(I32), 0)
 
         def half_list(b):
             return offsets[:, b * (BANK // LIST_ROWS) : (b + 1) * (BANK // LIST_ROWS)]
 
         def gather_scales(b):
-            nc.vector.tensor_copy(v_plane[b][:], tab_plane[:].indirect(half_list(b)))
+            nc.vector.tensor_copy(v_rows[:, b * BANK : (b + 1) * BANK], tab_plane[:].indirect(half_list(b)))
 
         def gather_words(b):
             nc.vector.tensor_copy(v_codes[b][:], tab[:].bitcast(U32).indirect(half_list(b)))
 
         def snapshots(j0, width):
             cols = slice(j0 % BANK, j0 % BANK + width)
-            return v_codes[j0 // BANK][:, cols].bitcast(FP8X4), v_plane[j0 // BANK][:, cols]
+            return v_codes[j0 // BANK][:, cols].bitcast(FP8X4), v_plane[:, j0 : j0 + width]
 
         def by_row(source):
             return source.rearrange("p i (pair e) -> p pair i e", e=2)
@@ -245,8 +248,7 @@ def tile_list_sonar_envelopes_kernel(
                     is_transpose=True, start=((beam, c) == terms[0]), stop=((beam, c) == terms[-1]),
                 )
             nc.scalar.activation(env[u][:, t, :], bank[:], ACT.Sqrt, bias=ambient[:, g, t : t + 1])
-            if t % 2 == 1:
-                store_env(u, slice(t - 1, t + 1))
+            store_env(u, slice(t, t + 1))
 
         power = {}
 
@@ -287,9 +289,9 @@ def tile_list_sonar_envelopes_kernel(
                 codes[:, start % BANK : start % BANK + count], env_plane[g][:, start:end],
                 env_packed[u][:, first * PACK : (first + count) * PACK],
             )
-            if end % BANK == 0:
+            if end == j0 + width:
                 out_2_words = out_2[g].rearrange("p j t -> p (j t)").bitcast(I32)
-                nc.sync.dma_start(out_2_words[:, end - BANK : end], codes[:].bitcast(I32))
+                nc.sync.dma_start(out_2_words[:, j0:end], codes[:, j0 % BANK : j0 % BANK + width].bitcast(I32))
             if end == S:
                 for s in range(LIVE_ROWS):
                     nc.sync.dma_start(
@@ -352,6 +354,8 @@ def tile_list_sonar_envelopes_kernel(
 
         gather_scales(0)
         gather_scales(1)
+        for s in range(LIVE_ROWS):
+            nc.scalar.dma_start(v_plane[s:P:QUADRANT, :].bitcast(I32), v_rows[s * SPREAD : P : QUADRANT, :].bitcast(I32))
         gather_words(0)
         gather_words(1)
         low, high, every = slice(0, 2), slice(2, 4), slice(0, 4)
@@ -379,7 +383,7 @@ def tile_list_sonar_envelopes_kernel(
         square_on_vector("wq", 2, 3)
         square_pair("wq", 1, 2)
         root_turned(0, 3)
-        for t in range(PACK):
+        for t in (1, 0, 3, 2):
             add_squares(1, t)
         round_env(0, 0, BANK)
         square_pair("wi", 3, 0)
@@ -394,8 +398,8 @@ def tile_list_sonar_envelopes_kernel(
         root_turned(2, 1)
         square_pair("wq", 3, 0)
         quantize_env(1, 0, BANK)
-        add_squares(3, 0)
         add_squares(3, 1)
+        add_squares(3, 0)
         wide_passes(1, 0)
         root_turned(2, 2)
         root_turned(2, 3)
@@ -409,8 +413,8 @@ def tile_list_sonar_envelopes_kernel(
         store_env(3, every)
         square_pair("wq", 4, 0)
         round_env(3, 0, 2 * P)
-        add_squares(4, 0)
         add_squares(4, 1)
+        add_squares(4, 0)
         for n in range(ROW_TILES - 2, ROW_TILES):
             empty_wide(1, n, True)
         quantize_env(3, 0, 2 * P)

@@ -30,6 +30,10 @@ QUADRANT = 32
 SCALE_ROWS = PASS // 32
 LIVE_ROWS = 4
 SPREAD = P // SCALE_ROWS
+PLACES = {
+    "wq_raw0": 0, "wi_raw1": 8192, "wc_codes": 10240, "ambient": 11008, "wq_raw1": 11072, "wd_raw": 19264,
+    "tab_plane": 7680, "v_rows": 19264,
+}
 WI_ROW = 4
 TAB_FIRST = T // 4
 SCALAR_BANKS = 5
@@ -59,7 +63,11 @@ def tile_list_sonar_envelopes_kernel(
             taken[ring].append(rings[ring][len(taken[ring]) % len(rings[ring])])
             return taken[ring][-1]
 
+        reused = ctx.enter_context(tc.tile_pool(name="reused", bufs=1))
+
         def held(shape, dtype, name):
+            if name in PLACES:
+                return reused.tile(shape, dtype, name=name, align_bytes=64, offset=PLACES[name])
             return keep.tile(shape, dtype, name=name, align_bytes=64)
 
         offsets = lists.tile([P, S // LIST_ROWS], U16, name="offsets")
@@ -97,20 +105,21 @@ def tile_list_sonar_envelopes_kernel(
 
         wi_dram = wi_words[0].rearrange("p col i -> p (col i)").bitcast(I32)
         wq_dram = wq.rearrange("(p i) col -> p i col", i=PACK)
-        wi_raw, wq_raw = [], []
-        for g in range(GROUPS):
-            wi_raw.append(held([P, PASS], I32, "wi_raw%d" % g))
-            nc.sync.dma_start(wi_raw[g][:], wi_dram[:, g * PASS : (g + 1) * PASS])
-            wq_raw.append(held([P, PACK, PASS], F32, "wq_raw%d" % g))
-            nc.sync.dma_start(wq_raw[g][:], wq_dram[:, :, g * PASS : (g + 1) * PASS])
+        wi_raw = [held([P, PASS], I32, "wi_raw%d" % g) for g in range(GROUPS)]
+        wq_raw = [held([P, PACK, PASS], F32, "wq_raw%d" % g) for g in range(GROUPS)]
         ambient = held([P, GROUPS, PACK], F32, "ambient")
-        nc.sync.dma_start(ambient[:], amb.rearrange("(g p t) -> p g t", g=GROUPS, t=PACK))
         wd_raw = held([P, GROUPS, PACK * N], F32, "wd_raw")
-        nc.sync.dma_start(wd_raw[:], wd.rearrange("(g p i) n -> p g (i n)", g=GROUPS, i=PACK))
         wc_codes = held([P, 2 * N], U8, "wc_codes")
-        nc.sync.dma_start(wc_codes[:].bitcast(I32), wc_words[0].bitcast(I32))
-        load_plane(wc_plane, wc_scales[0], 0)
+        nc.sync.dma_start(wi_raw[0][:], wi_dram[:, 0:PASS])
 
+        def load_rest():
+            nc.sync.dma_start(wq_raw[0][:], wq_dram[:, :, 0:PASS])
+            nc.sync.dma_start(wi_raw[1][:], wi_dram[:, PASS:H])
+            nc.sync.dma_start(wq_raw[1][:], wq_dram[:, :, PASS:H])
+            nc.sync.dma_start(ambient[:], amb.rearrange("(g p t) -> p g t", g=GROUPS, t=PACK))
+            nc.sync.dma_start(wd_raw[:], wd.rearrange("(g p i) n -> p g (i n)", g=GROUPS, i=PACK))
+            nc.sync.dma_start(wc_codes[:].bitcast(I32), wc_words[0].bitcast(I32))
+            load_plane(wc_plane, wc_scales[0], 0)
 
         v_codes = [held([P, BANK], U32, "v_codes%d" % b) for b in range(HALVES)]
         v_rows = held([P, S], U8, "v_rows")
@@ -355,7 +364,8 @@ def tile_list_sonar_envelopes_kernel(
         gather_scales(0)
         gather_scales(1)
         for s in range(LIVE_ROWS):
-            nc.scalar.dma_start(v_plane[s:P:QUADRANT, :].bitcast(I32), v_rows[s * SPREAD : P : QUADRANT, :].bitcast(I32))
+            nc.sync.dma_start(v_plane[s:P:QUADRANT, :].bitcast(I32), v_rows[s * SPREAD : P : QUADRANT, :].bitcast(I32))
+        load_rest()
         gather_words(0)
         gather_words(1)
         low, high, every = slice(0, 2), slice(2, 4), slice(0, 4)
@@ -403,14 +413,14 @@ def tile_list_sonar_envelopes_kernel(
         wide_passes(1, 0)
         root_turned(2, 2)
         root_turned(2, 3)
+        roots_direct(3, every, 0, 2 * P)
+        store_env(3, every)
         square_pair("wi", 4, 0)
         wide_passes(1, 1)
         round_env(2, 0, BANK)
         for n in range(ROW_TILES - 2):
             empty_wide(1, n, False)
         quantize_env(2, 0, BANK)
-        roots_direct(3, every, 0, 2 * P)
-        store_env(3, every)
         square_pair("wq", 4, 0)
         round_env(3, 0, 2 * P)
         add_squares(4, 1)

@@ -29,11 +29,6 @@ LIST_ROWS = 16
 QUADRANT = 32
 SCALE_ROWS = PASS // 32
 LIVE_ROWS = 4
-SPREAD = P // SCALE_ROWS
-PLACES = {
-    "wq_raw0": 0, "wi_raw1": 8192, "wc_codes": 10240, "ambient": 11008, "wq_raw1": 11072, "wd_raw": 19264,
-    "tab_plane": 7680, "v_rows": 19264,
-}
 WI_ROW = 4
 TAB_FIRST = T // 4
 SCALAR_BANKS = 5
@@ -63,11 +58,7 @@ def tile_list_sonar_envelopes_kernel(
             taken[ring].append(rings[ring][len(taken[ring]) % len(rings[ring])])
             return taken[ring][-1]
 
-        reused = ctx.enter_context(tc.tile_pool(name="reused", bufs=1))
-
         def held(shape, dtype, name):
-            if name in PLACES:
-                return reused.tile(shape, dtype, name=name, align_bytes=64, offset=PLACES[name])
             return keep.tile(shape, dtype, name=name, align_bytes=64)
 
         offsets = lists.tile([P, S // LIST_ROWS], U16, name="offsets")
@@ -94,9 +85,9 @@ def tile_list_sonar_envelopes_kernel(
                     plane[first_row + s : P : QUADRANT, :].bitcast(I32), scales[s:SCALE_ROWS:LIVE_ROWS, :].bitcast(I32)
                 )
 
-        nc.sync.dma_start(tab_plane[0:P:SPREAD, :].bitcast(I32), tab_scales[0].bitcast(I32))
-        load_plane(wi_plane, wi_scales[0], WI_ROW)
+        load_plane(tab_plane, tab_scales[0], 0)
         nc.sync.dma_start(tab[:, TAB_FIRST:T], tab_dram[:, TAB_FIRST:T])
+        load_plane(wi_plane, wi_scales[0], WI_ROW)
 
         warm = held([P, 1], F32, "warm")
         nc.vector.memset(warm[:], 1.0)
@@ -105,39 +96,38 @@ def tile_list_sonar_envelopes_kernel(
 
         wi_dram = wi_words[0].rearrange("p col i -> p (col i)").bitcast(I32)
         wq_dram = wq.rearrange("(p i) col -> p i col", i=PACK)
-        wi_raw = [held([P, PASS], I32, "wi_raw%d" % g) for g in range(GROUPS)]
-        wq_raw = [held([P, PACK, PASS], F32, "wq_raw%d" % g) for g in range(GROUPS)]
-        ambient = held([P, GROUPS, PACK], F32, "ambient")
-        wd_raw = held([P, GROUPS, PACK * N], F32, "wd_raw")
-        wc_codes = held([P, 2 * N], U8, "wc_codes")
+        wi_raw, wq_raw = [], []
+        for g in range(GROUPS):
+            wi_raw.append(held([P, PASS], I32, "wi_raw%d" % g))
+            wq_raw.append(held([P, PACK, PASS], F32, "wq_raw%d" % g))
         nc.sync.dma_start(wi_raw[0][:], wi_dram[:, 0:PASS])
+        for g in range(GROUPS):
+            nc.sync.dma_start(wq_raw[g][:], wq_dram[:, :, g * PASS : (g + 1) * PASS])
+        nc.sync.dma_start(wi_raw[1][:], wi_dram[:, PASS:H])
+        ambient = held([P, GROUPS, PACK], F32, "ambient")
+        nc.sync.dma_start(ambient[:], amb.rearrange("(g p t) -> p g t", g=GROUPS, t=PACK))
+        wd_raw = held([P, GROUPS, PACK * N], F32, "wd_raw")
+        nc.sync.dma_start(wd_raw[:], wd.rearrange("(g p i) n -> p g (i n)", g=GROUPS, i=PACK))
+        wc_codes = held([P, 2 * N], U8, "wc_codes")
+        nc.sync.dma_start(wc_codes[:].bitcast(I32), wc_words[0].bitcast(I32))
+        load_plane(wc_plane, wc_scales[0], 0)
 
-        def load_rest():
-            nc.sync.dma_start(wq_raw[0][:], wq_dram[:, :, 0:PASS])
-            nc.sync.dma_start(wi_raw[1][:], wi_dram[:, PASS:H])
-            nc.sync.dma_start(wq_raw[1][:], wq_dram[:, :, PASS:H])
-            nc.sync.dma_start(ambient[:], amb.rearrange("(g p t) -> p g t", g=GROUPS, t=PACK))
-            nc.sync.dma_start(wd_raw[:], wd.rearrange("(g p i) n -> p g (i n)", g=GROUPS, i=PACK))
-            nc.sync.dma_start(wc_codes[:].bitcast(I32), wc_words[0].bitcast(I32))
-            load_plane(wc_plane, wc_scales[0], 0)
 
         v_codes = [held([P, BANK], U32, "v_codes%d" % b) for b in range(HALVES)]
-        v_rows = held([P, S], U8, "v_rows")
-        v_plane = held([P, S], U8, "v_plane")
-        nc.vector.memset(v_plane[:].bitcast(I32), 0)
+        v_plane = [held([P, BANK], U8, "v_plane%d" % b) for b in range(HALVES)]
 
         def half_list(b):
             return offsets[:, b * (BANK // LIST_ROWS) : (b + 1) * (BANK // LIST_ROWS)]
 
         def gather_scales(b):
-            nc.vector.tensor_copy(v_rows[:, b * BANK : (b + 1) * BANK], tab_plane[:].indirect(half_list(b)))
+            nc.vector.tensor_copy(v_plane[b][:], tab_plane[:].indirect(half_list(b)))
 
         def gather_words(b):
             nc.vector.tensor_copy(v_codes[b][:], tab[:].bitcast(U32).indirect(half_list(b)))
 
         def snapshots(j0, width):
             cols = slice(j0 % BANK, j0 % BANK + width)
-            return v_codes[j0 // BANK][:, cols].bitcast(FP8X4), v_plane[:, j0 : j0 + width]
+            return v_codes[j0 // BANK][:, cols].bitcast(FP8X4), v_plane[j0 // BANK][:, cols]
 
         def by_row(source):
             return source.rearrange("p i (pair e) -> p pair i e", e=2)
@@ -257,7 +247,8 @@ def tile_list_sonar_envelopes_kernel(
                     is_transpose=True, start=((beam, c) == terms[0]), stop=((beam, c) == terms[-1]),
                 )
             nc.scalar.activation(env[u][:, t, :], bank[:], ACT.Sqrt, bias=ambient[:, g, t : t + 1])
-            store_env(u, slice(t, t + 1))
+            if t % 2 == 1:
+                store_env(u, slice(t - 1, t + 1))
 
         power = {}
 
@@ -363,9 +354,6 @@ def tile_list_sonar_envelopes_kernel(
 
         gather_scales(0)
         gather_scales(1)
-        for s in range(LIVE_ROWS):
-            nc.sync.dma_start(v_plane[s:P:QUADRANT, :].bitcast(I32), v_rows[s * SPREAD : P : QUADRANT, :].bitcast(I32))
-        load_rest()
         gather_words(0)
         gather_words(1)
         low, high, every = slice(0, 2), slice(2, 4), slice(0, 4)
@@ -373,13 +361,13 @@ def tile_list_sonar_envelopes_kernel(
             square_pair("wi", u, 0)
             square_pair("wi", u, 2)
         round_wq(0)
-        deal_wi()
         quantize_wq(0)
         square_pair("wq", 0, 0)
         square_pair("wq", 0, 2)
         round_wq(1)
-        square_on_vector("wq", 2, 0)
+        deal_wi()
         quantize_wq(1)
+        square_on_vector("wq", 2, 0)
         square_pair("wi", 1, 0)
         root_turned(0, 0)
         square_on_vector("wq", 2, 1)

@@ -217,8 +217,9 @@ def tile_list_sonar_envelopes_kernel(
             return bank[:].rearrange("p (m t) -> p t m", t=PACK)
 
         def square_tile(beam, u, c):
-            squares[beam, u, c] = held([P, PACK, P], F32, "%s_square%d%d" % (beam, u, c))
-            return squares[beam, u, c][:]
+            if (beam, u) not in squares:
+                squares[beam, u] = held([P, UNITS[u][2] // P, PACK, P], F32, "%s_square%d" % (beam, u))
+            return squares[beam, u][:, c]
 
         def square_on_vector(beam, u, c):
             products = products_of(beam, u, c, "vector")
@@ -243,7 +244,7 @@ def tile_list_sonar_envelopes_kernel(
             terms = [(beam, c) for beam in ("wq", "wi") for c in reversed(range(PACK))]
             for beam, c in terms:
                 nc.tensor.matmul(
-                    bank[:, c * P : (c + 1) * P], lhsT=squares[beam, u, c][:, t, :], rhs=ident[:],
+                    bank[:, c * P : (c + 1) * P], lhsT=squares[beam, u][:, c, t, :], rhs=ident[:],
                     is_transpose=True, start=((beam, c) == terms[0]), stop=((beam, c) == terms[-1]),
                 )
             nc.scalar.activation(env[u][:, t, :], bank[:], ACT.Sqrt, bias=ambient[:, g, t : t + 1])
@@ -252,24 +253,23 @@ def tile_list_sonar_envelopes_kernel(
 
         power = {}
 
-        def add_squares(u, c):
-            g, j0, width, road = UNITS[u]
+        def add_squares(u, first, count):
             if u not in power:
-                power[u] = held([P, PACK, width], F32, "power%d" % u)
-            per_bank = BANK // width
-            for place in range(per_bank):
-                t = c * per_bank + place
-                cols = slice(place * width, (place + 1) * width)
-                nc.vector.scalar_tensor_tensor(
-                    out=power[u][:, t, :],
-                    in0=squares["wi", u, c][:].rearrange("p a z -> p (a z)")[:, cols],
-                    scalar=ambient[:, g, t : t + 1],
-                    in1=squares["wq", u, c][:].rearrange("p a z -> p (a z)")[:, cols],
-                    op0=ALU.add, op1=ALU.add,
-                )
+                power[u] = held([P, PACK, UNITS[u][2]], F32, "power%d" % u)
+            cols = slice(first * BANK, (first + count) * BANK)
+            nc.vector.tensor_tensor(
+                out=power[u][:].rearrange("p t j -> p (t j)")[:, cols],
+                in0=squares["wi", u][:].rearrange("p c a z -> p (c a z)")[:, cols],
+                in1=squares["wq", u][:].rearrange("p c a z -> p (c a z)")[:, cols], op=ALU.add,
+            )
 
         def roots_direct(u, rows, first, count):
-            nc.scalar.activation(env[u][:, rows, first : first + count], power[u][:, rows, first : first + count], ACT.Sqrt)
+            g = UNITS[u][0]
+            for t in range(rows.start, rows.stop):
+                nc.scalar.activation(
+                    env[u][:, t, first : first + count], power[u][:, t, first : first + count], ACT.Sqrt,
+                    bias=ambient[:, g, t : t + 1],
+                )
 
         def store_env(u, rows):
             g, j0, width, road = UNITS[u]
@@ -381,8 +381,8 @@ def tile_list_sonar_envelopes_kernel(
         square_on_vector("wq", 2, 3)
         square_pair("wq", 1, 2)
         root_turned(0, 3)
-        for t in (1, 0, 3, 2):
-            add_squares(1, t)
+        add_squares(1, 0, 2)
+        add_squares(1, 2, 2)
         round_env(0, 0, BANK)
         square_pair("wi", 3, 0)
         roots_direct(1, low, 0, BANK)
@@ -396,8 +396,7 @@ def tile_list_sonar_envelopes_kernel(
         root_turned(2, 1)
         square_pair("wq", 3, 0)
         quantize_env(1, 0, BANK)
-        add_squares(3, 1)
-        add_squares(3, 0)
+        add_squares(3, 0, 2)
         wide_passes(1, 0)
         root_turned(2, 2)
         root_turned(2, 3)
@@ -411,8 +410,7 @@ def tile_list_sonar_envelopes_kernel(
         quantize_env(2, 0, BANK)
         square_pair("wq", 4, 0)
         round_env(3, 0, 2 * P)
-        add_squares(4, 1)
-        add_squares(4, 0)
+        add_squares(4, 0, 2)
         for n in range(ROW_TILES - 2, ROW_TILES):
             empty_wide(1, n, True)
         quantize_env(3, 0, 2 * P)

@@ -130,10 +130,10 @@ def tile_list_sonar_envelopes_kernel(
             return v_codes[j0 // BANK][:, cols].bitcast(FP8X4), v_plane[j0 // BANK][:, cols]
 
         def by_row(source):
-            return source.rearrange("p i (pair e) -> p pair i e", e=2)
+            return source.rearrange("p i (quad e) -> p quad i e", e=PACK)
 
         def by_column(packed):
-            return packed.rearrange("p (pair e i) -> p pair i e", e=2, i=PACK)
+            return packed.rearrange("p (quad e i) -> p quad i e", e=PACK, i=PACK)
 
         def quantize(codes, plane, packed):
             nc.vector.quantize_mx(out=codes.bitcast(FP8X4), scales=plane, in_=packed)

@@ -229,7 +229,7 @@ def tile_list_sonar_envelopes_kernel(
 
         def squares_on_scalar(*terms):
             filled = [(term, products_of(*term, "scalar")) for term in terms]
-            for term, products in reversed(filled):
+            for term, products in filled:
                 nc.scalar.activation(square_tile(*term), products, ACT.Square)
 
         def square_pair(beam, u, c):

@@ -36,9 +36,9 @@ DEALT = 1
 
 TURNED, DIRECT = 0, 1
 UNITS = (
-    (0, 0, 512, TURNED), (1, 0, 512, DIRECT), (0, 512, 512, TURNED), (1, 512, 256, DIRECT), (1, 768, 256, DIRECT),
+    (0, 0, 512, TURNED), (1, 0, 512, DIRECT), (0, 512, 512, TURNED), (1, 512, 256, DIRECT),
+    (1, 768, 128, DIRECT), (1, 896, 128, DIRECT),
 )
-ON_VECTOR = (("wq", 2, 0), ("wq", 2, 1), ("wq", 2, 2))
 
 
 def tile_list_sonar_envelopes_kernel(
@@ -51,12 +51,15 @@ def tile_list_sonar_envelopes_kernel(
         keep = ctx.enter_context(tc.tile_pool(name="keep", bufs=1))
         psum = ctx.enter_context(tc.psum_pool(name="psum", bufs=1))
         banks = [psum.tile([P, BANK], F32, name="bank%d" % k) for k in range(8)]
-        rings = {"scalar": banks[:SCALAR_BANKS], "vector": banks[SCALAR_BANKS:]}
-        taken = {"scalar": [], "vector": []}
+        free = {"scalar": banks[:SCALAR_BANKS], "vector": banks[SCALAR_BANKS:]}
 
-        def take_bank(ring):
-            taken[ring].append(rings[ring][len(taken[ring]) % len(rings[ring])])
-            return taken[ring][-1]
+        def take_bank(ring="scalar"):
+            bank = free[ring].pop(0)
+            return bank
+
+        def release(bank):
+            ring = "scalar" if any(bank is own for own in banks[:SCALAR_BANKS]) else "vector"
+            free[ring].append(bank)
 
         def held(shape, dtype, name):
             return keep.tile(shape, dtype, name=name, align_bytes=64)
@@ -101,9 +104,9 @@ def tile_list_sonar_envelopes_kernel(
             wi_raw.append(held([P, PASS], I32, "wi_raw%d" % g))
             wq_raw.append(held([P, PACK, PASS], F32, "wq_raw%d" % g))
         nc.sync.dma_start(wi_raw[0][:], wi_dram[:, 0:PASS])
-        for g in range(GROUPS):
-            nc.sync.dma_start(wq_raw[g][:], wq_dram[:, :, g * PASS : (g + 1) * PASS])
+        nc.sync.dma_start(wq_raw[0][:], wq_dram[:, :, 0:PASS])
         nc.sync.dma_start(wi_raw[1][:], wi_dram[:, PASS:H])
+        nc.sync.dma_start(wq_raw[1][:], wq_dram[:, :, PASS:H])
         ambient = held([P, GROUPS, PACK], F32, "ambient")
         nc.sync.dma_start(ambient[:], amb.rearrange("(g p t) -> p g t", g=GROUPS, t=PACK))
         wd_raw = held([P, GROUPS, PACK * N], F32, "wd_raw")
@@ -122,8 +125,10 @@ def tile_list_sonar_envelopes_kernel(
         def gather_scales(b):
             nc.vector.tensor_copy(v_plane[b][:], tab_plane[:].indirect(half_list(b)))
 
-        def gather_words(b):
-            nc.vector.tensor_copy(v_codes[b][:], tab[:].bitcast(U32).indirect(half_list(b)))
+        def gather_words(first, count):
+            entries = offsets[:, first // LIST_ROWS : (first + count) // LIST_ROWS]
+            target = v_codes[first // BANK][:, first % BANK : first % BANK + count]
+            nc.vector.tensor_copy(target, tab[:].bitcast(U32).indirect(entries))
 
         def snapshots(j0, width):
             cols = slice(j0 % BANK, j0 % BANK + width)
@@ -158,45 +163,51 @@ def tile_list_sonar_envelopes_kernel(
         for g in range(GROUPS):
             weights["wi", g, False] = (wi_raw[g][:], wi_plane[WI_ROW:P, g * PASS : (g + 1) * PASS])
 
-        def deal_wi():
-            codes, plane = held([P, PASS], I32, "wi_dealt_codes"), held([P, PASS], U8, "wi_dealt_plane")
-            sources = (wi_raw[DEALT][:], wi_plane[:, DEALT * PASS : (DEALT + 1) * PASS])
-            for target, source, run in zip((codes, plane), sources, (4, 16)):
-                nc.vector.tensor_copy(
-                    target[:].rearrange("p (t hi lo) -> p hi t lo", t=PACK, lo=run),
-                    source.rearrange("p (hi lo t) -> p hi t lo", lo=run, t=PACK),
-                )
-            weights["wi", DEALT, True] = (codes[:], plane[WI_ROW:P, :])
+        dealt_codes, dealt_plane = held([P, PASS], I32, "wi_dealt_codes"), held([P, PASS], U8, "wi_dealt_plane")
+        weights["wi", DEALT, True] = (dealt_codes[:], dealt_plane[WI_ROW:P, :])
+
+        def deal(target, source, run):
+            nc.vector.tensor_copy(
+                target.rearrange("p (t hi lo) -> p hi t lo", t=PACK, lo=run),
+                source.rearrange("p (hi lo t) -> p hi t lo", lo=run, t=PACK),
+            )
+
+        def deal_wi_plane():
+            deal(dealt_plane[:], wi_plane[:, DEALT * PASS : (DEALT + 1) * PASS], 16)
+
+        def deal_wi_words():
+            deal(dealt_codes[:], wi_raw[DEALT][:], 4)
 
         wd_codes = held([P, GROUPS * N], U32, "wd_codes")
         wd_plane = held([P, GROUPS * N], U8, "wd_plane")
         wd_packed = held([P, GROUPS * N * PACK], BF16, "wd_packed")
 
-        def round_negated_wd():
-            for g in range(GROUPS):
-                nc.vector.tensor_scalar(
-                    out=by_column(wd_packed[:, g * N * PACK : (g + 1) * N * PACK]),
-                    in0=by_row(wd_raw[:, g, :].rearrange("p (i n) -> p i n", i=PACK)),
-                    scalar1=-1.0, scalar2=None, op0=ALU.mult,
-                )
+        def round_negated_wd(g):
+            nc.vector.tensor_scalar(
+                out=by_column(wd_packed[:, g * N * PACK : (g + 1) * N * PACK]),
+                in0=by_row(wd_raw[:, g, :].rearrange("p (i n) -> p i n", i=PACK)),
+                scalar1=-1.0, scalar2=None, op0=ALU.mult,
+            )
 
-        def quantize_wd():
-            for first, stop in ((0, PASS), (PASS, GROUPS * N)):
-                quantize(wd_codes[:, first:stop], wd_plane[:, first:stop], wd_packed[:, first * PACK : stop * PACK])
+        def quantize_wd(g):
+            cols = slice(g * N, (g + 1) * N)
+            quantize(wd_codes[:, cols], wd_plane[:, cols], wd_packed[:, g * N * PACK : (g + 1) * N * PACK])
 
         env_codes = {
             (g, b): held([P, BANK], U32, "env_codes%d%d" % (g, b)) for g in range(GROUPS) for b in range(HALVES)
         }
-        env_plane = [held([P, S], U8, "env_plane%d" % g) for g in range(GROUPS)]
+        env_planes = [held([P, GROUPS, BANK], U8, "env_planes%d" % b) for b in range(HALVES)]
+
+        def env_plane(g, j0, width):
+            return env_planes[j0 // BANK][:, g, j0 % BANK : j0 % BANK + width]
         out_1_rows = out_1.rearrange("(g p t) j -> g p t j", g=GROUPS, t=PACK)
         out_0_rows = out_0.rearrange("(n p) j -> p n j", p=P)
         squares = {}
 
-        def products_of(beam, u, c, ring):
+        def products_of(beam, u, c, bank):
             g, j0, width, road = UNITS[u]
             dealt = g == DEALT and (beam == "wq" or road == DIRECT)
             codes, plane = weights[beam, g, dealt]
-            bank = take_bank(ring)
             if road == DIRECT:
                 v, v_scale = snapshots(j0, width)
                 per_bank = BANK // width
@@ -221,35 +232,53 @@ def tile_list_sonar_envelopes_kernel(
                 squares[beam, u] = held([P, UNITS[u][2] // P, PACK, P], F32, "%s_square%d" % (beam, u))
             return squares[beam, u][:, c]
 
+        filled = {}
+
+        def fill(beam, u, c, ring="scalar"):
+            bank = take_bank(ring)
+            filled[beam, u, c] = (bank, products_of(beam, u, c, bank))
+
         def square_on_vector(beam, u, c):
-            products = products_of(beam, u, c, "vector")
+            bank, products = filled[beam, u, c]
             nc.vector.tensor_reduce(
                 square_tile(beam, u, c), products.unsqueeze(3).to_broadcast([P, PACK, P, 2]), AXIS.X, ALU.mult
             )
+            release(bank)
 
-        def squares_on_scalar(*terms):
-            filled = [(term, products_of(*term, "scalar")) for term in terms]
-            for term, products in filled:
-                nc.scalar.activation(square_tile(*term), products, ACT.Square)
+        def square(beam, u, c):
+            bank, products = filled[beam, u, c]
+            nc.scalar.activation(square_tile(beam, u, c), products, ACT.Square)
+            release(bank)
 
-        def square_pair(beam, u, c):
-            squares_on_scalar((beam, u, c), (beam, u, c + 1))
-
-        env = [held([P, PACK, width], F32, "env%d" % u) for u, (g, j0, width, road) in enumerate(UNITS)]
+        env = [held([P, PACK, width], F32, "env%d" % u)[:] for u, (g, j0, width, road) in enumerate(UNITS[:4])]
+        last_env = held([P, PACK, 2 * P], F32, "last_env")
+        env.extend([last_env[:, :, 0:P], last_env[:, :, P : 2 * P]])
         env_packed = [held([P, PACK * width], BF16, "env_packed%d" % u) for u, (g, j0, width, road) in enumerate(UNITS)]
 
-        def root_turned(u, t):
-            g, j0, width, road = UNITS[u]
-            bank = take_bank("scalar")
-            terms = [(beam, c) for beam in ("wq", "wi") for c in reversed(range(PACK))]
-            for beam, c in terms:
+        sums = {}
+
+        def turn(u, k):
+            width = UNITS[u][2]
+            rows, blocks = BANK // width, width // P
+            bank = take_bank()
+            sums[u, k] = bank
+            terms = [(beam, r, c) for beam in ("wi", "wq") for r in range(rows) for c in range(blocks)]
+            for beam, r, c in terms:
+                place = r * width + c * P
                 nc.tensor.matmul(
-                    bank[:, c * P : (c + 1) * P], lhsT=squares[beam, u][:, c, t, :], rhs=ident[:],
-                    is_transpose=True, start=((beam, c) == terms[0]), stop=((beam, c) == terms[-1]),
+                    bank[:, place : place + P], lhsT=squares[beam, u][:, c, k * rows + r, :], rhs=ident[:],
+                    is_transpose=True, start=((beam, r, c) == terms[0]), stop=((beam, r, c) == terms[-1]),
                 )
-            nc.scalar.activation(env[u][:, t, :], bank[:], ACT.Sqrt, bias=ambient[:, g, t : t + 1])
-            if t % 2 == 1:
-                store_env(u, slice(t - 1, t + 1))
+
+        def roots_turned(u, k):
+            g, j0, width, road = UNITS[u]
+            rows = BANK // width
+            for r in range(rows):
+                t = k * rows + r
+                nc.scalar.activation(
+                    env[u][:, t, :], sums[u, k][:, r * width : (r + 1) * width], ACT.Sqrt, bias=ambient[:, g, t : t + 1]
+                )
+            release(sums[u, k])
 
         power = {}
 
@@ -275,6 +304,9 @@ def tile_list_sonar_envelopes_kernel(
             g, j0, width, road = UNITS[u]
             nc.sync.dma_start(out_1_rows[g, :, rows, j0 : j0 + width], env[u][:, rows, :])
 
+        def store_last_env():
+            nc.sync.dma_start(out_1_rows[1, :, :, S - 2 * P : S], last_env[:])
+
         def round_env(u, first, count):
             nc.vector.tensor_copy(
                 by_column(env_packed[u][:, first * PACK : (first + count) * PACK]),
@@ -286,17 +318,23 @@ def tile_list_sonar_envelopes_kernel(
             start, end = j0 + first, j0 + first + count
             codes = env_codes[g, j0 // BANK]
             quantize(
-                codes[:, start % BANK : start % BANK + count], env_plane[g][:, start:end],
+                codes[:, start % BANK : start % BANK + count], env_plane(g, start, count),
                 env_packed[u][:, first * PACK : (first + count) * PACK],
             )
-            if end == j0 + width:
+
+        def store_codes(g, j0, end):
+            codes = env_codes[g, j0 // BANK]
+            width = end - j0
+            if width:
                 out_2_words = out_2[g].rearrange("p j t -> p (j t)").bitcast(I32)
                 nc.sync.dma_start(out_2_words[:, j0:end], codes[:, j0 % BANK : j0 % BANK + width].bitcast(I32))
-            if end == S:
-                for s in range(LIVE_ROWS):
-                    nc.sync.dma_start(
-                        out_3[g, s:SCALE_ROWS:LIVE_ROWS, :].bitcast(I32), env_plane[g][s:P:QUADRANT, :].bitcast(I32)
-                    )
+
+        def store_scales(first, stop):
+            for s in range(LIVE_ROWS):
+                nc.sync.dma_start(
+                    out_3[:, s:SCALE_ROWS:LIVE_ROWS, first:stop].rearrange("g q j -> q g j").bitcast(I32),
+                    env_planes[first // BANK][s:P:QUADRANT].bitcast(I32),
+                )
 
         def readout_pass(target, source, n, j0, width, start, stop):
             if source == "clutter":
@@ -310,7 +348,7 @@ def tile_list_sonar_envelopes_kernel(
             nc.tensor.matmul_mx(
                 out=target, lhsT=wd_codes[:, cols].bitcast(FP8X4), lhsT_scale=wd_plane[:, cols],
                 rhs=env_codes[source, j0 // BANK][:, j0 % BANK : j0 % BANK + width].bitcast(FP8X4),
-                rhs_scale=env_plane[source][:, j0 : j0 + width], start=start, stop=stop,
+                rhs_scale=env_plane(source, j0, width), start=start, stop=stop,
             )
 
         def empty(target, bank, on_scalar):
@@ -319,11 +357,13 @@ def tile_list_sonar_envelopes_kernel(
             else:
                 nc.vector.tensor_scalar(out=target, in0=bank, scalar1=-1.0, scalar2=None, op0=ALU.mult)
 
-        y = {u: held([P, ROW_TILES, UNITS[u][2]], F32, "y%d" % u) for u in (1, 3, 4)}
+        y = {u: held([P, ROW_TILES, UNITS[u][2]], F32, "y%d" % u)[:] for u in (1, 3)}
+        last_y = held([P, ROW_TILES, 2 * P], F32, "last_y")
+        y[4], y[5] = last_y[:, :, 0:P], last_y[:, :, P : 2 * P]
         opened = {}
 
-        def wide_passes(u, source):
-            for n in range(ROW_TILES):
+        def wide_passes(u, source, first=0, stop=ROW_TILES):
+            for n in range(first, stop):
                 if source == "clutter":
                     opened[u, n] = take_bank("vector")
                 readout_pass(opened[u, n][:], source, n, UNITS[u][1], BANK, source == "clutter", source == 1)
@@ -331,12 +371,13 @@ def tile_list_sonar_envelopes_kernel(
         def empty_wide(u, n, on_scalar):
             j0 = UNITS[u][1]
             empty(y[u][:, n, :], opened[u, n][:], on_scalar)
+            release(opened[u, n])
             nc.sync.dma_start(out_0_rows[:, n, j0 : j0 + BANK], y[u][:, n, :])
 
-        def readout_passes(u, first, ring, sources, start, stop):
+        def readout_passes(u, first, sources, start, stop):
             j0 = UNITS[u][1]
             if start:
-                opened[u, first] = take_bank(ring)[:, 0 : ROW_TILES * P].rearrange("p (n j) -> p n j", n=ROW_TILES)
+                opened[u, first] = take_bank()[:, 0 : ROW_TILES * P].rearrange("p (n j) -> p n j", n=ROW_TILES)
             for source in sources:
                 for n in range(ROW_TILES):
                     readout_pass(
@@ -345,8 +386,25 @@ def tile_list_sonar_envelopes_kernel(
                         stop and source == sources[-1] and n == ROW_TILES - 1,
                     )
 
+        def middle_passes(u, source, ring="scalar"):
+            j0, width = UNITS[u][1], UNITS[u][2]
+            if source == "clutter":
+                opened[u, 0], opened[u, 1] = take_bank(ring), take_bank(ring)
+            for n in range(ROW_TILES):
+                target = opened[u, n // 2][:, (n % 2) * width : (n % 2 + 1) * width]
+                readout_pass(target, source, n, j0, width, source == "clutter" and n != 1, source == 1 and n != 0)
+
+        def empty_middle(u, k, on_scalar):
+            width = UNITS[u][2]
+            rows = min(2, ROW_TILES - 2 * k)
+            empty(y[u][:, 2 * k : 2 * k + rows, :].rearrange("p n j -> p (n j)"), opened[u, k][:, 0 : rows * width], on_scalar)
+            release(opened[u, k])
+
         def empty_narrow(u, first, on_scalar):
             empty(y[u][:, :, first : first + P], opened[u, first], on_scalar)
+
+        def store_last_y():
+            nc.sync.dma_start(out_0_rows[:, :, S - 2 * P : S], last_y[:])
 
         def store_y(u, first, count):
             j0 = UNITS[u][1]
@@ -354,81 +412,158 @@ def tile_list_sonar_envelopes_kernel(
 
         gather_scales(0)
         gather_scales(1)
-        gather_words(0)
-        gather_words(1)
+        gather_words(0, 2 * P)
+        gather_words(2 * P, 2 * P)
+        gather_words(BANK, BANK)
         low, high, every = slice(0, 2), slice(2, 4), slice(0, 4)
-        for u in (0, 2):
-            square_pair("wi", u, 0)
-            square_pair("wi", u, 2)
+
+        def row(t):
+            return slice(t, t + 1)
+
+        fill("wi", 0, 0)
+        fill("wi", 0, 1)
+        square("wi", 0, 0)
+        square("wi", 0, 1)
+        fill("wi", 0, 2)
+        fill("wi", 0, 3)
+        square("wi", 0, 2)
+        square("wi", 0, 3)
+        fill("wi", 2, 0)
+        fill("wi", 2, 1)
+        square("wi", 2, 0)
+        square("wi", 2, 1)
+        fill("wi", 2, 2)
+        fill("wi", 2, 3)
+        square("wi", 2, 2)
+        square("wi", 2, 3)
         round_wq(0)
+        deal_wi_words()
         quantize_wq(0)
-        square_pair("wq", 0, 0)
-        square_pair("wq", 0, 2)
+        fill("wq", 0, 0)
+        fill("wq", 0, 1)
+        square("wq", 0, 0)
+        square("wq", 0, 1)
+        fill("wq", 0, 2)
+        fill("wq", 0, 3)
+        square("wq", 0, 2)
+        square("wq", 0, 3)
         round_wq(1)
-        deal_wi()
-        quantize_wq(1)
+        deal_wi_plane()
+        fill("wq", 2, 0, "vector")
         square_on_vector("wq", 2, 0)
-        square_pair("wi", 1, 0)
-        root_turned(0, 0)
+        quantize_wq(1)
+        fill("wi", 1, 0)
+        fill("wi", 1, 1)
+        square("wi", 1, 0)
+        square("wi", 1, 1)
+        turn(0, 0)
+        roots_turned(0, 0)
+        fill("wq", 2, 1, "vector")
         square_on_vector("wq", 2, 1)
-        square_pair("wi", 1, 2)
-        root_turned(0, 1)
-        round_negated_wd()
-        square_on_vector("wq", 2, 2)
-        quantize_wd()
-        square_pair("wq", 1, 0)
-        root_turned(0, 2)
-        square_on_vector("wq", 2, 3)
-        square_pair("wq", 1, 2)
-        root_turned(0, 3)
+        fill("wq", 1, 0)
+        fill("wq", 1, 1)
+        square("wq", 1, 0)
+        square("wq", 1, 1)
+        turn(0, 1)
+        roots_turned(0, 1)
+        store_env(0, low)
+        round_negated_wd(0)
+        round_negated_wd(1)
         add_squares(1, 0, 2)
+        fill("wi", 1, 2)
+        fill("wi", 1, 3)
+        square("wi", 1, 2)
+        square("wi", 1, 3)
+        turn(0, 2)
+        roots_turned(0, 2)
+        fill("wq", 2, 2, "vector")
+        square_on_vector("wq", 2, 2)
+        fill("wq", 2, 3, "vector")
+        square_on_vector("wq", 2, 3)
+        fill("wq", 1, 2)
+        fill("wq", 1, 3)
+        square("wq", 1, 2)
+        square("wq", 1, 3)
+        turn(0, 3)
+        roots_turned(0, 3)
+        store_env(0, high)
         add_squares(1, 2, 2)
-        round_env(0, 0, BANK)
-        square_pair("wi", 3, 0)
         roots_direct(1, low, 0, BANK)
         store_env(1, low)
+        round_env(0, 0, BANK)
+        fill("wi", 3, 0)
+        turn(2, 0)
+        wide_passes(1, "clutter", 0, 1)
+        turn(2, 1)
+        fill("wi", 3, 1)
+        fill("wq", 3, 0)
+        wide_passes(1, "clutter", 1, 3)
+        square("wi", 3, 0)
         roots_direct(1, high, 0, BANK)
         store_env(1, high)
+        quantize_wd(0)
         quantize_env(0, 0, BANK)
+        store_codes(0, 0, BANK)
         round_env(1, 0, BANK)
-        root_turned(2, 0)
-        wide_passes(1, "clutter")
-        root_turned(2, 1)
-        square_pair("wq", 3, 0)
+        quantize_wd(1)
         quantize_env(1, 0, BANK)
-        add_squares(3, 0, 2)
+        store_codes(1, 0, BANK)
+        store_scales(0, BANK)
+        roots_turned(2, 0)
+        turn(2, 2)
+        roots_turned(2, 1)
+        store_env(2, low)
         wide_passes(1, 0)
-        root_turned(2, 2)
-        root_turned(2, 3)
-        roots_direct(3, every, 0, 2 * P)
-        store_env(3, every)
-        square_pair("wi", 4, 0)
+        fill("wq", 3, 1)
+        square("wi", 3, 1)
+        turn(2, 3)
+        square("wq", 3, 0)
         wide_passes(1, 1)
+        roots_turned(2, 2)
+        square("wq", 3, 1)
+        roots_turned(2, 3)
+        store_env(2, high)
+        empty_wide(1, 0, False)
+        add_squares(3, 0, 2)
+        fill("wi", 4, 0)
+        square("wi", 4, 0)
+        fill("wq", 4, 0)
+        square("wq", 4, 0)
         round_env(2, 0, BANK)
-        for n in range(ROW_TILES - 2):
-            empty_wide(1, n, False)
+        empty_wide(1, 1, True)
+        roots_direct(3, every, 0, 2*P)
+        store_env(3, every)
+        add_squares(4, 0, 1)
         quantize_env(2, 0, BANK)
-        square_pair("wq", 4, 0)
-        round_env(3, 0, 2 * P)
-        add_squares(4, 0, 2)
-        for n in range(ROW_TILES - 2, ROW_TILES):
-            empty_wide(1, n, True)
-        quantize_env(3, 0, 2 * P)
-        for first in (0, P):
-            readout_passes(3, first, "scalar", ("clutter", 0, 1), True, True)
-        for first in (0, P):
-            readout_passes(4, first, "scalar", ("clutter", 0), True, False)
-        for first in (0, P):
-            roots_direct(4, every, first, P)
-        store_env(4, every)
-        for first in (0, P):
-            round_env(4, first, P)
-        for first in (0, P):
-            quantize_env(4, first, P)
-        for first in (0, P):
-            empty_narrow(3, first, True)
-        store_y(3, 0, 2 * P)
-        for first in (0, P):
-            readout_passes(4, first, "scalar", (1,), False, True)
-            empty_narrow(4, first, first == 0)
-        store_y(4, 0, 2 * P)
+        store_codes(0, BANK, S)
+        fill("wi", 5, 0)
+        square("wi", 5, 0)
+        fill("wq", 5, 0)
+        square("wq", 5, 0)
+        round_env(3, 0, 2*P)
+        add_squares(5, 0, 1)
+        quantize_env(3, 0, 2*P)
+        store_codes(1, BANK, BANK+2*P)
+        empty_wide(1, 2, True)
+        roots_direct(4, every, 0, P)
+        middle_passes(3, "clutter")
+        middle_passes(3, 0)
+        middle_passes(3, 1)
+        readout_passes(4, 0, ("clutter", 0), True, False)
+        readout_passes(5, 0, ("clutter", 0), True, False)
+        roots_direct(5, every, 0, P)
+        store_last_env()
+        round_env(4, 0, P)
+        quantize_env(4, 0, P)
+        round_env(5, 0, P)
+        empty_middle(3, 0, True)
+        empty_middle(3, 1, True)
+        store_y(3, 0, 2*P)
+        readout_passes(4, 0, (1,), False, True)
+        quantize_env(5, 0, P)
+        store_codes(1, BANK+2*P, S)
+        store_scales(BANK, S)
+        readout_passes(5, 0, (1,), False, True)
+        empty_narrow(4, 0, False)
+        empty_narrow(5, 0, True)
+        store_last_y()

@@ -148,9 +148,10 @@ def tile_list_sonar_envelopes_kernel(
 
         def round_wq(g):
             if g == DEALT:
-                nc.vector.tensor_copy(
-                    wq_packed[g][:].rearrange("p (t m i) -> p m t i", t=PACK, i=PACK),
-                    wq_raw[g][:].rearrange("p i (m t) -> p m t i", t=PACK),
+                nc.gpsimd.tensor_scalar(
+                    out=wq_packed[g][:].rearrange("p (t m i) -> p m t i", t=PACK, i=PACK),
+                    in0=wq_raw[g][:].rearrange("p i (m t) -> p m t i", t=PACK),
+                    scalar1=1.0, scalar2=0.0, op0=ALU.mult, op1=ALU.add,
                 )
             else:
                 nc.vector.tensor_copy(by_column(wq_packed[g][:]), by_row(wq_raw[g][:]))
@@ -438,19 +439,25 @@ def tile_list_sonar_envelopes_kernel(
         square("wi", 2, 3)
         round_wq(0)
         deal_wi_words()
+        deal_wi_plane()
         quantize_wq(0)
+        fill("wi", 1, 3, "vector")
+        square_on_vector("wi", 1, 3)
         fill("wq", 0, 0)
         fill("wq", 0, 1)
         square("wq", 0, 0)
         square("wq", 0, 1)
+        round_wq(1)
+        fill("wq", 2, 0, "vector")
+        square_on_vector("wq", 2, 0)
         fill("wq", 0, 2)
         fill("wq", 0, 3)
         square("wq", 0, 2)
         square("wq", 0, 3)
-        round_wq(1)
-        deal_wi_plane()
-        fill("wq", 2, 0, "vector")
-        square_on_vector("wq", 2, 0)
+        fill("wq", 2, 1, "vector")
+        square_on_vector("wq", 2, 1)
+        fill("wq", 2, 2, "vector")
+        square_on_vector("wq", 2, 2)
         quantize_wq(1)
         fill("wi", 1, 0)
         fill("wi", 1, 1)
@@ -458,28 +465,24 @@ def tile_list_sonar_envelopes_kernel(
         square("wi", 1, 1)
         turn(0, 0)
         roots_turned(0, 0)
-        fill("wq", 2, 1, "vector")
-        square_on_vector("wq", 2, 1)
-        fill("wq", 1, 0)
-        fill("wq", 1, 1)
-        square("wq", 1, 0)
-        square("wq", 1, 1)
+        fill("wq", 2, 3, "vector")
+        square_on_vector("wq", 2, 3)
+        fill("wi", 1, 2)
+        fill("wi", 3, 0)
+        square("wi", 1, 2)
+        square("wi", 3, 0)
         turn(0, 1)
         roots_turned(0, 1)
         store_env(0, low)
         round_negated_wd(0)
         round_negated_wd(1)
-        add_squares(1, 0, 2)
-        fill("wi", 1, 2)
-        fill("wi", 1, 3)
-        square("wi", 1, 2)
-        square("wi", 1, 3)
+        fill("wq", 1, 0)
+        fill("wq", 1, 1)
+        square("wq", 1, 0)
+        square("wq", 1, 1)
         turn(0, 2)
         roots_turned(0, 2)
-        fill("wq", 2, 2, "vector")
-        square_on_vector("wq", 2, 2)
-        fill("wq", 2, 3, "vector")
-        square_on_vector("wq", 2, 3)
+        add_squares(1, 0, 2)
         fill("wq", 1, 2)
         fill("wq", 1, 3)
         square("wq", 1, 2)
@@ -487,83 +490,81 @@ def tile_list_sonar_envelopes_kernel(
         turn(0, 3)
         roots_turned(0, 3)
         store_env(0, high)
+        quantize_wd(0)
+        quantize_wd(1)
         add_squares(1, 2, 2)
         roots_direct(1, low, 0, BANK)
         store_env(1, low)
         round_env(0, 0, BANK)
-        fill("wi", 3, 0)
+        fill("wi", 3, 1)
         turn(2, 0)
         wide_passes(1, "clutter", 0, 1)
         turn(2, 1)
-        fill("wi", 3, 1)
         fill("wq", 3, 0)
+        fill("wq", 3, 1)
         wide_passes(1, "clutter", 1, 3)
-        square("wi", 3, 0)
+        square("wi", 3, 1)
         roots_direct(1, high, 0, BANK)
         store_env(1, high)
-        quantize_wd(0)
         quantize_env(0, 0, BANK)
         store_codes(0, 0, BANK)
         round_env(1, 0, BANK)
-        quantize_wd(1)
         quantize_env(1, 0, BANK)
         store_codes(1, 0, BANK)
         store_scales(0, BANK)
-        roots_turned(2, 0)
         turn(2, 2)
+        roots_turned(2, 0)
+        turn(2, 3)
         roots_turned(2, 1)
         store_env(2, low)
         wide_passes(1, 0)
-        fill("wq", 3, 1)
-        square("wi", 3, 1)
-        turn(2, 3)
         square("wq", 3, 0)
-        wide_passes(1, 1)
-        roots_turned(2, 2)
         square("wq", 3, 1)
+        fill("wi", 4, 0)
+        fill("wq", 4, 0)
+        roots_turned(2, 2)
+        wide_passes(1, 1)
+        add_squares(3, 0, 2)
         roots_turned(2, 3)
         store_env(2, high)
-        empty_wide(1, 0, False)
-        add_squares(3, 0, 2)
-        fill("wi", 4, 0)
-        square("wi", 4, 0)
-        fill("wq", 4, 0)
-        square("wq", 4, 0)
         round_env(2, 0, BANK)
-        empty_wide(1, 1, True)
+        square("wi", 4, 0)
+        square("wq", 4, 0)
+        empty_wide(1, 0, False)
+        empty_wide(1, 1, False)
         roots_direct(3, every, 0, 2*P)
         store_env(3, every)
-        add_squares(4, 0, 1)
         quantize_env(2, 0, BANK)
         store_codes(0, BANK, S)
+        add_squares(4, 0, 1)
         fill("wi", 5, 0)
         square("wi", 5, 0)
         fill("wq", 5, 0)
         square("wq", 5, 0)
         round_env(3, 0, 2*P)
+        middle_passes(3, "clutter", "vector")
+        middle_passes(3, 0)
         add_squares(5, 0, 1)
         quantize_env(3, 0, 2*P)
         store_codes(1, BANK, BANK+2*P)
         empty_wide(1, 2, True)
         roots_direct(4, every, 0, P)
-        middle_passes(3, "clutter")
-        middle_passes(3, 0)
         middle_passes(3, 1)
         readout_passes(4, 0, ("clutter", 0), True, False)
         readout_passes(5, 0, ("clutter", 0), True, False)
         roots_direct(5, every, 0, P)
         store_last_env()
         round_env(4, 0, P)
+        empty_middle(3, 1, False)
         quantize_env(4, 0, P)
         round_env(5, 0, P)
         empty_middle(3, 0, True)
-        empty_middle(3, 1, True)
         store_y(3, 0, 2*P)
         readout_passes(4, 0, (1,), False, True)
         quantize_env(5, 0, P)
         store_codes(1, BANK+2*P, S)
         store_scales(BANK, S)
         readout_passes(5, 0, (1,), False, True)
-        empty_narrow(4, 0, False)
-        empty_narrow(5, 0, True)
+        empty_narrow(4, 0, True)
+        empty_narrow(5, 0, False)
         store_last_y()

@@ -37,8 +37,9 @@ DEALT = 1
 TURNED, DIRECT = 0, 1
 UNITS = (
     (0, 0, 512, TURNED), (1, 0, 512, DIRECT), (0, 512, 512, TURNED), (1, 512, 256, DIRECT),
-    (1, 768, 128, DIRECT), (1, 896, 128, DIRECT),
+    (1, 768, 128, TURNED), (1, 896, 128, TURNED),
 )
+REUSED = {}
 
 
 def tile_list_sonar_envelopes_kernel(
@@ -61,8 +62,8 @@ def tile_list_sonar_envelopes_kernel(
             ring = "scalar" if any(bank is own for own in banks[:SCALAR_BANKS]) else "vector"
             free[ring].append(bank)
 
-        def held(shape, dtype, name):
-            return keep.tile(shape, dtype, name=name, align_bytes=64)
+        def held(shape, dtype, name, tag=None):
+            return keep.tile(shape, dtype, name=name, tag=tag or name, align_bytes=64)
 
         offsets = lists.tile([P, S // LIST_ROWS], U16, name="offsets")
         nc.sync.dma_start(offsets[:], offs)
@@ -230,7 +231,7 @@ def tile_list_sonar_envelopes_kernel(
 
         def square_tile(beam, u, c):
             if (beam, u) not in squares:
-                squares[beam, u] = held([P, UNITS[u][2] // P, PACK, P], F32, "%s_square%d" % (beam, u))
+                squares[beam, u] = held([P, UNITS[u][2] // P, PACK, P], F32, "%s_square%d" % (beam, u), REUSED.get((beam, u)))
             return squares[beam, u][:, c]
 
         filled = {}
@@ -254,7 +255,7 @@ def tile_list_sonar_envelopes_kernel(
         env = [held([P, PACK, width], F32, "env%d" % u)[:] for u, (g, j0, width, road) in enumerate(UNITS[:4])]
         last_env = held([P, PACK, 2 * P], F32, "last_env")
         env.extend([last_env[:, :, 0:P], last_env[:, :, P : 2 * P]])
-        env_packed = [held([P, PACK * width], BF16, "env_packed%d" % u) for u, (g, j0, width, road) in enumerate(UNITS)]
+        env_packed = {}
 
         sums = {}
 
@@ -309,6 +310,8 @@ def tile_list_sonar_envelopes_kernel(
             nc.sync.dma_start(out_1_rows[1, :, :, S - 2 * P : S], last_env[:])
 
         def round_env(u, first, count):
+            if u not in env_packed:
+                env_packed[u] = held([P, PACK * UNITS[u][2]], BF16, "env_packed%d" % u, REUSED.get(("packed", u)))
             nc.vector.tensor_copy(
                 by_column(env_packed[u][:, first * PACK : (first + count) * PACK]),
                 by_row(env[u][:, :, first : first + count]),
@@ -418,8 +421,23 @@ def tile_list_sonar_envelopes_kernel(
         gather_words(BANK, BANK)
         low, high, every = slice(0, 2), slice(2, 4), slice(0, 4)
 
-        def row(t):
-            return slice(t, t + 1)
+        def pair(beam, u, c):
+            fill(beam, u, c)
+            fill(beam, u, c + 1)
+            square(beam, u, c)
+            square(beam, u, c + 1)
+
+        def one(beam, u, c=0):
+            fill(beam, u, c)
+            square(beam, u, c)
+
+        def on_vector(beam, u, c):
+            fill(beam, u, c, "vector")
+            square_on_vector(beam, u, c)
+
+        def turned_root(u, k):
+            turn(u, k)
+            roots_turned(u, k)
 
         fill("wi", 0, 0)
         fill("wi", 0, 1)
@@ -476,83 +494,85 @@ def tile_list_sonar_envelopes_kernel(
         store_env(0, low)
         round_negated_wd(0)
         round_negated_wd(1)
-        fill("wq", 1, 0)
-        fill("wq", 1, 1)
-        square("wq", 1, 0)
-        square("wq", 1, 1)
-        turn(0, 2)
-        roots_turned(0, 2)
+        pair("wq", 1, 0)
         add_squares(1, 0, 2)
-        fill("wq", 1, 2)
-        fill("wq", 1, 3)
-        square("wq", 1, 2)
-        square("wq", 1, 3)
-        turn(0, 3)
-        roots_turned(0, 3)
-        store_env(0, high)
+        pair("wq", 1, 2)
+        add_squares(1, 2, 2)
+        turned_root(0, 2)
+        store_env(0, slice(2, 3))
+        turned_root(0, 3)
+        store_env(0, slice(3, 4))
         quantize_wd(0)
         quantize_wd(1)
-        add_squares(1, 2, 2)
-        roots_direct(1, low, 0, BANK)
-        store_env(1, low)
+        roots_direct(1, slice(0, 1), 0, BANK)
+        store_env(1, slice(0, 1))
+        roots_direct(1, slice(1, 2), 0, BANK)
+        store_env(1, slice(1, 2))
+        roots_direct(1, slice(2, 3), 0, BANK)
+        store_env(1, slice(2, 3))
+        roots_direct(1, slice(3, 4), 0, BANK)
+        store_env(1, slice(3, 4))
         round_env(0, 0, BANK)
-        fill("wi", 3, 1)
+        wide_passes(1, "clutter", 0, 2)
         turn(2, 0)
-        wide_passes(1, "clutter", 0, 1)
         turn(2, 1)
+        fill("wi", 3, 1)
         fill("wq", 3, 0)
-        fill("wq", 3, 1)
-        wide_passes(1, "clutter", 1, 3)
-        square("wi", 3, 1)
-        roots_direct(1, high, 0, BANK)
-        store_env(1, high)
-        quantize_env(0, 0, BANK)
-        store_codes(0, 0, BANK)
+        turn(2, 2)
+        wide_passes(1, "clutter", 2, 3)
         round_env(1, 0, BANK)
+        quantize_env(0, 0, BANK)
         quantize_env(1, 0, BANK)
+        roots_turned(2, 0)
+        store_env(2, slice(0, 1))
+        fill("wq", 3, 1)
+        roots_turned(2, 1)
+        turn(2, 3)
+        store_env(2, slice(1, 2))
+        store_codes(0, 0, BANK)
         store_codes(1, 0, BANK)
         store_scales(0, BANK)
-        turn(2, 2)
-        roots_turned(2, 0)
-        turn(2, 3)
-        roots_turned(2, 1)
-        store_env(2, low)
-        wide_passes(1, 0)
-        square("wq", 3, 0)
-        square("wq", 3, 1)
+        square("wi", 3, 1)
         fill("wi", 4, 0)
+        square("wq", 3, 0)
         fill("wq", 4, 0)
-        roots_turned(2, 2)
-        wide_passes(1, 1)
+        square("wq", 3, 1)
+        wide_passes(1, 0, 0, 1)
+        wide_passes(1, 1, 0, 1)
+        wide_passes(1, 0, 1, 2)
+        wide_passes(1, 1, 1, 2)
+        wide_passes(1, 0, 2, 3)
+        wide_passes(1, 1, 2, 3)
         add_squares(3, 0, 2)
+        roots_turned(2, 2)
+        fill("wi", 5, 0)
         roots_turned(2, 3)
+        fill("wq", 5, 0)
         store_env(2, high)
+        empty_wide(1, 0, False)
+        empty_wide(1, 1, False)
+        empty_wide(1, 2, False)
         round_env(2, 0, BANK)
         square("wi", 4, 0)
         square("wq", 4, 0)
-        empty_wide(1, 0, False)
-        empty_wide(1, 1, False)
+        turn(4, 0)
         roots_direct(3, every, 0, 2*P)
         store_env(3, every)
+        round_env(3, 0, 2*P)
         quantize_env(2, 0, BANK)
         store_codes(0, BANK, S)
-        add_squares(4, 0, 1)
-        fill("wi", 5, 0)
         square("wi", 5, 0)
-        fill("wq", 5, 0)
         square("wq", 5, 0)
-        round_env(3, 0, 2*P)
+        turn(5, 0)
+        roots_turned(4, 0)
         middle_passes(3, "clutter", "vector")
         middle_passes(3, 0)
-        add_squares(5, 0, 1)
         quantize_env(3, 0, 2*P)
         store_codes(1, BANK, BANK+2*P)
-        empty_wide(1, 2, True)
-        roots_direct(4, every, 0, P)
         middle_passes(3, 1)
         readout_passes(4, 0, ("clutter", 0), True, False)
         readout_passes(5, 0, ("clutter", 0), True, False)
-        roots_direct(5, every, 0, P)
+        roots_turned(5, 0)
         store_last_env()
         round_env(4, 0, P)
         empty_middle(3, 1, False)

@@ -39,7 +39,7 @@ UNITS = (
     (0, 0, 512, TURNED), (1, 0, 512, DIRECT), (0, 512, 512, TURNED), (1, 512, 256, DIRECT),
     (1, 768, 128, TURNED), (1, 896, 128, TURNED),
 )
-REUSED = {}
+REUSED = {("packed", 2): "env_packed2"}
 
 
 def tile_list_sonar_envelopes_kernel(
@@ -259,10 +259,10 @@ def tile_list_sonar_envelopes_kernel(
 
         sums = {}
 
-        def turn(u, k):
+        def turn(u, k, ring="scalar"):
             width = UNITS[u][2]
             rows, blocks = BANK // width, width // P
-            bank = take_bank()
+            bank = take_bank(ring)
             sums[u, k] = bank
             terms = [(beam, r, c) for beam in ("wi", "wq") for r in range(rows) for c in range(blocks)]
             for beam, r, c in terms:
@@ -355,11 +355,14 @@ def tile_list_sonar_envelopes_kernel(
                 rhs_scale=env_plane(source, j0, width), start=start, stop=stop,
             )
 
-        def empty(target, bank, on_scalar):
+        minus_one = held([P, 1], F32, "minus_one", "env_packed2")
+        nc.vector.memset(minus_one[:], -1.0)
+
+        def empty(target, bank, on_scalar, sign=-1.0):
             if on_scalar:
                 nc.scalar.activation(target, bank, ACT.Copy, scale=-1.0)
             else:
-                nc.vector.tensor_scalar(out=target, in0=bank, scalar1=-1.0, scalar2=None, op0=ALU.mult)
+                nc.vector.tensor_scalar(out=target, in0=bank, scalar1=sign, scalar2=None, op0=ALU.mult)
 
         y = {u: held([P, ROW_TILES, UNITS[u][2]], F32, "y%d" % u)[:] for u in (1, 3)}
         last_y = held([P, ROW_TILES, 2 * P], F32, "last_y")
@@ -374,7 +377,7 @@ def tile_list_sonar_envelopes_kernel(
 
         def empty_wide(u, n, on_scalar):
             j0 = UNITS[u][1]
-            empty(y[u][:, n, :], opened[u, n][:], on_scalar)
+            empty(y[u][:, n, :], opened[u, n][:], on_scalar, minus_one[:] if n < 2 else -1.0)
             release(opened[u, n])
             nc.sync.dma_start(out_0_rows[:, n, j0 : j0 + BANK], y[u][:, n, :])
 

from contextlib import ExitStack

import concourse.mybir as mybir
from concourse.masks import make_identity

K, H, N, T, S = 512, 1024, 384, 4096, 1024
FLOPS = 2 * (2 * K * H * S + K * N * S + H * N * S)

F32 = mybir.dt.float32
BF16 = mybir.dt.bfloat16
I32 = mybir.dt.int32
U32 = mybir.dt.uint32
U16 = mybir.dt.uint16
U8 = mybir.dt.uint8
FP8X4 = mybir.dt.float8_e4m3fn_x4
FP4X4 = mybir.dt.float4_e2m1fn_x4
ACT = mybir.ActivationFunctionType
ALU = mybir.AluOpType
AXIS = mybir.AxisListType

P = 128
PACK = 4
PASS = P * PACK
BANK = 512
GROUPS = H // PASS
HALVES = S // BANK
ROW_TILES = N // P
LIST_ROWS = 16
QUADRANT = 32
SCALE_ROWS = PASS // 32
LIVE_ROWS = 4
WI_ROW = 4
TAB_FIRST = T // 4
SCALAR_BANKS = 5
DEALT = 1

TURNED, DIRECT = 0, 1
UNITS = (
    (0, 0, 512, TURNED), (1, 0, 512, DIRECT), (0, 512, 512, TURNED), (1, 512, 256, DIRECT),
    (1, 768, 128, TURNED), (1, 896, 128, TURNED),
)
REUSED = {("packed", 2): "env_packed2"}


def tile_list_sonar_envelopes_kernel(
    tc, tab_words, tab_scales, offs, wi_words, wi_scales, wq, amb, wd, wc_words, wc_scales,
    out_0, out_1, out_2, out_3,
):
    nc = tc.nc
    with ExitStack() as ctx:
        lists = ctx.enter_context(tc.tile_pool(name="lists", bufs=1))
        keep = ctx.enter_context(tc.tile_pool(name="keep", bufs=1))
        psum = ctx.enter_context(tc.psum_pool(name="psum", bufs=1))
        banks = [psum.tile([P, BANK], F32, name="bank%d" % k) for k in range(8)]
        free = {"scalar": banks[:SCALAR_BANKS], "vector": banks[SCALAR_BANKS:]}

        def take_bank(ring="scalar"):
            bank = free[ring].pop(0)
            return bank

        def release(bank):
            ring = "scalar" if any(bank is own for own in banks[:SCALAR_BANKS]) else "vector"
            free[ring].append(bank)

        def held(shape, dtype, name, tag=None):
            return keep.tile(shape, dtype, name=name, tag=tag or name, align_bytes=64)

        offsets = lists.tile([P, S // LIST_ROWS], U16, name="offsets")
        nc.sync.dma_start(offsets[:], offs)

        tab = held([P, T], I32, "tab")
        tab_dram = tab_words[0].rearrange("p col i -> p (col i)").bitcast(I32)
        nc.sync.dma_start(tab[:, 0:TAB_FIRST], tab_dram[:, 0:TAB_FIRST])

        tab_plane = held([P, T], U8, "tab_plane")
        nc.vector.memset(tab_plane[:].bitcast(I32), 0)
        wi_plane = held([P, H], U8, "wi_plane")
        nc.vector.memset(wi_plane[:].bitcast(I32), 0)
        wc_plane = held([P, N], U8, "wc_plane")
        nc.vector.memset(wc_plane[:].bitcast(I32), 0)

        ident = held([P, P], F32, "ident")
        nc.vector.memset(ident[:], 0.0)
        make_identity(nc, ident[:], nomemset=True)

        def load_plane(plane, scales, first_row):
            for s in range(LIVE_ROWS):
                nc.sync.dma_start(
                    plane[first_row + s : P : QUADRANT, :].bitcast(I32), scales[s:SCALE_ROWS:LIVE_ROWS, :].bitcast(I32)
                )

        load_plane(tab_plane, tab_scales[0], 0)
        nc.sync.dma_start(tab[:, TAB_FIRST:T], tab_dram[:, TAB_FIRST:T])
        load_plane(wi_plane, wi_scales[0], WI_ROW)

        warm = held([P, 1], F32, "warm")
        nc.vector.memset(warm[:], 1.0)
        warm_out = held([P, 1], F32, "warm_out")
        nc.scalar.activation(warm_out[:], warm[:], ACT.Sqrt)

        wi_dram = wi_words[0].rearrange("p col i -> p (col i)").bitcast(I32)
        wq_dram = wq.rearrange("(p i) col -> p i col", i=PACK)
        wi_raw, wq_raw = [], []
        for g in range(GROUPS):
            wi_raw.append(held([P, PASS], I32, "wi_raw%d" % g))
            wq_raw.append(held([P, PACK, PASS], F32, "wq_raw%d" % g))
        nc.sync.dma_start(wi_raw[0][:], wi_dram[:, 0:PASS])
        nc.sync.dma_start(wq_raw[0][:], wq_dram[:, :, 0:PASS])
        nc.sync.dma_start(wi_raw[1][:], wi_dram[:, PASS:H])
        nc.sync.dma_start(wq_raw[1][:], wq_dram[:, :, PASS:H])
        ambient = held([P, GROUPS, PACK], F32, "ambient")
        nc.sync.dma_start(ambient[:], amb.rearrange("(g p t) -> p g t", g=GROUPS, t=PACK))
        wd_raw = held([P, GROUPS, PACK * N], F32, "wd_raw")
        nc.sync.dma_start(wd_raw[:], wd.rearrange("(g p i) n -> p g (i n)", g=GROUPS, i=PACK))
        wc_codes = held([P, 2 * N], U8, "wc_codes")
        nc.sync.dma_start(wc_codes[:].bitcast(I32), wc_words[0].bitcast(I32))
        load_plane(wc_plane, wc_scales[0], 0)


        v_codes = [held([P, BANK], U32, "v_codes%d" % b) for b in range(HALVES)]
        v_plane = [held([P, BANK], U8, "v_plane%d" % b) for b in range(HALVES)]

        def half_list(b):
            return offsets[:, b * (BANK // LIST_ROWS) : (b + 1) * (BANK // LIST_ROWS)]

        def gather_scales(b):
            nc.vector.tensor_copy(v_plane[b][:], tab_plane[:].indirect(half_list(b)))

        def gather_words(first, count):
            entries = offsets[:, first // LIST_ROWS : (first + count) // LIST_ROWS]
            target = v_codes[first // BANK][:, first % BANK : first % BANK + count]
            nc.vector.tensor_copy(target, tab[:].bitcast(U32).indirect(entries))

        def snapshots(j0, width):
            cols = slice(j0 % BANK, j0 % BANK + width)
            return v_codes[j0 // BANK][:, cols].bitcast(FP8X4), v_plane[j0 // BANK][:, cols]

        def by_row(source):
            return source.rearrange("p i (quad e) -> p quad i e", e=PACK)

        def by_column(packed):
            return packed.rearrange("p (quad e i) -> p quad i e", e=PACK, i=PACK)

        def quantize(codes, plane, packed):
            nc.vector.quantize_mx(out=codes.bitcast(FP8X4), scales=plane, in_=packed)

        weights = {}
        wq_packed = [held([P, PACK * PASS], BF16, "wq_packed%d" % g) for g in range(GROUPS)]

        def round_wq(g):
            if g == DEALT:
                nc.gpsimd.tensor_scalar(
                    out=wq_packed[g][:].rearrange("p (t m i) -> p m t i", t=PACK, i=PACK),
                    in0=wq_raw[g][:].rearrange("p i (m t) -> p m t i", t=PACK),
                    scalar1=1.0, scalar2=0.0, op0=ALU.mult, op1=ALU.add,
                )
            else:
                nc.vector.tensor_copy(by_column(wq_packed[g][:]), by_row(wq_raw[g][:]))

        def quantize_wq(g):
            codes, plane = held([P, PASS], I32, "wq_codes%d" % g), held([P, PASS], U8, "wq_plane%d" % g)
            quantize(codes[:], plane[:], wq_packed[g][:])
            weights["wq", g, g == DEALT] = (codes[:], plane[:])

        for g in range(GROUPS):
            weights["wi", g, False] = (wi_raw[g][:], wi_plane[WI_ROW:P, g * PASS : (g + 1) * PASS])

        dealt_codes, dealt_plane = held([P, PASS], I32, "wi_dealt_codes"), held([P, PASS], U8, "wi_dealt_plane")
        weights["wi", DEALT, True] = (dealt_codes[:], dealt_plane[WI_ROW:P, :])

        def deal(target, source, run):
            nc.vector.tensor_copy(
                target.rearrange("p (t hi lo) -> p hi t lo", t=PACK, lo=run),
                source.rearrange("p (hi lo t) -> p hi t lo", lo=run, t=PACK),
            )

        def deal_wi_plane():
            deal(dealt_plane[:], wi_plane[:, DEALT * PASS : (DEALT + 1) * PASS], 16)

        def deal_wi_words():
            deal(dealt_codes[:], wi_raw[DEALT][:], 4)

        wd_codes = held([P, GROUPS * N], U32, "wd_codes")
        wd_plane = held([P, GROUPS * N], U8, "wd_plane")
        wd_packed = held([P, GROUPS * N * PACK], BF16, "wd_packed")

        def round_negated_wd(g):
            nc.vector.tensor_scalar(
                out=by_column(wd_packed[:, g * N * PACK : (g + 1) * N * PACK]),
                in0=by_row(wd_raw[:, g, :].rearrange("p (i n) -> p i n", i=PACK)),
                scalar1=-1.0, scalar2=None, op0=ALU.mult,
            )

        def quantize_wd(g):
            cols = slice(g * N, (g + 1) * N)
            quantize(wd_codes[:, cols], wd_plane[:, cols], wd_packed[:, g * N * PACK : (g + 1) * N * PACK])

        env_codes = {
            (g, b): held([P, BANK], U32, "env_codes%d%d" % (g, b)) for g in range(GROUPS) for b in range(HALVES)
        }
        env_planes = [held([P, GROUPS, BANK], U8, "env_planes%d" % b) for b in range(HALVES)]

        def env_plane(g, j0, width):
            return env_planes[j0 // BANK][:, g, j0 % BANK : j0 % BANK + width]
        out_1_rows = out_1.rearrange("(g p t) j -> g p t j", g=GROUPS, t=PACK)
        out_0_rows = out_0.rearrange("(n p) j -> p n j", p=P)
        squares = {}

        def products_of(beam, u, c, bank):
            g, j0, width, road = UNITS[u]
            dealt = g == DEALT and (beam == "wq" or road == DIRECT)
            codes, plane = weights[beam, g, dealt]
            if road == DIRECT:
                v, v_scale = snapshots(j0, width)
                per_bank = BANK // width
                for place in range(per_bank):
                    cols = slice((c * per_bank + place) * P, (c * per_bank + place + 1) * P)
                    nc.tensor.matmul_mx(
                        out=bank[:, place * width : (place + 1) * width], lhsT=codes[:, cols].bitcast(FP8X4),
                        lhsT_scale=plane[:, cols], rhs=v, rhs_scale=v_scale, start=True, stop=True,
                    )
            else:
                v, v_scale = snapshots(j0 + c * P, P)
                nc.tensor.matmul_mx(
                    out=bank[:], lhsT=v, lhsT_scale=v_scale, rhs=codes.bitcast(FP8X4), rhs_scale=plane,
                    start=True, stop=True,
                )
            if dealt:
                return bank[:].rearrange("p (t m) -> p t m", t=PACK)
            return bank[:].rearrange("p (m t) -> p t m", t=PACK)

        def square_tile(beam, u, c):
            if (beam, u) not in squares:
                squares[beam, u] = held([P, UNITS[u][2] // P, PACK, P], F32, "%s_square%d" % (beam, u), REUSED.get((beam, u)))
            return squares[beam, u][:, c]

        filled = {}

        def fill(beam, u, c, ring="scalar"):
            bank = take_bank(ring)
            filled[beam, u, c] = (bank, products_of(beam, u, c, bank))

        def square_on_vector(beam, u, c):
            bank, products = filled[beam, u, c]
            nc.vector.tensor_reduce(
                square_tile(beam, u, c), products.unsqueeze(3).to_broadcast([P, PACK, P, 2]), AXIS.X, ALU.mult
            )
            release(bank)

        def square(beam, u, c):
            bank, products = filled[beam, u, c]
            nc.scalar.activation(square_tile(beam, u, c), products, ACT.Square)
            release(bank)

        env = [held([P, PACK, width], F32, "env%d" % u)[:] for u, (g, j0, width, road) in enumerate(UNITS[:4])]
        last_env = held([P, PACK, 2 * P], F32, "last_env")
        env.extend([last_env[:, :, 0:P], last_env[:, :, P : 2 * P]])
        env_packed = {}

        sums = {}

        def turn(u, k, ring="scalar"):
            width = UNITS[u][2]
            rows, blocks = BANK // width, width // P
            bank = take_bank(ring)
            sums[u, k] = bank
            terms = [(beam, r, c) for beam in ("wi", "wq") for r in range(rows) for c in range(blocks)]
            for beam, r, c in terms:
                place = r * width + c * P
                nc.tensor.matmul(
                    bank[:, place : place + P], lhsT=squares[beam, u][:, c, k * rows + r, :], rhs=ident[:],
                    is_transpose=True, start=((beam, r, c) == terms[0]), stop=((beam, r, c) == terms[-1]),
                )

        def roots_turned(u, k):
            g, j0, width, road = UNITS[u]
            rows = BANK // width
            for r in range(rows):
                t = k * rows + r
                nc.scalar.activation(
                    env[u][:, t, :], sums[u, k][:, r * width : (r + 1) * width], ACT.Sqrt, bias=ambient[:, g, t : t + 1]
                )
            release(sums[u, k])

        power = {}

        def add_squares(u, first, count):
            if u not in power:
                power[u] = held([P, PACK, UNITS[u][2]], F32, "power%d" % u)
            cols = slice(first * BANK, (first + count) * BANK)
            nc.vector.tensor_tensor(
                out=power[u][:].rearrange("p t j -> p (t j)")[:, cols],
                in0=squares["wi", u][:].rearrange("p c a z -> p (c a z)")[:, cols],
                in1=squares["wq", u][:].rearrange("p c a z -> p (c a z)")[:, cols], op=ALU.add,
            )

        def roots_direct(u, rows, first, count):
            g = UNITS[u][0]
            for t in range(rows.start, rows.stop):
                nc.scalar.activation(
                    env[u][:, t, first : first + count], power[u][:, t, first : first + count], ACT.Sqrt,
                    bias=ambient[:, g, t : t + 1],
                )

        def store_env(u, rows):
            g, j0, width, road = UNITS[u]
            nc.sync.dma_start(out_1_rows[g, :, rows, j0 : j0 + width], env[u][:, rows, :])

        def store_last_env():
            nc.sync.dma_start(out_1_rows[1, :, :, S - 2 * P : S], last_env[:])

        def round_env(u, first, count):
            if u not in env_packed:
                env_packed[u] = held([P, PACK * UNITS[u][2]], BF16, "env_packed%d" % u, REUSED.get(("packed", u)))
            nc.vector.tensor_copy(
                by_column(env_packed[u][:, first * PACK : (first + count) * PACK]),
                by_row(env[u][:, :, first : first + count]),
            )

        def quantize_env(u, first, count):
            g, j0, width, road = UNITS[u]
            start, end = j0 + first, j0 + first + count
            codes = env_codes[g, j0 // BANK]
            quantize(
                codes[:, start % BANK : start % BANK + count], env_plane(g, start, count),
                env_packed[u][:, first * PACK : (first + count) * PACK],
            )

        def store_codes(g, j0, end):
            codes = env_codes[g, j0 // BANK]
            width = end - j0
            if width:
                out_2_words = out_2[g].rearrange("p j t -> p (j t)").bitcast(I32)
                nc.sync.dma_start(out_2_words[:, j0:end], codes[:, j0 % BANK : j0 % BANK + width].bitcast(I32))

        def store_scales(first, stop):
            for s in range(LIVE_ROWS):
                nc.sync.dma_start(
                    out_3[:, s:SCALE_ROWS:LIVE_ROWS, first:stop].rearrange("g q j -> q g j").bitcast(I32),
                    env_planes[first // BANK][s:P:QUADRANT].bitcast(I32),
                )

        def readout_pass(target, source, n, j0, width, start, stop):
            if source == "clutter":
                v, v_scale = snapshots(j0, width)
                nc.tensor.matmul_mx(
                    out=target, lhsT=wc_codes[:, 2 * n * P : 2 * (n + 1) * P].bitcast(FP4X4),
                    lhsT_scale=wc_plane[:, n * P : (n + 1) * P], rhs=v, rhs_scale=v_scale, start=start, stop=stop,
                )
                return
            cols = slice(source * N + n * P, source * N + (n + 1) * P)
            nc.tensor.matmul_mx(
                out=target, lhsT=wd_codes[:, cols].bitcast(FP8X4), lhsT_scale=wd_plane[:, cols],
                rhs=env_codes[source, j0 // BANK][:, j0 % BANK : j0 % BANK + width].bitcast(FP8X4),
                rhs_scale=env_plane(source, j0, width), start=start, stop=stop,
            )

        minus_one = held([P, 1], F32, "minus_one", "env_packed2")
        nc.vector.memset(minus_one[:], -1.0)

        def empty(target, bank, on_scalar, sign=-1.0):
            if on_scalar:
                nc.scalar.activation(target, bank, ACT.Copy, scale=-1.0)
            else:
                nc.vector.tensor_scalar(out=target, in0=bank, scalar1=sign, scalar2=None, op0=ALU.mult)

        y = {u: held([P, ROW_TILES, UNITS[u][2]], F32, "y%d" % u)[:] for u in (1, 3)}
        last_y = held([P, ROW_TILES, 2 * P], F32, "last_y")
        y[4], y[5] = last_y[:, :, 0:P], last_y[:, :, P : 2 * P]
        opened = {}

        def wide_passes(u, source, first=0, stop=ROW_TILES):
            for n in range(first, stop):
                if source == "clutter":
                    opened[u, n] = take_bank("vector")
                readout_pass(opened[u, n][:], source, n, UNITS[u][1], BANK, source == "clutter", source == 1)

        def empty_wide(u, n, on_scalar):
            j0 = UNITS[u][1]
            empty(y[u][:, n, :], opened[u, n][:], on_scalar, minus_one[:] if n < 2 else -1.0)
            release(opened[u, n])
            nc.sync.dma_start(out_0_rows[:, n, j0 : j0 + BANK], y[u][:, n, :])

        def readout_passes(u, first, sources, start, stop):
            j0 = UNITS[u][1]
            if start:
                opened[u, first] = take_bank()[:, 0 : ROW_TILES * P].rearrange("p (n j) -> p n j", n=ROW_TILES)
            for source in sources:
                for n in range(ROW_TILES):
                    readout_pass(
                        opened[u, first][:, n, :], source, n, j0 + first, P,
                        start and source == sources[0] and n == 0,
                        stop and source == sources[-1] and n == ROW_TILES - 1,
                    )

        def middle_passes(u, source, ring="scalar"):
            j0, width = UNITS[u][1], UNITS[u][2]
            if source == "clutter":
                opened[u, 0], opened[u, 1] = take_bank(ring), take_bank(ring)
            for n in range(ROW_TILES):
                target = opened[u, n // 2][:, (n % 2) * width : (n % 2 + 1) * width]
                readout_pass(target, source, n, j0, width, source == "clutter" and n != 1, source == 1 and n != 0)

        def empty_middle(u, k, on_scalar):
            width = UNITS[u][2]
            rows = min(2, ROW_TILES - 2 * k)
            empty(y[u][:, 2 * k : 2 * k + rows, :].rearrange("p n j -> p (n j)"), opened[u, k][:, 0 : rows * width], on_scalar)
            release(opened[u, k])

        def empty_narrow(u, first, on_scalar):
            empty(y[u][:, :, first : first + P], opened[u, first], on_scalar)

        def store_last_y():
            nc.sync.dma_start(out_0_rows[:, :, S - 2 * P : S], last_y[:])

        def store_y(u, first, count):
            j0 = UNITS[u][1]
            nc.sync.dma_start(out_0_rows[:, :, j0 + first : j0 + first + count], y[u][:, :, first : first + count])

        gather_scales(0)
        gather_scales(1)
        gather_words(0, 2 * P)
        gather_words(2 * P, 2 * P)
        gather_words(BANK, BANK)
        low, high, every = slice(0, 2), slice(2, 4), slice(0, 4)

        def pair(beam, u, c):
            fill(beam, u, c)
            fill(beam, u, c + 1)
            square(beam, u, c)
            square(beam, u, c + 1)

        def one(beam, u, c=0):
            fill(beam, u, c)
            square(beam, u, c)

        def on_vector(beam, u, c):
            fill(beam, u, c, "vector")
            square_on_vector(beam, u, c)

        def turned_root(u, k):
            turn(u, k)
            roots_turned(u, k)

        fill("wi", 0, 0)
        fill("wi", 0, 1)
        square("wi", 0, 0)
        square("wi", 0, 1)
        fill("wi", 0, 2)
        fill("wi", 0, 3)
        square("wi", 0, 2)
        square("wi", 0, 3)
        fill("wi", 2, 0)
        fill("wi", 2, 1)
        square("wi", 2, 0)
        square("wi", 2, 1)
        fill("wi", 2, 2)
        fill("wi", 2, 3)
        square("wi", 2, 2)
        square("wi", 2, 3)
        round_wq(0)
        deal_wi_words()
        deal_wi_plane()
        quantize_wq(0)
        fill("wi", 1, 3, "vector")
        square_on_vector("wi", 1, 3)
        fill("wq", 0, 0)
        fill("wq", 0, 1)
        square("wq", 0, 0)
        square("wq", 0, 1)
        round_wq(1)
        fill("wq", 2, 0, "vector")
        square_on_vector("wq", 2, 0)
        fill("wq", 0, 2)
        fill("wq", 0, 3)
        square("wq", 0, 2)
        square("wq", 0, 3)
        fill("wq", 2, 1, "vector")
        square_on_vector("wq", 2, 1)
        fill("wq", 2, 2, "vector")
        square_on_vector("wq", 2, 2)
        quantize_wq(1)
        fill("wi", 1, 0)
        fill("wi", 1, 1)
        square("wi", 1, 0)
        square("wi", 1, 1)
        turn(0, 0)
        roots_turned(0, 0)
        fill("wq", 2, 3, "vector")
        square_on_vector("wq", 2, 3)
        fill("wi", 1, 2)
        fill("wi", 3, 0)
        square("wi", 1, 2)
        square("wi", 3, 0)
        turn(0, 1)
        roots_turned(0, 1)
        store_env(0, low)
        round_negated_wd(0)
        round_negated_wd(1)
        pair("wq", 1, 0)
        add_squares(1, 0, 2)
        pair("wq", 1, 2)
        add_squares(1, 2, 2)
        turned_root(0, 2)
        store_env(0, slice(2, 3))
        turned_root(0, 3)
        store_env(0, slice(3, 4))
        quantize_wd(0)
        quantize_wd(1)
        roots_direct(1, slice(0, 1), 0, BANK)
        store_env(1, slice(0, 1))
        roots_direct(1, slice(1, 2), 0, BANK)
        store_env(1, slice(1, 2))
        roots_direct(1, slice(2, 3), 0, BANK)
        store_env(1, slice(2, 3))
        roots_direct(1, slice(3, 4), 0, BANK)
        store_env(1, slice(3, 4))
        round_env(0, 0, BANK)
        wide_passes(1, "clutter", 0, 2)
        turn(2, 0)
        turn(2, 1)
        fill("wi", 3, 1)
        fill("wq", 3, 0)
        turn(2, 2)
        wide_passes(1, "clutter", 2, 3)
        round_env(1, 0, BANK)
        quantize_env(0, 0, BANK)
        quantize_env(1, 0, BANK)
        roots_turned(2, 0)
        store_env(2, slice(0, 1))
        fill("wq", 3, 1)
        roots_turned(2, 1)
        turn(2, 3)
        store_env(2, slice(1, 2))
        store_codes(0, 0, BANK)
        store_codes(1, 0, BANK)
        store_scales(0, BANK)
        square("wi", 3, 1)
        fill("wi", 4, 0)
        square("wq", 3, 0)
        fill("wq", 4, 0)
        square("wq", 3, 1)
        wide_passes(1, 0, 0, 1)
        wide_passes(1, 1, 0, 1)
        wide_passes(1, 0, 1, 2)
        wide_passes(1, 1, 1, 2)
        wide_passes(1, 0, 2, 3)
        wide_passes(1, 1, 2, 3)
        add_squares(3, 0, 2)
        roots_turned(2, 2)
        fill("wi", 5, 0)
        roots_turned(2, 3)
        fill("wq", 5, 0)
        store_env(2, high)
        empty_wide(1, 0, False)
        empty_wide(1, 1, False)
        empty_wide(1, 2, False)
        round_env(2, 0, BANK)
        square("wi", 4, 0)
        square("wq", 4, 0)
        turn(4, 0)
        roots_direct(3, every, 0, 2*P)
        store_env(3, every)
        round_env(3, 0, 2*P)
        quantize_env(2, 0, BANK)
        store_codes(0, BANK, S)
        square("wi", 5, 0)
        square("wq", 5, 0)
        turn(5, 0)
        roots_turned(4, 0)
        middle_passes(3, "clutter", "vector")
        middle_passes(3, 0)
        quantize_env(3, 0, 2*P)
        store_codes(1, BANK, BANK+2*P)
        middle_passes(3, 1)
        readout_passes(4, 0, ("clutter", 0), True, False)
        readout_passes(5, 0, ("clutter", 0), True, False)
        roots_turned(5, 0)
        store_last_env()
        round_env(4, 0, P)
        empty_middle(3, 1, False)
        quantize_env(4, 0, P)
        round_env(5, 0, P)
        empty_middle(3, 0, True)
        store_y(3, 0, 2*P)
        readout_passes(4, 0, (1,), False, True)
        quantize_env(5, 0, P)
        store_codes(1, BANK+2*P, S)
        store_scales(BANK, S)
        readout_passes(5, 0, (1,), False, True)
        empty_narrow(4, 0, True)
        empty_narrow(5, 0, False)
        store_last_y()
